import numpy as np, ml_dtypes
CORES = [48,51,52,55]
N = 4
BF = ml_dtypes.bfloat16
def gentries(a):
    return np.ascontiguousarray(a.reshape(8, 16, -1).transpose(0, 2, 1)).reshape(8, -1)
def gtable(e):
    e = np.asarray(e); return np.ascontiguousarray(e.reshape(8, -1, 16).transpose(0, 2, 1)).reshape(128, -1).astype(np.int32)
V, H, B, RO, GM, LG = 1024, 2, 2, 3, 2047, 11
def parts(rng):
    s = (N, 8, 16, V)
    return (rng.integers(0, 256, s), rng.integers(1, GM + 1, s), (rng.random(s) < rng.choice(np.array([0.25, 0.4, 0.55]), (N, 8, 1, 1))).astype(np.int64),
            rng.integers(0, V, (N, 8, V)), rng.integers(50, 63, s))
def pack(c, g, p, f, t):
    def flat(a): return np.ascontiguousarray(a.reshape(N, 128, V)).astype(np.int32)
    return {"c0": flat(c).astype(np.float32).astype(BF), "gp": flat(g), "cp": flat(p), "rf": np.stack([gtable(a) for a in f]), "th": flat(t)}
def setup_inputs(rng):
    return pack(*parts(rng))
def setup_inputs_spread(rng):
    c, g, p, f, t = parts(rng)
    c = np.minimum((np.exp2(8 * rng.random((N, 1, 1, V))) * rng.random(c.shape)).astype(np.int64), 255)
    g = np.minimum(np.maximum(np.exp2(LG * rng.random(g.shape)).astype(np.int64), 1), GM)
    p = (rng.random(p.shape) < rng.random((N, 8, 1, V))).astype(np.int64)
    f = np.minimum((V * rng.random(f.shape) ** 3).astype(np.int64), V - 1)
    return pack(c, g, p, f, rng.integers(0, 129, t.shape))
def setup_inputs_ends(rng):
    s = (N, 8, 16, V)
    def runs(v): return np.repeat(rng.choice(np.array(v), (N, 1, 1, V // 32)), 32, axis=3)
    c = np.where(np.where(runs([0, 1]) == 1, rng.random(s), rng.random((N, 1, 1, V))) < runs([0.1, 0.5, 0.9]), 255, 0)
    c[..., :17] = 255; c[..., V - 17:V - 1] = 255; c[..., V - 1] = 0; c[..., 64:128] = 0
    g = np.where(rng.random(s) < rng.choice(np.array([0.0, 0.5, 1.0]), (N, 8, 1, V)), GM, 1)
    p = (rng.random(s) < rng.choice(np.array([0.0, 0.0, 0.5, 0.8, 1.0]), (N, 8, 1, V))).astype(np.int64)
    p[:, :, 0, V - 1] = 0; p[N - 1, 7, :, V - 1] = 0; g[N - 1, 7, :, V - 1] = GM; p[:, :, :, 96] = 0
    f = (V - 1) * rng.integers(0, 2, (N, 8, V))
    t = 128 * np.where(rng.random((N, 8, 1, V)) < 0.5, rng.integers(0, 2, (N, 8, 1, V)), rng.integers(0, 2, s)); t[:, :, 0, V - 1] = 128
    return pack(c, g, p, f, t)
def setup_inputs_corners(rng):
    c, g, p, f, t = parts(rng); v = np.arange(V); k = np.arange(16)
    kinds = [v * 0, v * 0 + V - 1, v, np.maximum(v - 1, 0), np.minimum(v + 1, V - 1), v ^ 1, V - 1 - v]
    o = np.argsort(rng.random((N, 8)), axis=1)
    for q in range(N):
        for a in range(8): f[q, o[q, a]] = kinds[a] if a < 7 else rng.choice(np.array([0, V - 1]), V)
    one = rng.integers(0, 8, (N, 8, V)); run = np.repeat(rng.integers(0, 8, (N, 8, V // 16)), 16, axis=2)
    w = np.where(np.repeat(rng.random((N, 8, V // 16)) < 0.5, 16, axis=2), run, one)
    pat = np.stack([k < 0, k >= 0, k == 0, k == 15, k != 0, k != 15, (k & 1) == 1]).astype(np.int64)
    p = np.where(w[:, :, None, :] == 7, p, pat[np.minimum(w, 6)].transpose(0, 1, 3, 2))
    g = np.where(rng.random((N, 8, 1, V)) < 0.3, rng.choice(np.array([1, GM]), (N, 8, 1, V)), g)
    u = rng.random((N, 1, 1, V)); u[0, :, :, 0] = 0.5; u[N // 2 - 1::N // 2, :, :, V - 24:] = 0.5
    c = np.where(u < 0.1, 0, np.where(u > 0.9, 255, c)); t = rng.choice(np.array([0, 1, 52, 56, 60, 127, 128]), t.shape)
    for q in range(N - 1):
        a, b, e = o[q, 0], o[q, 1], o[q, 3]; i, j = rng.permutation(16)[:2]
        p[q, a] = 1; p[q, b] = 0; p[q, e, i] = 1; p[q, e, j] = 0
        g[q, b] = rng.integers(1, 4, (16, V)); g[q, b, 0] = V - v + rng.integers(0, V - 64, V)
    p[N - 1, :, :, V - 1] = 0; g[N - 1, :, :, V - 1] = GM; t[N - 1, :, :, V - 1] = 128
    return pack(c, g, p, f, t)
def setup_inputs_crowd(rng):
    c, g, p, f, t = parts(rng); s = c.shape
    u = rng.random((N, 1, 1, V)); u[..., 0] = 0.0; u[..., V - 1] = 0.0; u[..., 1] = 0.9; u[..., V - 2] = 0.9
    low = u < 0.03125; mixed = (u >= 0.03125) & (u < 0.15625)
    miss = (rng.random((N, 8, 1, V)) < 0.1) & (np.arange(16)[:, None] == rng.integers(0, 16, (N, 8, 1, V)))
    z = np.where(low, 0, np.where(mixed, rng.integers(0, 2, s), np.where(miss, 0, 1)))
    c = 2 * rng.integers(0, 128, (1, 8, 16, 1)) + z
    t = np.where(low, rng.integers(127, 129, s), np.where(mixed, rng.integers(48, 63, s), rng.integers(0, 5, s)))
    for q in range(N):
        a = rng.integers(0, 8); x = rng.integers(0, V); f[q, a] = x; p[q, a] = 1; p[q, a, :, x] = 0; p[q, a, :, V - 1] = 0
    return pack(c, g, p, f, t)
def check_inputs(d):
    bad = []
    for k, lo, hi in (("c0", 0, 255), ("gp", 1, GM), ("cp", 0, 1), ("rf", 0, V - 1), ("th", 0, 128)):
        a = np.asarray(d[k]).astype(np.float64)
        if not (np.min(a) >= lo and np.max(a) <= hi): bad.append("range of " + k)
        elif np.any(a != np.floor(a)): bad.append("whole numbers in " + k)
    return bad
def reference(c0, gp, cp, rf, th):
    C = c0.astype(np.float32).astype(np.int32).reshape(N, 8, 16, V); g = gp.astype(np.int64).reshape(N, 8, 16, V)
    own = cp.reshape(N, 8, 16, V) == 0; t = th.astype(np.int64).reshape(N, 8, 16, V)
    rl = np.stack([gentries(a) for a in rf]).astype(np.int64)[:, :, None, :]; base = np.arange(N * V).reshape(N, 1, 1, V)
    for rnd in range(RO):
        G = (base + np.add.accumulate(np.where(own, g, 0), axis=2)) & (N * V - 1)
        S = G
        for h in range(H): S = np.where(own, G, np.take_along_axis(S, rl, 3))
        T = np.ascontiguousarray(C.transpose(1, 2, 0, 3)).reshape(8, 16, N * V)
        f = []; new = []
        for r in range(N):
            P = np.take_along_axis(T, S[r].reshape(8, 1, 16 * V), 2).reshape(8, 16, 16, V)
            f.append(np.add.reduce((P > C[r][:, :, None, :]).astype(np.int64), axis=(0, 1)))
            best = np.maximum.reduce(P.reshape(8, 16, B, 16 // B, V), axis=3)
            new.append((C[r] + np.add.reduce(best, axis=2)) & 255)
        m = own & (np.stack(f)[:, None] < t)
        first = m & (np.add.accumulate(m.astype(np.int64), axis=2) == 1)
        g = g + first.astype(np.int64); C = np.stack(new)
    return {"yc": C.reshape(N, 128, V).astype(np.float32).astype(BF), "yg": g.reshape(N, 128, V).astype(np.float32)}

@@ -1,0 +1,463 @@
+from concourse.bass import DstId, RemoteDMATransfer
+from concourse.mybir import AluOpType as ALU, ActivationFunctionType as AF
+
+V = 1024
+NR = 4
+RO = 3
+TW = NR * V
+BIG = 65536.0
+QOFF = 129.0
+
+CFG = {
+    "units": [(0, 64, "A"), (64, 128, "V"), (128, 256, "A"), (256, 384, "A"), (384, 512, "A"), (512, 640, "A"),
+              (640, 768, "A"), (768, 896, "A"), (896, 960, "A"), (960, 1024, "A")],
+    "chunks": [(0, 256), (256, 512), (512, 768), (768, 960), (960, 1024)],
+    "wq": {},
+    "fast": [(0, 128), (128, 384)],
+    "pieces": [(0, 64), (64, 256), (256, 512), (512, 1024)],
+    "hop1": [(0, 768), (768, 1024)],
+    "c0a": 128,
+    "loads": ["c0a", "c0b", "cp0", "gp0", "cp1", "gp1", "rfs"],
+    "delta": 0.0,
+    "boost": {"a": 1e5, "M": 1000, "L": 2000, "B7": 1e4, "B4": 2000, "B5": 2000, "B1": 1e4, "Y": 1e5, "B6": 1e5,
+              "sg": 1e4, "S2": 1000, "h21": 3000, "h22": 3000, "B0": 1e4},
+    "xbanks": ["B6", "B7"],
+    "regv": [],
+    "dbanks": ["B7"],
+}
+EST = {"cyc": 1.04, "g": 1.56, "ov": 60.0, "oa": 70.0, "pe": 0.6, "op": 30.0, "sem": 100.0,
+       "dfix": 2000.0, "drow": 50.0, "dbw": 16.0, "rfix": 2200.0, "riss": 600.0}
+
+SCRATCH = {}
+
+
+def _decl(names, where, shape, dtype):
+    for n in names.split():
+        SCRATCH[n] = (where, shape, dtype)
+
+
+_decl("cpi gpi thi s2i s2m", "sbuf", [128, V], "int32")
+_decl("rfi", "sbuf", [128, 64], "int32")
+_decl("pcol pand", "sbuf", [128, 8], "int32")
+_decl("rf16", "sbuf", [128, 64], "uint16")
+_decl("L", "sbuf", [128, V], "uint16")
+_decl("tab0 tab1 tab2", "sbuf", [128, TW + 16], "bfloat16")
+_decl("P M CM", "sbuf", [128, 16 * V], "bfloat16")
+_decl("rst", "sbuf", [128, 2048], "bfloat16")
+_decl("nog S16", "sbuf", [128, V], "float16")
+_decl("ycb cpb nth qs sg any0 any1 any2 Y h1 h21 h22 qr", "sbuf", [128, V], "bfloat16")
+_decl("ygb Gw Hw Y2 S1 S2", "sbuf", [128, V], "float32")
+_decl("lo", "sbuf", [128, 512], "bfloat16")
+_decl("ones I nI I256 nI256 n2I nI4096 nBI tri0 tri sh Dm", "sbuf", [128, 128], "bfloat16")
+_decl("ntri16 I16", "sbuf", [128, 128], "float16")
+_decl("qoff", "sbuf", [128, 256], "bfloat16")
+_decl("I32", "sbuf", [128, 128], "float32")
+_decl("E Eh", "sbuf", [128, 144], "bfloat16")
+_decl("kcol wb wc", "sbuf", [128, 24], "float32")
+_decl("B0 B1 B2 B3 B4 B5 B6 B7", "psum", [128, 512], "float32")
+
+SEMAPHORES = ["sV", "sA", "sP", "sG", "c0a", "c0b", "cp0", "cp1", "gp0", "gp1", "rfs", "ths", "outs",
+              "arr0", "arr1", "arr2", "loc"]
+ENGSEM = {"V": "sV", "A": "sA", "P": "sP", "G": "sG"}
+
+
+def build(rank, cfg):
+    ops = []
+
+    def add(q, fn, rd, wr, kind, n, sig=None, rows=0):
+        ops.append({"q": q, "fn": fn, "rd": rd, "wr": wr, "kind": kind, "n": n, "sig": sig, "rows": rows,
+                    "boost": cfg["boost"].get(wr[0][0] if wr else "", cfg["boost"].get(kind, 0.0))})
+
+    def reg(name, lo, hi, step=1):
+        return (name, lo, hi, step)
+
+    def ap(T, r):
+        name, lo, hi, step = r
+        return T[name][:, lo:hi:step] if step != 1 else T[name][:, lo:hi]
+
+    def cnt(r):
+        return (r[2] - r[1] + r[3] - 1) // r[3]
+
+    def memset(o, c, half=True):
+        add("V", lambda g, T: g.vector.memset(ap(T, o), c), [], [o], "v", cnt(o) * (0.5 if half else 1))
+
+    def tscal(o, i, s1, s2, op0, op1=None, half=False):
+        def fn(g, T):
+            if op1 is None:
+                return g.vector.tensor_scalar(ap(T, o), ap(T, i), s1, None, op0)
+            return g.vector.tensor_scalar(ap(T, o), ap(T, i), s1, s2, op0, op1)
+        add("V", fn, [i], [o], "v", cnt(o) * (0.5 if half else 1))
+
+    def vcopy(o, i):
+        add("V", lambda g, T: g.vector.tensor_copy(ap(T, o), ap(T, i)), [i], [o], "v", cnt(o))
+
+    def tt(o, a, b, op, w=1):
+        add("V", lambda g, T: g.vector.tensor_tensor(ap(T, o), ap(T, a), ap(T, b), op), [a, b], [o], "v", cnt(o) * w)
+
+    def hop(o, win, y, v0, v1, op):
+        off = reg("rf16", v0 // 16, v1 // 16)
+        w = reg(win, 0, V)
+        add("V", lambda g, T: g.vector.tensor_tensor(ap(T, reg(o, v0, v1)), ap(T, w).indirect(ap(T, off)),
+                                                     ap(T, reg(y, v0, v1)), op),
+            [w, off, reg(y, v0, v1)], [reg(o, v0, v1)], "vg", v1 - v0)
+
+    def act(o, i, func, bias=0.0, scale=1.0):
+        col = bias if isinstance(bias, tuple) else None
+
+        def fn(g, T):
+            return g.scalar.activation(ap(T, o), ap(T, i), func, bias=(ap(T, col) if col else bias), scale=scale)
+        add("A", fn, [i] + ([col] if col else []), [o], "a", cnt(o))
+
+    def mm(o, w, x, start, stop, wide=1):
+        add("P", lambda g, T: g.tensor.matmul(ap(T, o), ap(T, w), ap(T, x), start, stop), [w, x], [o], "p",
+            max(64, cnt(o)) * wide)
+
+    def full(name):
+        return reg(name, 0, 128)
+
+    def load(q, name, src, c0, c1, d0, sem, size, extra=()):
+        def fn(g, T):
+            return (g.sync if q == "S" else g.scalar).dma_start(T[name][:, d0:d0 + c1 - c0], T[src][:, c0:c1])
+        add(q, fn, list(extra), [reg(name, d0, d0 + c1 - c0)], "d", (c1 - c0) * size, sig=(sem, 16), rows=128)
+
+    def store(dst, name, v0, v1, size):
+        add("S", lambda g, T: g.sync.dma_start(T[dst][:, v0:v1], T[name][:, v0:v1]), [reg(name, v0, v1)],
+            [], "d", (v1 - v0) * size, sig=("outs", None), rows=128)
+
+    nsend = [0]
+
+    def send(r, s0, s1, d0):
+        tab = "tab%d" % r
+        nsend[0] += 1
+        add("G", ("send", tab, s0, s1, d0, "arr%d" % r), [reg(tab, s0, s1)], [reg("far%d" % r, nsend[0], nsend[0] + 1)],
+            "r", (s1 - s0) * 2 * (NR - 1), sig=("arr%d" % r, None), rows=128 * (NR - 1))
+
+    own0 = V * rank
+    units, chunks, wq = cfg["units"], cfg["chunks"], cfg["wq"]
+    ca = cfg["c0a"]
+
+    loads = {"c0a": ("tab0", "c0", 0, ca, own0, 2), "c0b": ("tab0", "c0", ca, V, own0 + ca, 2),
+             "cp0": ("cpi", "cp", 0, 512, 0, 4), "cp1": ("cpi", "cp", 512, V, 512, 4),
+             "gp0": ("gpi", "gp", 0, 512, 0, 4), "gp1": ("gpi", "gp", 512, V, 512, 4),
+             "rfs": ("rfi", "rf", 0, 64, 0, 4)}
+    for s in cfg["loads"]:
+        load("S", *loads[s][:5], s, loads[s][5])
+    memset(full("ones"), 1.0)
+    add("G", lambda g, T: g.affine_select(T.I[:], T.ones[:], [[-1, 128]], ALU.is_equal, 0.0, 0, 1),
+        [full("ones")], [full("I")], "g", 128)
+    add("G", lambda g, T: g.affine_select(T.tri0[:], T.ones[:], [[1, 128]], ALU.is_ge, 0.0, 0, -1),
+        [full("ones")], [full("tri0")], "g", 128)
+    add("G", lambda g, T: g.affine_select(T.tri[:], T.tri0[:], [[-16, 8], [0, 16]], ALU.is_ge, 0.0, 0, 1),
+        [full("tri0")], [full("tri")], "g", 128)
+    add("G", lambda g, T: g.iota(T.lo[:], [[0, 2], [1, 256]], 0, 0, allow_small_or_imprecise_dtypes=True),
+        [], [reg("lo", 0, 512)], "g", 512)
+    send(0, own0, own0 + ca, own0)
+    send(0, own0 + ca, own0 + V, own0 + ca)
+    add("G", lambda g, T: g.iota(T.pcol[:, 0:1], [[0, 1]], 0, 1), [], [reg("pcol", 0, 1)], "g", 1)
+    add("G", lambda g, T: g.affine_select(T.sh[:], T.tri[:], [[1, 128]], ALU.is_equal, 0.0, -1, -1),
+        [full("tri")], [full("sh")], "g", 128)
+    load("S", "thi", "th", 0, V, 0, "ths", 4, extra=[reg("far0", 0, 999)])
+    tscal(full("ntri16"), full("tri"), -1.0, None, ALU.mult, half=True)
+    for name, c in (("nBI", -4 * BIG), ("I32", 1.0), ("I16", 1.0), ("nI4096", -4096.0), ("nI", -1.0), ("I256", 256.0),
+                    ("nI256", -256.0), ("n2I", -2.0)):
+        tscal(full(name), full("I"), c, None, ALU.mult, half=True)
+    if cfg["regv"]:
+        memset(reg("qoff", 0, 256), QOFF)
+    memset(reg("rst", 0, 2048), 1.0)
+    memset(reg("rst", 0, 2048, 8), 0.0)
+    for name, c in (("E", 1.0), ("Eh", 0.5))[:2 if wq else 1]:
+        memset(reg(name, 0, 144), 0.0)
+        memset(reg(name, 15, 144, 16), c)
+    tscal(reg("pand", 0, 1), reg("pcol", 0, 1), 15, None, ALU.bitwise_and)
+    tscal(reg("kcol", 0, 1), reg("pand", 0, 1), 1.0, None, ALU.add)
+    for w in sorted(set(wq.values())):
+        tscal(reg("wc", w, w + 1), reg("kcol", 0, 1), 16.5 - w, 64.0, ALU.is_gt, ALU.mult)
+        tscal(reg("wb", w, w + 1), reg("wc", w, w + 1), 0.5, None, ALU.add)
+    tt(full("Dm"), full("I"), full("sh"), ALU.subtract, 2)
+    vcopy(reg("rf16", 0, 64), reg("rfi", 0, 64))
+
+    for h in range(2):
+        a, b = 512 * h, 512 * h + 512
+        nown, z1, z2 = reg("B%d" % (4 + h), 0, 512), reg("B%d" % (6 + h), 0, 512), reg("B%d" % (2 + h), 0, 512)
+        tscal(nown, reg("cpi", a, b), -1.0, None, ALU.add)
+        act(reg("cpb", a, b), nown, AF.Identity, bias=1.0)
+        tt(reg("nog", a, b), reg("gpi", a, b), nown, ALU.mult)
+        mm(z1, full("I"), reg("lo", 0, 512), True, False)
+        mm(z1, full("ntri16"), reg("nog", a, b), False, True)
+        mm(z2, full("I"), reg("lo", 0, 512), True, False)
+        mm(z2, full("nBI"), reg("cpb", a, b), False, False)
+        mm(z2, full("ntri16"), reg("nog", a, b), False, True)
+        for j in range(2):
+            act(reg("Gw", a + 256 * j, a + 256 * j + 256), reg(z1[0], 256 * j, 256 * j + 256), AF.Identity,
+                bias=float(own0 + a + 256 * j))
+        for j in range(2):
+            tscal(reg("Hw", a + 256 * j, a + 256 * j + 256), reg(z2[0], 256 * j, 256 * j + 256),
+                  float(own0 + a + 256 * j) + BIG, 0.0, ALU.add, ALU.max)
+        for j in range(2):
+            act(reg("Y2", a + 256 * j, a + 256 * j + 256), reg(z2[0], 256 * j, 256 * j + 256), AF.Relu,
+                bias=float(own0 + a + 256 * j) + 2 * BIG)
+    hop("S1", "Gw", "Hw", 0, 512, ALU.max)
+    hop("S1", "Gw", "Hw", 512, V, ALU.max)
+    for v0, v1 in cfg["fast"]:
+        hop("s2i", "S1", "Y2", v0, v1, ALU.max)
+        tscal(reg("s2m", v0, v1), reg("s2i", v0, v1), TW - 1, None, ALU.bitwise_and)
+        vcopy(reg("L", v0, v1), reg("s2m", v0, v1))
+    done = cfg["fast"][-1][1]
+    for h in range(2):
+        a, b = max(512 * h, done), 512 * h + 512
+        if a < b:
+            bank = reg("B%d" % h, 0, b - a)
+            hop("S2", "S1", "Y2", a, b, ALU.max)
+            act(reg("qs", a, b), reg("S2", a, b), AF.Identity, bias=QOFF - 0.5 + 2.0 ** -13, scale=2.0 ** -12)
+            mm(bank, full("I32"), reg("S2", a, b), True, False, 4)
+            mm(bank, full("nI4096"), reg("qs", a, b), False, True)
+            tscal(reg("L", a, b), bank, QOFF * 4096, None, ALU.add)
+    tscal(reg("S16", 0, V), reg("L", 0, V), -TW / 2, None, ALU.add, half=True)
+    for h in range(2):
+        a, b = 512 * h, 512 * h + 512
+        mm(reg("B%d" % h, 0, 512), full("I256"), reg("cpb", a, b), True, True)
+        tt(reg("nth", a, b), reg("B%d" % h, 0, 512), reg("thi", a, b), ALU.subtract)
+
+    nd = [0]
+    for r in range(RO):
+        tab = "tab%d" % r
+        wlen = TW if r == 0 else TW + 8
+        last = r == RO - 1
+        if r > 0:
+            for v0, v1 in cfg["hop1"]:
+                hop("h1", "any%d" % (r - 1), "Y", v0, v1, ALU.is_ge)
+            for j, (v0, v1) in enumerate(cfg["pieces"]):
+                hop("h2%d" % r, "h1", "Y", v0, v1, ALU.is_ge)
+                o = reg("B%d" % (j % 2), 0, v1 - v0)
+                mm(o, full("I16"), reg("S16", v0, v1), True, False)
+                for rr in range(1, r + 1):
+                    mm(o, full("I"), reg("h2%d" % rr, v0, v1), False, rr == r)
+                tscal(reg("L", v0, v1), o, TW / 2, None, ALU.add)
+        for ci, (c0, c1) in enumerate(chunks):
+            n = c1 - c0
+            nw = wq.get(ci, 0)
+            mine = [(ui, u) for ui, u in enumerate(units) if c0 <= u[0] < c1]
+            for ui, (v0, v1, eng) in mine:
+                m = v1 - v0
+                pr, win, off = reg("P", 16 * v0, 16 * v1), reg(tab, 0, wlen), reg("L", v0, v1)
+                rd = [win, off, reg("far%d" % r, 0, 999)]
+                if eng == "A":
+                    add("A", lambda g, T, pr=pr, win=win, off=off: g.scalar.activation(
+                        ap(T, pr), ap(T, win).indirect(ap(T, off)), AF.Copy), rd, [pr], "ag", 16 * m)
+                else:
+                    add("V", lambda g, T, pr=pr, win=win, off=off: g.vector.tensor_copy(
+                        ap(T, pr), ap(T, win).indirect(ap(T, off))), rd, [pr], "vg", 16 * m)
+                add("V", lambda g, T, pr=pr, v0=v0, v1=v1, m=m: g.vector.tensor_tensor_scan(
+                    T.M[:, 16 * v0:16 * v1], T.rst[:, 0:16 * m], ap(T, pr), 0.0, ALU.mult, ALU.max),
+                    [pr, reg("rst", 0, 2048)], [reg("M", 16 * v0, 16 * v1)], "v", 8 * m)
+            cown = reg(tab, own0 + c0, own0 + c1)
+            cb = reg("B%d" % (2 + (r * len(chunks) + ci) % 2), 0, n)
+            if nw < 16:
+                mm(cb, full("I"), cown, True, True)
+            for k in range(16 - nw):
+                tt(reg("CM", 16 * c0 + k * n, 16 * c0 + (k + 1) * n), reg("P", 16 * c0 + k, 16 * c1, 16), cb, ALU.is_gt)
+            per = 512 // n
+            for k0 in range(16 - nw, 16, per):
+                k1 = min(16, k0 + per)
+                dbs = cfg["dbanks"] + ([cb[0]] if nw == 16 else [])
+                db = dbs[nd[0] % len(dbs)]
+                nd[0] += 1
+                for k in range(k0, k1):
+                    d = reg(db, (k - k0) * n, (k - k0 + 1) * n)
+                    mm(d, full("nI"), cown, True, False)
+                    mm(d, full("I"), reg("P", 16 * c0 + k, 16 * c1, 16), False, True)
+                act(reg("CM", 16 * c0 + k0 * n, 16 * c0 + k1 * n), reg(db, 0, (k1 - k0) * n), AF.Sign, bias=-0.5)
+            three = [cown, reg("M", 16 * c0 + 7, 16 * c1, 16), reg("M", 16 * c0 + 15, 16 * c1, 16)]
+            byv = ci in cfg["regv"]
+            nxt = "ycb" if last else "tab%d" % (r + 1)
+            outs = [(c0 if last else own0 + c0, n)] + ([(TW, 8)] if rank == 0 and c0 == 0 and not last else [])
+            if byv:
+                x = reg(cfg["xbanks"][ci % 2], 0, n)
+                mm(x, full("I256"), reg("qoff", 0, n), True, False)
+                for j in range(3):
+                    mm(x, full("I"), three[j], False, j == 2)
+                act(reg("qr", c0, c1), x, AF.Identity, bias=-127.5)
+                for d0, m in outs:
+                    tt(reg(nxt, d0, d0 + m), reg(x[0], 0, m), reg("qr", c0, c0 + m), ALU.subtract)
+            else:
+                x, x2 = reg(cfg["xbanks"][0], 0, n), reg(cfg["xbanks"][1], 0, n)
+                for j in range(3):
+                    mm(x, full("I"), three[j], j == 0, j == 2)
+                act(reg("qr", c0, c1), x, AF.Identity, bias=QOFF - 0.5 + 2.0 ** -9, scale=2.0 ** -8)
+                for j in range(3):
+                    mm(x2, full("I"), three[j], j == 0, False)
+                mm(x2, full("nI256"), reg("qr", c0, c1), False, True)
+                for d0, m in outs:
+                    act(reg(nxt, d0, d0 + m), reg(x2[0], 0, m), AF.Identity, bias=QOFF * 256)
+            if last:
+                store("yc", "ycb", c0, c1, 2)
+            else:
+                send(r + 1, own0 + c0, own0 + c1, own0 + c0)
+                if len(outs) > 1:
+                    send(r + 1, 0, 8, TW)
+            fb = "B%d" % (4 + (r * len(chunks) + ci) % 2)
+            F, Cc = reg(fb, 0, n), reg(fb, 256, 256 + n)
+            terms = [(full("I"), reg("nth", c0, c1))]
+            ks = [(reg("E" if k < 16 - nw else "Eh", 15 - k, 143 - k),
+                   reg("CM", 16 * c0 + k * n, 16 * c0 + (k + 1) * n)) for k in range(16)]
+            terms = ks + terms if (r == 0 and ci == 0) else terms + ks
+            for j, (w, xx) in enumerate(terms):
+                mm(F, w, xx, j == 0, j == len(terms) - 1)
+            act(reg("sg", c0, c1), F, AF.Sign, bias=reg("wb", nw, nw + 1) if nw else 0.5)
+            mm(Cc, full("tri"), reg("sg", c0, c1), True, True)
+            act(reg("any%d" % r, c0, c1), Cc, AF.Sign, bias=reg("kcol", 0, 1), scale=-1.0)
+            if last:
+                for j in range(RO):
+                    mm(F, full("Dm"), reg("any%d" % j, c0, c1), j == 0, j == RO - 1)
+                tt(reg("ygb", c0, c1), F, reg("gpi", c0, c1), ALU.add)
+                store("yg", "ygb", c0, c1, 4)
+            else:
+                mm(F, full("nI"), reg("cpb", c0, c1), True, False)
+                mm(F, full("n2I"), reg("any%d" % r, c0, c1), False, True)
+                act(reg("Y", c0, c1), F, AF.Abs, bias=2.0)
+    return ops
+
+
+def link(ops):
+    hist, bank = {}, {}
+    for i, o in enumerate(ops):
+        pre = {}
+        for rs, iswr in ((o["rd"], False), (o["wr"], True)):
+            for name, lo, hi, step in rs:
+                for j, a, b, w in hist.get(name, []):
+                    if (w or iswr) and a < hi and lo < b and j != i:
+                        both_pe = ops[j]["q"] == "P" and o["q"] == "P"
+                        pre[j] = pre.get(j, False) or not both_pe
+                if name[0] == "B" and len(name) == 2:
+                    j = bank.get(name)
+                    if j is not None and j != i:
+                        pre[j] = pre.get(j, False) or ops[j]["q"] != o["q"]
+                    bank[name] = i
+        for rs, iswr in ((o["rd"], False), (o["wr"], True)):
+            for name, lo, hi, step in rs:
+                h = hist.setdefault(name, [])
+                if iswr and step == 1:
+                    h[:] = [e for e in h if not (lo <= e[1] and e[2] <= hi)]
+                h.append((i, lo, hi, iswr))
+        o["pre"] = pre
+    return ops
+
+
+def cost(o, e):
+    k, n = o["kind"], o["n"]
+    if k == "v":
+        return e["ov"] + max(64, n) * e["cyc"], 0, 0
+    if k == "vg":
+        return e["ov"] + n * e["g"] * e["cyc"], 0, 0
+    if k == "a":
+        return e["oa"] + max(64, n) * e["cyc"], 0, 0
+    if k == "ag":
+        return e["oa"] + n * e["g"] * e["cyc"], 0, 0
+    if k == "p":
+        return e["op"] + n * e["pe"], 0, 0
+    if k == "g":
+        return 170 + 2 * n * e["cyc"], 0, 0
+    move = o["rows"] / 16 * e["drow"] + 8 * n / e["dbw"]
+    if k == "d":
+        return 60, move, e["dfix"]
+    return e["riss"], move, e["rfix"]
+
+
+def schedule(ops, e, delta):
+    n = len(ops)
+    succ = [[] for _ in range(n)]
+    for i, o in enumerate(ops):
+        for j in o["pre"]:
+            succ[j].append(i)
+    prio = [0.0] * n
+    for i in range(n - 1, -1, -1):
+        prio[i] = sum(cost(ops[i], e)) + max([prio[j] + e["sem"] for j in succ[i]] + [0.0])
+    for i in range(n):
+        prio[i] += ops[i].get("boost", 0.0)
+    left = [len(o["pre"]) for o in ops]
+    fin, ready = [0.0] * n, [0.0] * n
+    cand = {q: [] for q in "VAPGS"}
+    free = {q: 0.0 for q in "VAPGS"}
+    order = {q: [] for q in "VAPGS"}
+    dma = [0.0]
+    for i in range(n):
+        if left[i] == 0:
+            cand[ops[i]["q"]].append(i)
+    for _ in range(n):
+        t, q = min((max(free[q], min(ready[i] for i in cand[q])), q) for q in "VAPGS" if cand[q])
+        isdma = [i for i in cand[q] if ops[i]["kind"] == "d" and ready[i] <= t]
+        if isdma:
+            i = min(isdma)
+        else:
+            i = max((i for i in cand[q] if ready[i] <= t + delta), key=lambda i: (prio[i], -i))
+        cand[q].remove(i)
+        order[q].append(i)
+        a, b, c = cost(ops[i], e)
+        st = max(free[q], ready[i])
+        free[q] = st + a
+        if b:
+            dma[0] = max(dma[0], st + a + c) + b
+            fin[i] = dma[0]
+        else:
+            fin[i] = st + a
+        for j in succ[i]:
+            ready[j] = max(ready[j], fin[i] + (e["sem"] if ops[j]["pre"][i] else 0.0))
+            left[j] -= 1
+            if left[j] == 0:
+                cand[ops[j]["q"]].append(j)
+    return order
+
+
+def rank_program(g, core, T, topo):
+    rank = T.rank_of(core)
+    if rank is None:
+        return
+    ops = link(build(rank, CFG))
+    order = schedule(ops, EST, CFG["delta"])
+    peers = [c for c in T.cores if c != core]
+    mask = -1
+    for c in peers:
+        mask &= topo.mask(core, c)
+    neng = bin(mask).count("1")
+    dst_ids = [DstId(rid=topo.addr(c)[0], pnc=topo.addr(c)[1]) for c in peers]
+    total = {"loc": 0, "outs": 0, "arr0": 2 * (NR - 1) * neng}
+    for r in range(1, RO):
+        total["arr%d" % r] = (len(CFG["chunks"]) * (NR - 1) + (1 if rank else 0)) * neng
+    for q in "VAPGS":
+        k = 0
+        for i in order[q]:
+            o = ops[i]
+            if o["sig"] is None:
+                k += 1
+                o["sig"] = (ENGSEM[q], k)
+                total[ENGSEM[q]] = k
+            elif o["kind"] == "r":
+                o["sig"] = (o["sig"][0], total[o["sig"][0]])
+                total["loc"] += neng
+            elif o["sig"][0] == "outs":
+                total["outs"] += 16
+            else:
+                total[o["sig"][0]] = 16
+    queue = {"V": g.vector, "A": g.scalar, "P": g.tensor, "G": g, "S": g.sync}
+    for q in "VAPGS":
+        seen = {}
+        for i in order[q]:
+            o = ops[i]
+            need = {}
+            for j, w in o["pre"].items():
+                if w:
+                    s, val = ops[j]["sig"]
+                    need[s] = max(need.get(s, 0), val)
+            for s in sorted(need):
+                if need[s] > seen.get(s, 0):
+                    queue[q].wait_ge(T.sem[s], need[s])
+                    seen[s] = need[s]
+            if o["kind"] == "r":
+                tab, s0, s1, d0, arr = o["fn"][1:]
+                g.remote_dma_fused([RemoteDMATransfer(
+                    dst_ids=dst_ids, dma_engine_mask=mask, remote_sem=T.sem[arr], src=T[tab][:, s0:s1],
+                    dsts=[T[tab][:, d0:d0 + s1 - s0] for _ in peers])], local_sem=T.sem.loc)
+            else:
+                o["fn"](g, T).then_inc(T.sem[o["sig"][0]], 16 if o["kind"] == "d" else 1)
+    for s in SEMAPHORES:
+        g.sync.wait_ge(T.sem[s], total[s])

@@ -9,24 +9,29 @@ BIG = 65536.0
 QOFF = 129.0
 
 CFG = {
-    "units": [(0, 64, "A"), (64, 128, "V"), (128, 256, "A"), (256, 384, "A"), (384, 512, "A"), (512, 640, "A"),
-              (640, 768, "A"), (768, 896, "A"), (896, 960, "A"), (960, 1024, "A")],
-    "chunks": [(0, 256), (256, 512), (512, 768), (768, 960), (960, 1024)],
-    "wq": {},
-    "fast": [(0, 128), (128, 384)],
-    "pieces": [(0, 64), (64, 256), (256, 512), (512, 1024)],
+    "lm": (128, 1024),
+    "nat": [(0, 128, "A")],
+    "units": [("A", 0, 128, 384, 0), ("V", 1, 128, 384, 0), ("A", 0, 384, 640, 0), ("V", 1, 384, 640, 0),
+              ("A", 0, 640, 896, 8), ("A", 1, 640, 896, 2), ("A", 0, 896, 1024, 0), ("V", 1, 896, 1024, 0)],
+    "cnt": [(0, 128), (128, 384), (384, 640), (640, 896), (896, 1024)],
+    "reg": [(0, 128), (128, 384), (384, 640), (640, 896), (896, 1024)],
+    "links": {"A": 4, "V": 2},
+    "dbanks": ["B0", "B1"],
+    "fbanks": ["B4", "B5", "B6"],
+    "xbanks": ["B7", "B7"],
+    "turn": [1, 0],
+    "seq": "gn0 gu0 o0 gu1 o1 cn0 f0 r0 gu2 o2 s0 s1 cu1 cu0 f1 gu3 o3 gu4 o4 cu4 gu5 o5 r1 cu3 cu2 f2 gu7 o7 gu6 o6 "
+           "r2 cu5 f3 cu7 cu6 f4 r3 r4",
+    "folds": [[0], [1], [2], [3], [4], [5], [6], [7]],
     "hop1": [(0, 768), (768, 1024)],
     "c0a": 128,
     "loads": ["c0a", "c0b", "cp0", "gp0", "cp1", "gp1", "rfs"],
     "delta": 0.0,
-    "boost": {"a": 1e5, "M": 1000, "L": 2000, "B7": 1e4, "B4": 2000, "B5": 2000, "B1": 1e4, "Y": 1e5, "B6": 1e5,
-              "sg": 1e4, "S2": 1000, "h21": 3000, "h22": 3000, "B0": 1e4},
-    "xbanks": ["B6", "B7"],
-    "regv": [],
-    "dbanks": ["B7"],
+    "boost": {"VP": 5, "VM": 5, "VCM": 5, "VS16T": 2, "VS16": 8, "Vnth": 6, "AP": 5, "F": 5},
 }
-EST = {"cyc": 1.04, "g": 1.56, "ov": 60.0, "oa": 70.0, "pe": 0.6, "op": 30.0, "sem": 100.0,
-       "dfix": 2000.0, "drow": 50.0, "dbw": 16.0, "rfix": 2200.0, "riss": 600.0}
+EST = {"cyc": 0.87, "g": 1.56, "ov": 40.0, "oa": 45.0, "pe": 0.48, "op": 15.0, "sem": 100.0,
+       "dfix": 2000.0, "drow": 15.0, "dbw": 22.0, "rfix": 2200.0, "riss": 600.0, "rfirst": 3000.0,
+       "frow": 4.0, "fb": 0.8}
 
 SCRATCH = {}
 
@@ -40,53 +45,80 @@ _decl("cpi gpi thi s2i s2m", "sbuf", [128, V], "int32")
 _decl("rfi", "sbuf", [128, 64], "int32")
 _decl("pcol pand", "sbuf", [128, 8], "int32")
 _decl("rf16", "sbuf", [128, 64], "uint16")
-_decl("L", "sbuf", [128, V], "uint16")
-_decl("tab0 tab1 tab2", "sbuf", [128, TW + 16], "bfloat16")
-_decl("P M CM", "sbuf", [128, 16 * V], "bfloat16")
-_decl("rst", "sbuf", [128, 2048], "bfloat16")
-_decl("nog S16", "sbuf", [128, V], "float16")
-_decl("ycb cpb nth qs sg any0 any1 any2 Y h1 h21 h22 qr", "sbuf", [128, V], "bfloat16")
-_decl("ygb Gw Hw Y2 S1 S2", "sbuf", [128, V], "float32")
+_decl("L L2", "sbuf", [128, V], "uint16")
+_decl("tab0 tab1 tab2", "sbuf", [128, TW + 256], "bfloat16")
+_decl("P CM", "sbuf", [128, 16 * V], "bfloat16")
+_decl("M", "sbuf", [128, 8 * V], "bfloat16")
+_decl("rst", "sbuf", [128, 1024], "bfloat16")
+_decl("nog S16 hT h21 h22", "sbuf", [128, V], "float16")
+_decl("ycb ypt cpb nth sg run any0 any1 any2 Y h1 qr", "sbuf", [128, V], "bfloat16")
+_decl("FM00 FM01 FM10 FM11 FM20 FM21", "sbuf", [128, V], "bfloat16")
+_decl("ygb Gw Hw Y2 S1", "sbuf", [128, V], "float32")
 _decl("lo", "sbuf", [128, 512], "bfloat16")
-_decl("ones I nI I256 nI256 n2I nI4096 nBI tri0 tri sh Dm", "sbuf", [128, 128], "bfloat16")
+_decl("I nI I2 I3 I256 nI256 n2I nBI tri0 tri sh Dm Z", "sbuf", [128, 128], "bfloat16")
+_decl("ones J", "sbuf", [128, 160], "bfloat16")
+_decl("J0 J1", "sbuf", [128, 160], "float16")
 _decl("ntri16 I16", "sbuf", [128, 128], "float16")
-_decl("qoff", "sbuf", [128, 256], "bfloat16")
-_decl("I32", "sbuf", [128, 128], "float32")
-_decl("E Eh", "sbuf", [128, 144], "bfloat16")
+_decl("r16", "sbuf", [128, 256], "bfloat16")
+_decl("hv", "sbuf", [128, 8], "bfloat16")
 _decl("kcol wb wc", "sbuf", [128, 24], "float32")
-_decl("B0 B1 B2 B3 B4 B5 B6 B7", "psum", [128, 512], "float32")
+_decl("B0 B1", "psum", [128, 8, 64], "float32")
+_decl("B2 B3 B4 B5 B6 B7", "psum", [128, 512], "float32")
+_decl("ST", "sbuf", [128, 16, 64], "float32")
+_decl("I32", "sbuf", [128, 128], "float32")
+_decl("cw", "sbuf", [128, 4 * V], "bfloat16")
 
-SEMAPHORES = ["sV", "sA", "sP", "sG", "c0a", "c0b", "cp0", "cp1", "gp0", "gp1", "rfs", "ths", "outs",
-              "arr0", "arr1", "arr2", "loc"]
+SEMAPHORES = (["sV", "sA", "sP", "sG", "c0a", "c0b", "cp0", "cp1", "gp0", "gp1", "rfs", "ths", "outs",
+               "arr0", "arr1", "arr2", "loc", "fl0", "fl1", "fl2"]
+              + ["f%d_%d" % (r, u) for r in range(RO) for u in range(len(CFG["folds"]))]
+              + ["yb%d" % j for j in range(len(CFG["reg"]))])
 ENGSEM = {"V": "sV", "A": "sA", "P": "sP", "G": "sG"}
 
 
-def build(rank, cfg):
+def build(rank, par, cfg):
     ops = []
 
-    def add(q, fn, rd, wr, kind, n, sig=None, rows=0):
+    def add(q, fn, rd, wr, kind, n, sig=None, rows=0, boost=None):
+        if boost is None:
+            boost = cfg["boost"].get(q + (wr[0][0] if wr else ""), 9)
         ops.append({"q": q, "fn": fn, "rd": rd, "wr": wr, "kind": kind, "n": n, "sig": sig, "rows": rows,
-                    "boost": cfg["boost"].get(wr[0][0] if wr else "", cfg["boost"].get(kind, 0.0))})
+                    "boost": boost, "first": False})
 
     def reg(name, lo, hi, step=1):
         return (name, lo, hi, step)
 
+    def box(name, ra, rb, ca, cb):
+        w = SCRATCH[name][1][2]
+        return (name, ra * w + ca, (rb - 1) * w + cb, (ra, rb, ca, cb))
+
     def ap(T, r):
         name, lo, hi, step = r
+        if isinstance(step, tuple):
+            return T[name][:, step[0]:step[1], step[2]:step[3]]
+        if len(SCRATCH[name][1]) == 3:
+            w = SCRATCH[name][1][2]
+            if lo // w == (hi - 1) // w:
+                return T[name][:, lo // w, lo % w:(hi - 1) % w + 1:step]
+            return T[name][:, lo // w:hi // w, :]
         return T[name][:, lo:hi:step] if step != 1 else T[name][:, lo:hi]
 
     def cnt(r):
+        if isinstance(r[3], tuple):
+            return (r[3][1] - r[3][0]) * (r[3][3] - r[3][2])
         return (r[2] - r[1] + r[3] - 1) // r[3]
 
     def memset(o, c, half=True):
         add("V", lambda g, T: g.vector.memset(ap(T, o), c), [], [o], "v", cnt(o) * (0.5 if half else 1))
 
     def tscal(o, i, s1, s2, op0, op1=None, half=False):
+        cols = [s for s in (s1, s2) if isinstance(s, tuple)]
+
         def fn(g, T):
+            a, b = [ap(T, s) if isinstance(s, tuple) else s for s in (s1, s2)]
             if op1 is None:
-                return g.vector.tensor_scalar(ap(T, o), ap(T, i), s1, None, op0)
-            return g.vector.tensor_scalar(ap(T, o), ap(T, i), s1, s2, op0, op1)
-        add("V", fn, [i], [o], "v", cnt(o) * (0.5 if half else 1))
+                return g.vector.tensor_scalar(ap(T, o), ap(T, i), a, None, op0)
+            return g.vector.tensor_scalar(ap(T, o), ap(T, i), a, b, op0, op1)
+        add("V", fn, [i] + cols, [o], "v", cnt(o) * (0.5 if half else 1))
 
     def vcopy(o, i):
         add("V", lambda g, T: g.vector.tensor_copy(ap(T, o), ap(T, i)), [i], [o], "v", cnt(o))
@@ -94,23 +126,31 @@ def build(rank, cfg):
     def tt(o, a, b, op, w=1):
         add("V", lambda g, T: g.vector.tensor_tensor(ap(T, o), ap(T, a), ap(T, b), op), [a, b], [o], "v", cnt(o) * w)
 
-    def hop(o, win, y, v0, v1, op):
-        off = reg("rf16", v0 // 16, v1 // 16)
-        w = reg(win, 0, V)
-        add("V", lambda g, T: g.vector.tensor_tensor(ap(T, reg(o, v0, v1)), ap(T, w).indirect(ap(T, off)),
-                                                     ap(T, reg(y, v0, v1)), op),
-            [w, off, reg(y, v0, v1)], [reg(o, v0, v1)], "vg", v1 - v0)
+    def fused(o, w, off, y, op, extra=()):
+        add("V", lambda g, T: g.vector.tensor_tensor(ap(T, o), ap(T, w).indirect(ap(T, off)), ap(T, y), op),
+            [w, off, y] + list(extra), [o], "vg", cnt(o))
 
-    def act(o, i, func, bias=0.0, scale=1.0):
+    def hop(o, win, y, v0, v1, op):
+        fused(reg(o, v0, v1), reg(win, 0, V), reg("rf16", v0 // 16, v1 // 16), reg(y, v0, v1), op)
+
+    def gather(eng, o, w, off, extra):
+        if eng == "A":
+            add("A", lambda g, T: g.scalar.activation(ap(T, o), ap(T, w).indirect(ap(T, off)), AF.Copy),
+                [w, off] + extra, [o], "ag", cnt(o))
+        else:
+            add("V", lambda g, T: g.vector.tensor_copy(ap(T, o), ap(T, w).indirect(ap(T, off))),
+                [w, off] + extra, [o], "vg", cnt(o))
+
+    def act(o, i, func, bias=0.0, scale=1.0, boost=None):
         col = bias if isinstance(bias, tuple) else None
 
         def fn(g, T):
             return g.scalar.activation(ap(T, o), ap(T, i), func, bias=(ap(T, col) if col else bias), scale=scale)
-        add("A", fn, [i] + ([col] if col else []), [o], "a", cnt(o))
+        add("A", fn, [i] + ([col] if col else []), [o], "a", cnt(o), boost=boost)
 
-    def mm(o, w, x, start, stop, wide=1):
-        add("P", lambda g, T: g.tensor.matmul(ap(T, o), ap(T, w), ap(T, x), start, stop), [w, x], [o], "p",
-            max(64, cnt(o)) * wide)
+    def mm(o, w, x, start, stop, extra=(), boost=None):
+        add("P", lambda g, T: g.tensor.matmul(ap(T, o), ap(T, w), ap(T, x), start, stop), [w, x] + list(extra), [o],
+            "p", max(64, cnt(o)), boost=boost)
 
     def full(name):
         return reg(name, 0, 128)
@@ -126,15 +166,36 @@ def build(rank, cfg):
 
     nsend = [0]
 
-    def send(r, s0, s1, d0):
+    def send(r, s0, s1, behind=False):
         tab = "tab%d" % r
         nsend[0] += 1
-        add("G", ("send", tab, s0, s1, d0, "arr%d" % r), [reg(tab, s0, s1)], [reg("far%d" % r, nsend[0], nsend[0] + 1)],
-            "r", (s1 - s0) * 2 * (NR - 1), sig=("arr%d" % r, None), rows=128 * (NR - 1))
+        dsts = [reg(tab, s0, s1)] + ([reg(tab, TW, TW + s1 - s0)] if behind else [])
+        add("G", ([([reg(tab, s0, s1)], dsts)], "all", "loc"), [reg(tab, s0, s1)],
+            [reg("far%d" % r, nsend[0], nsend[0] + 1)], "r", (s1 - s0) * 2 * (NR - 1), sig=("arr%d" % r, None),
+            rows=128 * (NR - 1))
 
-    own0 = V * rank
-    units, chunks, wq = cfg["units"], cfg["chunks"], cfg["wq"]
+    own0, par0 = V * rank, V * par
+    r0, r1 = cfg["lm"]
+    nb = (r1 - r0) // 16
+    nat, units = cfg["nat"], cfg["units"]
+    natr = [(a, b) for a, b in ((0, r0), (r1, V)) if a < b]
     ca = cfg["c0a"]
+    ubase, at = [], 16 * r0
+    for u in units:
+        ubase.append(at)
+        at += 8 * (u[3] - u[2])
+
+    def ulist(u, ka, kb):
+        m = (units[u][3] - units[u][2]) // 16
+        return reg("L2", ubase[u] // 16 - r0 + ka * m, ubase[u] // 16 - r0 + kb * m)
+
+    def mcol(v):
+        return 16 * (v if v <= r0 else v - r1 + r0)
+
+    def signset(c0):
+        return tuple((8 * b + 8 - w, 8 * b + 8) for e, b, v0, v1, w in units if w and v0 <= c0 < v1)
+
+    sets = sorted(set(signset(c0) for c0, c1 in cfg["cnt"]) - {()})
 
     loads = {"c0a": ("tab0", "c0", 0, ca, own0, 2), "c0b": ("tab0", "c0", ca, V, own0 + ca, 2),
              "cp0": ("cpi", "cp", 0, 512, 0, 4), "cp1": ("cpi", "cp", 512, V, 512, 4),
@@ -142,39 +203,73 @@ def build(rank, cfg):
              "rfs": ("rfi", "rf", 0, 64, 0, 4)}
     for s in cfg["loads"]:
         load("S", *loads[s][:5], s, loads[s][5])
-    memset(full("ones"), 1.0)
-    add("G", lambda g, T: g.affine_select(T.I[:], T.ones[:], [[-1, 128]], ALU.is_equal, 0.0, 0, 1),
-        [full("ones")], [full("I")], "g", 128)
-    add("G", lambda g, T: g.affine_select(T.tri0[:], T.ones[:], [[1, 128]], ALU.is_ge, 0.0, 0, -1),
+    memset(reg("ones", 0, 160), 1.0)
+    add("G", lambda g, T: g.affine_select(T.J[:], T.ones[:], [[-1, 160]], ALU.is_equal, 0.0, 16, 1),
+        [reg("ones", 0, 160)], [reg("J", 0, 160)], "g", 160)
+    add("G", lambda g, T: g.affine_select(T.tri0[:], T.ones[:, 0:128], [[1, 128]], ALU.is_ge, 0.0, 0, -1),
         [full("ones")], [full("tri0")], "g", 128)
     add("G", lambda g, T: g.affine_select(T.tri[:], T.tri0[:], [[-16, 8], [0, 16]], ALU.is_ge, 0.0, 0, 1),
         [full("tri0")], [full("tri")], "g", 128)
     add("G", lambda g, T: g.iota(T.lo[:], [[0, 2], [1, 256]], 0, 0, allow_small_or_imprecise_dtypes=True),
         [], [reg("lo", 0, 512)], "g", 512)
-    send(0, own0, own0 + ca, own0)
-    send(0, own0 + ca, own0 + V, own0 + ca)
+    send(0, own0, own0 + ca)
+    ops[-1]["first"] = True
+    send(0, own0 + ca, own0 + V)
     add("G", lambda g, T: g.iota(T.pcol[:, 0:1], [[0, 1]], 0, 1), [], [reg("pcol", 0, 1)], "g", 1)
     add("G", lambda g, T: g.affine_select(T.sh[:], T.tri[:], [[1, 128]], ALU.is_equal, 0.0, -1, -1),
         [full("tri")], [full("sh")], "g", 128)
     load("S", "thi", "th", 0, V, 0, "ths", 4, extra=[reg("far0", 0, 999)])
+    eye = reg("J", 16, 144)
     tscal(full("ntri16"), full("tri"), -1.0, None, ALU.mult, half=True)
-    for name, c in (("nBI", -4 * BIG), ("I32", 1.0), ("I16", 1.0), ("nI4096", -4096.0), ("nI", -1.0), ("I256", 256.0),
-                    ("nI256", -256.0), ("n2I", -2.0)):
-        tscal(full(name), full("I"), c, None, ALU.mult, half=True)
-    if cfg["regv"]:
-        memset(reg("qoff", 0, 256), QOFF)
-    memset(reg("rst", 0, 2048), 1.0)
-    memset(reg("rst", 0, 2048, 8), 0.0)
-    for name, c in (("E", 1.0), ("Eh", 0.5))[:2 if wq else 1]:
-        memset(reg(name, 0, 144), 0.0)
-        memset(reg(name, 15, 144, 16), c)
+    for name, c in (("nBI", -4 * BIG), ("I16", 1.0), ("I32", 1.0), ("nI", -1.0), ("I256", 256.0), ("nI256", -256.0),
+                    ("I2", 2.0), ("I3", 3.0), ("Z", 0.0)):
+        tscal(full(name), eye, c, None, ALU.mult, half=True)
+    memset(reg("rst", 0, 1024), 1.0)
+    memset(reg("rst", 0, 1024, 8), 0.0)
+    memset(reg("hv", 0, 8), 0.5)
+    memset(reg("r16", 0, 256), -1.0)
+    memset(reg("r16", 0, 256, 16), 1.0)
     tscal(reg("pand", 0, 1), reg("pcol", 0, 1), 15, None, ALU.bitwise_and)
     tscal(reg("kcol", 0, 1), reg("pand", 0, 1), 1.0, None, ALU.add)
-    for w in sorted(set(wq.values())):
-        tscal(reg("wc", w, w + 1), reg("kcol", 0, 1), 16.5 - w, 64.0, ALU.is_gt, ALU.mult)
-        tscal(reg("wb", w, w + 1), reg("wc", w, w + 1), 0.5, None, ALU.add)
-    tt(full("Dm"), full("I"), full("sh"), ALU.subtract, 2)
+    tscal(reg("pand", 1, 2), reg("pcol", 0, 1), 16, None, ALU.bitwise_and)
+    tscal(reg("kcol", 1, 2), reg("pand", 1, 2), 8.0, None, ALU.is_lt)
+    tscal(reg("kcol", 2, 3), reg("pand", 1, 2), 8.0, None, ALU.is_gt)
+    for j in range(2):
+        tscal(reg("J%d" % j, 0, 160), reg("J", 0, 160), reg("kcol", 1 + j, 2 + j), None, ALU.mult, half=True)
+    nw = [0]
+    for si, st in enumerate(sets):
+        cur = 0.0
+        for k0, k1 in st:
+            a, b, c = reg("wc", nw[0], nw[0] + 1), reg("wc", nw[0] + 1, nw[0] + 2), reg("wc", nw[0] + 2, nw[0] + 3)
+            nw[0] += 3
+            tscal(a, reg("kcol", 0, 1), k0 + 0.5, 64.0, ALU.is_gt, ALU.mult)
+            tscal(b, reg("kcol", 0, 1), k1 + 0.5, -64.0, ALU.is_gt, ALU.mult)
+            o = reg("wb", si, si + 1) if (k0, k1) == st[-1] else c
+            tscal(o, a, b, cur, ALU.add, ALU.add)
+            cur = o
+    tt(full("Dm"), eye, full("sh"), ALU.subtract, 2)
     vcopy(reg("rf16", 0, 64), reg("rfi", 0, 64))
+
+    def turn(src, first):
+        n = r1 - r0
+        add("V", lambda g, T: g.vector.transpose(T.hT[:, 0:n], T[src][:, r0:r1]), [reg(src, r0, r1)],
+            [reg("hT", 0, n)], "v", n * 0.5)
+        for h in cfg["turn"]:
+            bank = "B%d" % h
+            if first:
+                mm(box(bank, 0, 8, 0, nb), full("Z"), reg("lo", 0, 8 * nb), True, False)
+            else:
+                mm(box(bank, 0, 8, 0, nb), full("I32"), box("ST", 8 * h, 8 * h + 8, 0, nb), True, False)
+                ops[-1]["n"] *= 4
+            for kk in range(8):
+                for d in range(2):
+                    for c in range(2):
+                        w = reg("J%d" % d, 16 + 16 * (d - c), 144 + 16 * (d - c))
+                        mm(reg(bank, kk * 64 + d, kk * 64 + nb, 2), w, reg("hT", 16 * c + 8 * h + kk, n, 32), False,
+                           (kk, d, c) == (7, 1, 1))
+            for u, (eng, blk, v0, v1, w) in enumerate(units):
+                if blk == h:
+                    tscal(ulist(u, 0, 8), box(bank, 0, 8, (v0 - r0) // 16, (v1 - r0) // 16), TW / 2, None, ALU.add)
 
     for h in range(2):
         a, b = 512 * h, 512 * h + 512
@@ -182,9 +277,9 @@ def build(rank, cfg):
         tscal(nown, reg("cpi", a, b), -1.0, None, ALU.add)
         act(reg("cpb", a, b), nown, AF.Identity, bias=1.0)
         tt(reg("nog", a, b), reg("gpi", a, b), nown, ALU.mult)
-        mm(z1, full("I"), reg("lo", 0, 512), True, False)
+        mm(z1, eye, reg("lo", 0, 512), True, False)
         mm(z1, full("ntri16"), reg("nog", a, b), False, True)
-        mm(z2, full("I"), reg("lo", 0, 512), True, False)
+        mm(z2, eye, reg("lo", 0, 512), True, False)
         mm(z2, full("nBI"), reg("cpb", a, b), False, False)
         mm(z2, full("ntri16"), reg("nog", a, b), False, True)
         for j in range(2):
@@ -198,123 +293,198 @@ def build(rank, cfg):
                 bias=float(own0 + a + 256 * j) + 2 * BIG)
     hop("S1", "Gw", "Hw", 0, 512, ALU.max)
     hop("S1", "Gw", "Hw", 512, V, ALU.max)
-    for v0, v1 in cfg["fast"]:
+    for v0, v1 in natr[:1] + [(r0, r1)] + natr[1:]:
         hop("s2i", "S1", "Y2", v0, v1, ALU.max)
         tscal(reg("s2m", v0, v1), reg("s2i", v0, v1), TW - 1, None, ALU.bitwise_and)
-        vcopy(reg("L", v0, v1), reg("s2m", v0, v1))
-    done = cfg["fast"][-1][1]
-    for h in range(2):
-        a, b = max(512 * h, done), 512 * h + 512
-        if a < b:
-            bank = reg("B%d" % h, 0, b - a)
-            hop("S2", "S1", "Y2", a, b, ALU.max)
-            act(reg("qs", a, b), reg("S2", a, b), AF.Identity, bias=QOFF - 0.5 + 2.0 ** -13, scale=2.0 ** -12)
-            mm(bank, full("I32"), reg("S2", a, b), True, False, 4)
-            mm(bank, full("nI4096"), reg("qs", a, b), False, True)
-            tscal(reg("L", a, b), bank, QOFF * 4096, None, ALU.add)
-    tscal(reg("S16", 0, V), reg("L", 0, V), -TW / 2, None, ALU.add, half=True)
+        if v0 == r0:
+            tscal(reg("S16", v0, v1), reg("s2m", v0, v1), -TW / 2, None, ALU.add)
+            turn("S16", True)
+        else:
+            vcopy(reg("L", v0, v1), reg("s2m", v0, v1))
+            tscal(reg("S16", v0, v1), reg("L", v0, v1), -TW / 2, None, ALU.add, half=True)
     for h in range(2):
         a, b = 512 * h, 512 * h + 512
-        mm(reg("B%d" % h, 0, 512), full("I256"), reg("cpb", a, b), True, True)
-        tt(reg("nth", a, b), reg("B%d" % h, 0, 512), reg("thi", a, b), ALU.subtract)
+        mm(reg("B%d" % (4 + h), 0, 512), full("I256"), reg("cpb", a, b), True, True, boost=0)
+        tt(reg("nth", a, b), reg("B%d" % (4 + h), 0, 512), reg("thi", a, b), ALU.subtract)
+    for c0, c1 in cfg["cnt"]:
+        if signset(c0):
+            j = sets.index(signset(c0))
+            tscal(reg("nth", c0, c1), reg("nth", c0, c1), reg("wb", j, j + 1), None, ALU.add, half=True)
 
-    nd = [0]
+    nd, nc, nf = [0], [0], [0]
     for r in range(RO):
         tab = "tab%d" % r
-        wlen = TW if r == 0 else TW + 8
+        win = reg(tab, 0, TW if r == 0 else TW + 8)
+        far = [reg("far%d" % r, 0, 999)]
         last = r == RO - 1
         if r > 0:
             for v0, v1 in cfg["hop1"]:
                 hop("h1", "any%d" % (r - 1), "Y", v0, v1, ALU.is_ge)
-            for j, (v0, v1) in enumerate(cfg["pieces"]):
+            for j, (v0, v1) in enumerate(natr[:1] + [(r0, r1)] + natr[1:]):
                 hop("h2%d" % r, "h1", "Y", v0, v1, ALU.is_ge)
-                o = reg("B%d" % (j % 2), 0, v1 - v0)
+                if v0 == r0:
+                    turn("h2%d" % r, False)
+                    continue
+                o = reg("B%d" % (6 + j // 2), 0, v1 - v0)
                 mm(o, full("I16"), reg("S16", v0, v1), True, False)
                 for rr in range(1, r + 1):
-                    mm(o, full("I"), reg("h2%d" % rr, v0, v1), False, rr == r)
+                    mm(o, full("I16"), reg("h2%d" % rr, v0, v1), False, rr == r)
                 tscal(reg("L", v0, v1), o, TW / 2, None, ALU.add)
-        for ci, (c0, c1) in enumerate(chunks):
-            n = c1 - c0
-            nw = wq.get(ci, 0)
-            mine = [(ui, u) for ui, u in enumerate(units) if c0 <= u[0] < c1]
-            for ui, (v0, v1, eng) in mine:
-                m = v1 - v0
-                pr, win, off = reg("P", 16 * v0, 16 * v1), reg(tab, 0, wlen), reg("L", v0, v1)
-                rd = [win, off, reg("far%d" % r, 0, 999)]
+
+        def keep(h):
+            if not last:
+                act(box("ST", 8 * h, 8 * h + 8, 0, nb), box("B%d" % h, 0, 8, 0, nb), AF.Identity)
+
+        def natural(j):
+            v0, v1, eng = nat[j]
+            for a in range(v0, v1, 64):
+                pr = reg("P", 16 * a, 16 * a + 1024)
+                gather(eng, pr, win, reg("L", a, a + 64), far)
+                mo = reg("M", mcol(a), mcol(a) + 1024)
+                add("V", lambda g, T, pr=pr, mo=mo: g.vector.tensor_tensor_scan(
+                    ap(T, mo), T.rst[:], ap(T, pr), 0.0, ALU.mult, ALU.max), [pr, reg("rst", 0, 1024)], [mo], "v", 512)
+
+        def unit(u):
+            eng, blk, v0, v1, w = units[u]
+            n = v1 - v0
+            per = cfg["links"][eng]
+            if eng == "V":
+                src = reg(tab, own0 + v0, own0 + v1)
+                for j in range(per):
+                    cw = reg("cw", per * v0 + j * n, per * v0 + (j + 1) * n)
+                    add("G", lambda g, T, cw=cw: g.affine_select(ap(T, cw), ap(T, src), [[0, n]], ALU.is_ge, 0.0, 0, 0),
+                        [src] + far, [cw], "g", n)
+            for kk in range(0, 8, per):
+                o = reg("P", ubase[u] + kk * n, ubase[u] + (kk + per) * n)
                 if eng == "A":
-                    add("A", lambda g, T, pr=pr, win=win, off=off: g.scalar.activation(
-                        ap(T, pr), ap(T, win).indirect(ap(T, off)), AF.Copy), rd, [pr], "ag", 16 * m)
+                    gather("A", o, win, ulist(u, kk, kk + per), far)
                 else:
-                    add("V", lambda g, T, pr=pr, win=win, off=off: g.vector.tensor_copy(
-                        ap(T, pr), ap(T, win).indirect(ap(T, off))), rd, [pr], "vg", 16 * m)
-                add("V", lambda g, T, pr=pr, v0=v0, v1=v1, m=m: g.vector.tensor_tensor_scan(
-                    T.M[:, 16 * v0:16 * v1], T.rst[:, 0:16 * m], ap(T, pr), 0.0, ALU.mult, ALU.max),
-                    [pr, reg("rst", 0, 2048)], [reg("M", 16 * v0, 16 * v1)], "v", 8 * m)
-            cown = reg(tab, own0 + c0, own0 + c1)
-            cb = reg("B%d" % (2 + (r * len(chunks) + ci) % 2), 0, n)
-            if nw < 16:
-                mm(cb, full("I"), cown, True, True)
-            for k in range(16 - nw):
-                tt(reg("CM", 16 * c0 + k * n, 16 * c0 + (k + 1) * n), reg("P", 16 * c0 + k, 16 * c1, 16), cb, ALU.is_gt)
-            per = 512 // n
-            for k0 in range(16 - nw, 16, per):
-                k1 = min(16, k0 + per)
-                dbs = cfg["dbanks"] + ([cb[0]] if nw == 16 else [])
-                db = dbs[nd[0] % len(dbs)]
+                    fused(o, win, ulist(u, kk, kk + per), reg("cw", per * v0, per * v1), ALU.subtract, far)
+
+        def fold(j):
+            moves = []
+            for u in cfg["folds"][j]:
+                eng, blk, v0, v1, w = units[u]
+                n = v1 - v0
+                moves.append(([reg("P", ubase[u] + kk * n, ubase[u] + (kk + 1) * n) for kk in range(8)],
+                              [reg("FM%d%d" % (r, blk), v0, v1)]))
+            add("G", (moves, "par", "fl%d" % r), [x for m in moves for x in m[0]], [m[1][0] for m in moves], "f",
+                16 * n * len(moves), sig=("f%d_%d" % (r, j), None), rows=128 * len(moves))
+
+        def compare(kind, j):
+            if kind == "n":
+                v0, v1 = nat[j][:2]
+                n, w, base = v1 - v0, 0, 16 * v0
+                src = [reg("P", base + k, 16 * v1, 16) for k in range(16)]
+            else:
+                eng, blk, v0, v1, w = units[j]
+                n, base = v1 - v0, ubase[j]
+                if eng == "V":
+                    for h in range(2):
+                        a, b = base + 4 * n * h, base + 4 * n * (h + 1)
+                        tscal(reg("CM", a, b), reg("P", a, b), 0.0, None, ALU.is_gt, half=True)
+                    return
+                src = [reg("P", base + k * n, base + (k + 1) * n) for k in range(8)]
+            cown = reg(tab, own0 + v0, own0 + v1)
+            nv = len(src) - w
+            per = 1 if kind == "n" else min(8, 512 // n)
+            if nv:
+                cb = "B%d" % (2 + nc[0] % 2)
+                nc[0] += 1
+                for i in range(min(per, nv)):
+                    mm(reg(cb, i * n, (i + 1) * n), eye, cown, True, True, far)
+            for k in range(0, nv, per):
+                m = min(per, nv - k)
+                tt(reg("CM", base + k * n, base + (k + m) * n),
+                   src[k] if kind == "n" else reg("P", base + k * n, base + (k + m) * n), reg(cb, 0, m * n), ALU.is_gt)
+            for k0 in range(nv, len(src), per):
+                k1 = min(len(src), k0 + per)
+                db = cfg["dbanks"][nd[0] % len(cfg["dbanks"])]
                 nd[0] += 1
+                mm(reg(db, 0, (k1 - k0) * n), eye, reg("P", base + k0 * n, base + k1 * n), True, False, boost=5)
                 for k in range(k0, k1):
-                    d = reg(db, (k - k0) * n, (k - k0 + 1) * n)
-                    mm(d, full("nI"), cown, True, False)
-                    mm(d, full("I"), reg("P", 16 * c0 + k, 16 * c1, 16), False, True)
-                act(reg("CM", 16 * c0 + k0 * n, 16 * c0 + k1 * n), reg(db, 0, (k1 - k0) * n), AF.Sign, bias=-0.5)
-            three = [cown, reg("M", 16 * c0 + 7, 16 * c1, 16), reg("M", 16 * c0 + 15, 16 * c1, 16)]
-            byv = ci in cfg["regv"]
-            nxt = "ycb" if last else "tab%d" % (r + 1)
-            outs = [(c0 if last else own0 + c0, n)] + ([(TW, 8)] if rank == 0 and c0 == 0 and not last else [])
-            if byv:
-                x = reg(cfg["xbanks"][ci % 2], 0, n)
-                mm(x, full("I256"), reg("qoff", 0, n), True, False)
-                for j in range(3):
-                    mm(x, full("I"), three[j], False, j == 2)
-                act(reg("qr", c0, c1), x, AF.Identity, bias=-127.5)
-                for d0, m in outs:
-                    tt(reg(nxt, d0, d0 + m), reg(x[0], 0, m), reg("qr", c0, c0 + m), ALU.subtract)
+                    mm(reg(db, (k - k0) * n, (k - k0 + 1) * n), full("nI"), cown, False, k == k1 - 1, far, boost=5)
+                act(reg("CM", base + k0 * n, base + k1 * n), reg(db, 0, (k1 - k0) * n), AF.Sign, bias=-0.5, boost=5)
+
+        def registers(j):
+            c0, c1 = cfg["reg"][j]
+            n = c1 - c0
+            folded = r0 <= c0 < r1
+            if folded:
+                nv = sum(1 for e, b, v0, v1, w in units if e == "V" and v0 <= c0 < v1)
+                three = [([eye, full("I2"), full("I3")][nv], reg(tab, par0 + c0, par0 + c1))]
+                three += [(eye, reg("FM%d%d" % (r, b), c0, c1)) for b in range(2)]
             else:
-                x, x2 = reg(cfg["xbanks"][0], 0, n), reg(cfg["xbanks"][1], 0, n)
-                for j in range(3):
-                    mm(x, full("I"), three[j], j == 0, j == 2)
-                act(reg("qr", c0, c1), x, AF.Identity, bias=QOFF - 0.5 + 2.0 ** -9, scale=2.0 ** -8)
-                for j in range(3):
-                    mm(x2, full("I"), three[j], j == 0, False)
-                mm(x2, full("nI256"), reg("qr", c0, c1), False, True)
-                for d0, m in outs:
-                    act(reg(nxt, d0, d0 + m), reg(x2[0], 0, m), AF.Identity, bias=QOFF * 256)
-            if last:
-                store("yc", "ycb", c0, c1, 2)
-            else:
-                send(r + 1, own0 + c0, own0 + c1, own0 + c0)
-                if len(outs) > 1:
-                    send(r + 1, 0, 8, TW)
-            fb = "B%d" % (4 + (r * len(chunks) + ci) % 2)
+                three = [(eye, reg(tab, own0 + c0, own0 + c1))]
+                three += [(eye, reg("M", mcol(c0) + 7 + 8 * b, mcol(c0) + 16 * n, 16)) for b in range(2)]
+            nxt = ("ypt" if folded else "ycb") if last else "tab%d" % (r + 1)
+            d0 = c0 if last else (par0 if folded else own0) + c0
+            x, x2 = [reg(b, 0, n) for b in cfg["xbanks"]]
+            for i, (w, xx) in enumerate(three):
+                mm(x, w, xx, i == 0, i == 2, far)
+            act(reg("qr", c0, c1), x, AF.Identity, bias=QOFF - 0.5 + 2.0 ** -9, scale=2.0 ** -8)
+            for i, (w, xx) in enumerate(three):
+                mm(x2, w, xx, i == 0, False, far)
+            mm(x2, full("nI256"), reg("qr", c0, c1), False, True)
+            act(reg(nxt, d0, d0 + n), x2, AF.Identity, bias=QOFF * 256)
+            if not last:
+                send(r + 1, d0, d0 + n, rank == 0 and c0 == 0)
+                if c0 == 0:
+                    act(reg(nxt, TW, TW + 8), reg(x2[0], 0, 8), AF.Identity, bias=QOFF * 256)
+                    ops[-1]["only0"] = True
+                return
+            if folded:
+                src, dst = reg("ypt", c0, c1), reg("ycb", c0, c1)
+                add("G", ([([src], [dst])], "par", "loc"), [src], [dst], "r", 2 * n, sig=("yb%d" % j, None), rows=128)
+            store("yc", "ycb", c0, c1, 2)
+
+        def counts(c0, c1):
+            n = c1 - c0
+            fb = cfg["fbanks"][nf[0] % len(cfg["fbanks"])]
+            nf[0] += 1
             F, Cc = reg(fb, 0, n), reg(fb, 256, 256 + n)
-            terms = [(full("I"), reg("nth", c0, c1))]
-            ks = [(reg("E" if k < 16 - nw else "Eh", 15 - k, 143 - k),
-                   reg("CM", 16 * c0 + k * n, 16 * c0 + (k + 1) * n)) for k in range(16)]
-            terms = ks + terms if (r == 0 and ci == 0) else terms + ks
-            for j, (w, xx) in enumerate(terms):
-                mm(F, w, xx, j == 0, j == len(terms) - 1)
-            act(reg("sg", c0, c1), F, AF.Sign, bias=reg("wb", nw, nw + 1) if nw else 0.5)
-            mm(Cc, full("tri"), reg("sg", c0, c1), True, True)
-            act(reg("any%d" % r, c0, c1), Cc, AF.Sign, bias=reg("kcol", 0, 1), scale=-1.0)
+            st = signset(c0)
+            ks = []
+            for k in range(16):
+                if r0 <= c0 < r1:
+                    u = [i for i, x in enumerate(units) if x[1] == k // 8 and x[2] <= c0 < x[3]][0]
+                    a = ubase[u] + (k % 8) * (units[u][3] - units[u][2]) + c0 - units[u][2]
+                else:
+                    a = 16 * c0 + k * n
+                half = any(k0 <= k < k1 for k0, k1 in st)
+                ks.append((k, a, reg("hv", 0, 8) if half else reg("ones", 0, 8)))
+            ks.sort(key=lambda t: max(i for i, o in enumerate(ops) if o["wr"] and o["wr"][0][0] == "CM"
+                                      and o["wr"][0][1] <= t[1] < o["wr"][0][2]))
+            low = cfg["boost"]["F"]
+            for j in range(0, n, 128):
+                mm(reg(fb, j, j + 128), reg("nth", c0 + j, c0 + j + 128), eye, j == 0, False, boost=low)
+            for i, (k, a, x) in enumerate(ks):
+                for j in range(0, n, 128):
+                    mm(reg(fb, j + k, j + 128, 16), reg("CM", a + j, a + j + 128), x, False,
+                       i == 15 and j == n - 128, boost=low)
+            sg, run = reg("sg", c0, c1), reg("run", c0, c1)
+            act(sg, F, AF.Sign, bias=0.5)
+            add("V", lambda g, T: g.vector.tensor_tensor_scan(ap(T, run), T.r16[:, 0:n], ap(T, sg), 1.0, ALU.max, ALU.min),
+                [sg, reg("r16", 0, 256)], [run], "v", n * 0.5)
+            for j in range(0, n, 128):
+                mm(reg(fb, j, j + 128), reg("run", c0 + j, c0 + j + 128), eye, True, True)
+            if not last:
+                mm(Cc, full("nI"), reg("cpb", c0, c1), True, False)
+                for j in range(0, n, 128):
+                    mm(reg(fb, 256 + j, 256 + j + 128), reg("run", c0 + j, c0 + j + 128), eye, False, j == n - 128)
+            act(reg("any%d" % r, c0, c1), F, AF.Identity, bias=0.5, scale=-0.5)
             if last:
                 for j in range(RO):
-                    mm(F, full("Dm"), reg("any%d" % j, c0, c1), j == 0, j == RO - 1)
-                tt(reg("ygb", c0, c1), F, reg("gpi", c0, c1), ALU.add)
+                    mm(Cc, full("Dm"), reg("any%d" % j, c0, c1), j == 0, j == RO - 1)
+                tt(reg("ygb", c0, c1), Cc, reg("gpi", c0, c1), ALU.add)
                 store("yg", "ygb", c0, c1, 4)
             else:
-                mm(F, full("nI"), reg("cpb", c0, c1), True, False)
-                mm(F, full("n2I"), reg("any%d" % r, c0, c1), False, True)
-                act(reg("Y", c0, c1), F, AF.Abs, bias=2.0)
+                act(reg("Y", c0, c1), Cc, AF.Abs, bias=1.0)
+
+        steps = {"gn": natural, "gu": unit, "cn": lambda j: compare("n", j), "cu": lambda j: compare("u", j),
+                 "f": lambda j: counts(*cfg["cnt"][j]), "r": registers, "o": fold, "s": keep}
+        for word in cfg["seq"].split():
+            steps[word[:-1]](int(word[-1]))
     return ops
 
 
@@ -324,7 +494,9 @@ def link(ops):
         pre = {}
         for rs, iswr in ((o["rd"], False), (o["wr"], True)):
             for name, lo, hi, step in rs:
-                for j, a, b, w in hist.get(name, []):
+                for j, a, b, w, st in hist.get(name, []):
+                    if isinstance(st, tuple) and isinstance(step, tuple) and (st[3] <= step[2] or step[3] <= st[2]):
+                        continue
                     if (w or iswr) and a < hi and lo < b and j != i:
                         both_pe = ops[j]["q"] == "P" and o["q"] == "P"
                         pre[j] = pre.get(j, False) or not both_pe
@@ -338,7 +510,7 @@ def link(ops):
                 h = hist.setdefault(name, [])
                 if iswr and step == 1:
                     h[:] = [e for e in h if not (lo <= e[1] and e[2] <= hi)]
-                h.append((i, lo, hi, iswr))
+                h.append((i, lo, hi, iswr, step))
         o["pre"] = pre
     return ops
 
@@ -348,19 +520,19 @@ def cost(o, e):
     if k == "v":
         return e["ov"] + max(64, n) * e["cyc"], 0, 0
     if k == "vg":
-        return e["ov"] + n * e["g"] * e["cyc"], 0, 0
+        return 50 + n * e["g"] * e["cyc"], 0, 0
     if k == "a":
         return e["oa"] + max(64, n) * e["cyc"], 0, 0
     if k == "ag":
-        return e["oa"] + n * e["g"] * e["cyc"], 0, 0
+        return 65 + n * e["g"] * e["cyc"], 0, 0
     if k == "p":
         return e["op"] + n * e["pe"], 0, 0
     if k == "g":
         return 170 + 2 * n * e["cyc"], 0, 0
-    move = o["rows"] / 16 * e["drow"] + 8 * n / e["dbw"]
+    move = o["rows"] / 16 * e["drow"] * (e["frow"] if k == "f" else 1) + 8 * n / e["dbw"] * (e["fb"] if k == "f" else 1)
     if k == "d":
         return 60, move, e["dfix"]
-    return e["riss"], move, e["rfix"]
+    return e["riss"] + (e["rfirst"] if o["first"] else 0), move, e["rfix"]
 
 
 def schedule(ops, e, delta):
@@ -369,16 +541,12 @@ def schedule(ops, e, delta):
     for i, o in enumerate(ops):
         for j in o["pre"]:
             succ[j].append(i)
-    prio = [0.0] * n
-    for i in range(n - 1, -1, -1):
-        prio[i] = sum(cost(ops[i], e)) + max([prio[j] + e["sem"] for j in succ[i]] + [0.0])
-    for i in range(n):
-        prio[i] += ops[i].get("boost", 0.0)
+    prio = [o["boost"] for o in ops]
     left = [len(o["pre"]) for o in ops]
     fin, ready = [0.0] * n, [0.0] * n
     cand = {q: [] for q in "VAPGS"}
     free = {q: 0.0 for q in "VAPGS"}
-    order = {q: [] for q in "VAPGS"}
+    start = [0.0] * n
     dma = [0.0]
     for i in range(n):
         if left[i] == 0:
@@ -391,9 +559,9 @@ def schedule(ops, e, delta):
         else:
             i = max((i for i in cand[q] if ready[i] <= t + delta), key=lambda i: (prio[i], -i))
         cand[q].remove(i)
-        order[q].append(i)
         a, b, c = cost(ops[i], e)
         st = max(free[q], ready[i])
+        start[i] = st
         free[q] = st + a
         if b:
             dma[0] = max(dma[0], st + a + c) + b
@@ -405,24 +573,88 @@ def schedule(ops, e, delta):
             left[j] -= 1
             if left[j] == 0:
                 cand[ops[j]["q"]].append(j)
-    return order
+    return justify(ops, e, start)
+
+
+def justify(ops, e, start, rounds=6):
+    n = len(ops)
+    res, dur, pre = [o["q"] for o in ops], [cost(o, e)[0] for o in ops], [[] for o in ops]
+    out, key = list(range(n)), list(start)
+    for i, o in enumerate(ops):
+        a, b, c = cost(o, e)
+        if b:
+            out[i] = len(res)
+            res.append("D")
+            dur.append(b)
+            pre.append([(i, c)])
+            key.append(start[i])
+    for i, o in enumerate(ops):
+        pre[i] = [(out[j], e["sem"] if w else 0.0) for j, w in o["pre"].items()]
+    m = len(res)
+    suc = [[] for _ in range(m)]
+    for i in range(m):
+        for j, lag in pre[i]:
+            suc[j].append((i, lag))
+
+    def place(before, after, rank):
+        left, ready, at = [len(x) for x in before], [0.0] * m, [0.0] * m
+        busy = {q: [] for q in "VAPGSD"}
+        cand = [(rank[i], i) for i in range(m) if not left[i]]
+        while cand:
+            pick = min(cand)
+            cand.remove(pick)
+            i = pick[1]
+            b, t = busy[res[i]], ready[i]
+            p = len(b)
+            while p and b[p - 1][1] > t:
+                p -= 1
+            while p < len(b) and b[p][0] < t + dur[i]:
+                t = b[p][1]
+                p += 1
+            b.insert(p, (t, t + dur[i]))
+            at[i] = t
+            for j, lag in after[i]:
+                ready[j] = max(ready[j], t + dur[i] + lag)
+                left[j] -= 1
+                if not left[j]:
+                    cand.append((rank[j], j))
+        return at
+
+    best = None
+    for _ in range(rounds):
+        at = place(pre, suc, key)
+        end = max(at[i] + dur[i] for i in range(m))
+        if best is None or end < best[0]:
+            best = (end, at)
+        back = place(suc, pre, [-(at[i] + dur[i]) for i in range(m)])
+        key = [-(back[i] + dur[i]) for i in range(m)]
+    return {q: sorted((i for i in range(n) if res[i] == q), key=lambda i: (best[1][i], i)) for q in "VAPGS"}
+
+
+ORDER = []
 
 
 def rank_program(g, core, T, topo):
     rank = T.rank_of(core)
     if rank is None:
         return
-    ops = link(build(rank, CFG))
-    order = schedule(ops, EST, CFG["delta"])
-    peers = [c for c in T.cores if c != core]
-    mask = -1
-    for c in peers:
-        mask &= topo.mask(core, c)
-    neng = bin(mask).count("1")
-    dst_ids = [DstId(rid=topo.addr(c)[0], pnc=topo.addr(c)[1]) for c in peers]
-    total = {"loc": 0, "outs": 0, "arr0": 2 * (NR - 1) * neng}
+    by_die = sorted(range(NR), key=lambda q: (topo.die(T.cores[q]), q))
+    par = by_die[by_die.index(rank) ^ 1]
+    if not ORDER:
+        ORDER.append(schedule(link(build(0, 1, CFG)), EST, CFG["delta"]))
+    order = ORDER[0]
+    every = build(rank, par, CFG)
+    keep = [i for i, o in enumerate(every) if rank == 0 or not o.get("only0")]
+    where = {i: j for j, i in enumerate(keep)}
+    order = {q: [where[i] for i in order[q] if i in where] for q in order}
+    ops = link([every[i] for i in keep])
+    dests = {"all": [c for c in T.cores if c != core], "par": [T.cores[par]]}
+    engines = [e for e in topo.engines(core, T.cores[par]) if all(e in topo.engines(core, c) for c in dests["all"])]
+    neng = len(engines)
+    total = {s: 0 for s in SEMAPHORES}
+    total["arr0"] = 2 * (NR - 1) * neng
     for r in range(1, RO):
-        total["arr%d" % r] = (len(CFG["chunks"]) * (NR - 1) + (1 if rank else 0)) * neng
+        total["arr%d" % r] = (len(CFG["reg"]) * (NR - 1) + (1 if rank else 0)) * neng
     for q in "VAPGS":
         k = 0
         for i in order[q]:
@@ -431,9 +663,11 @@ def rank_program(g, core, T, topo):
                 k += 1
                 o["sig"] = (ENGSEM[q], k)
                 total[ENGSEM[q]] = k
-            elif o["kind"] == "r":
+            elif o["kind"] in "rf":
+                if o["fn"][1] == "par":
+                    total[o["sig"][0]] = neng
                 o["sig"] = (o["sig"][0], total[o["sig"][0]])
-                total["loc"] += neng
+                total[o["fn"][2]] += neng
             elif o["sig"][0] == "outs":
                 total["outs"] += 16
             else:
@@ -447,17 +681,26 @@ def rank_program(g, core, T, topo):
             for j, w in o["pre"].items():
                 if w:
                     s, val = ops[j]["sig"]
+                    if ops[j]["kind"] == "f" and all(x[0][:2] != "FM" for x in o["rd"]):
+                        s = ops[j]["fn"][2]
+                        val = total[s]
                     need[s] = max(need.get(s, 0), val)
             for s in sorted(need):
                 if need[s] > seen.get(s, 0):
                     queue[q].wait_ge(T.sem[s], need[s])
                     seen[s] = need[s]
-            if o["kind"] == "r":
-                tab, s0, s1, d0, arr = o["fn"][1:]
+            if o["kind"] in "rf":
+                moves, to, loc = o["fn"]
+                ids = [DstId(rid=topo.addr(c)[0], pnc=topo.addr(c)[1]) for c in dests[to]]
+                share = neng // len(moves)
                 g.remote_dma_fused([RemoteDMATransfer(
-                    dst_ids=dst_ids, dma_engine_mask=mask, remote_sem=T.sem[arr], src=T[tab][:, s0:s1],
-                    dsts=[T[tab][:, d0:d0 + s1 - s0] for _ in peers])], local_sem=T.sem.loc)
+                    dst_ids=[d for x in dsts for d in ids],
+                    dma_engine_mask=sum(1 << e for e in engines[share * m:share * (m + 1)]),
+                    remote_sem=T.sem[o["sig"][0]], srcs=[T[x[0]][:, x[1]:x[2]] for x in srcs],
+                    dsts=[T[x[0]][:, x[1]:x[2]] for x in dsts for d in ids], alu_op=2 if len(srcs) > 1 else 0)
+                    for m, (srcs, dsts) in enumerate(moves)], local_sem=T.sem[loc])
             else:
                 o["fn"](g, T).then_inc(T.sem[o["sig"][0]], 16 if o["kind"] == "d" else 1)
     for s in SEMAPHORES:
-        g.sync.wait_ge(T.sem[s], total[s])
+        if total[s]:
+            g.sync.wait_ge(T.sem[s], total[s])

@@ -9,29 +9,36 @@ BIG = 65536.0
 QOFF = 129.0
 
 CFG = {
-    "lm": (128, 1024),
-    "nat": [(0, 128, "A")],
-    "units": [("A", 0, 128, 384, 0), ("V", 1, 128, 384, 0), ("A", 0, 384, 640, 0), ("V", 1, 384, 640, 0),
-              ("A", 0, 640, 896, 8), ("A", 1, 640, 896, 2), ("A", 0, 896, 1024, 0), ("V", 1, 896, 1024, 0)],
+    "lm": (128, (896, 896, 896)),
+    "nat": [(0, 128, "AA", 128), (896, 1024, "AA", 128)],
+    "sign": "V",
+    "units": [("AAA", 0, 128, 384, 8), ("VVV", 1, 128, 384, 2), ("AAA", 0, 384, 640, 4),
+              ("VVV", 1, 384, 640, 8), ("AAA", 0, 640, 896, 0), ("VVV", 1, 640, 896, 0)],
     "cnt": [(0, 128), (128, 384), (384, 640), (640, 896), (896, 1024)],
     "reg": [(0, 128), (128, 384), (384, 640), (640, 896), (896, 1024)],
     "links": {"A": 4, "V": 2},
+    "call": {"A": 1024, "V": 512},
     "dbanks": ["B0", "B1"],
     "fbanks": ["B4", "B5", "B6"],
-    "xbanks": ["B7", "B7"],
+    "xbanks": ["71", "77", "77", "10", "77"],
+    "thwait": ("far0", 0, 999),
+    "nthwait": ("L2", 0, 896),
+    "cut": 192,
     "turn": [1, 0],
-    "seq": "gn0 gu0 o0 gu1 o1 cn0 f0 r0 gu2 o2 s0 s1 cu1 cu0 f1 gu3 o3 gu4 o4 cu4 gu5 o5 r1 cu3 cu2 f2 gu7 o7 gu6 o6 "
-           "r2 cu5 f3 cu7 cu6 f4 r3 r4",
-    "folds": [[0], [1], [2], [3], [4], [5], [6], [7]],
+    "seq": ["gu0 cu0 gu2 gn0 gu1 gu3 r0 gu4 o1 cn0 o0 o4 o3 gu5 o5 r1 f0 o2 cu2 r2 cu1 f1 gn1 cu5 r3 cu3 cu4 f2 cn1 f3 "
+            "r4 f4"] * 3,
+    "folds": [[0], [1], [2], [3], [4], [5]],
     "hop1": [(0, 768), (768, 1024)],
     "c0a": 128,
-    "loads": ["c0a", "c0b", "cp0", "gp0", "cp1", "gp1", "rfs"],
+    "loads": ["c0a", "c0b", "cp0", "gp0", "cp1", "rfs", "gp1", "gp2"],
+    "gaps": [(0, 512), (512, 768), (768, 1024)],
+    "late": ["f0"],
     "delta": 0.0,
-    "boost": {"VP": 5, "VM": 5, "VCM": 5, "VS16T": 2, "VS16": 8, "Vnth": 6, "AP": 5, "F": 5},
+    "boost": {"VP": 5, "VM": 5, "VCM": 5, "VST": 2, "VS16": 8, "Vnth": 6, "AP": 5, "F": 5},
 }
-EST = {"cyc": 0.87, "g": 1.56, "ov": 40.0, "oa": 45.0, "pe": 0.48, "op": 15.0, "sem": 100.0,
-       "dfix": 2000.0, "drow": 15.0, "dbw": 22.0, "rfix": 2200.0, "riss": 600.0, "rfirst": 3000.0,
-       "frow": 4.0, "fb": 0.8}
+EST = {"cyc": 0.9, "g": 1.56, "ov": 30.0, "oa": 30.0, "pe": 0.5, "op": 5.0, "sem": 90.0,
+       "dfix": 1800.0, "drow": 14.0, "dbw": 24.0, "rfix": 2000.0, "riss": 600.0, "rfirst": 2000.0,
+       "frow": 6.0, "fb": 0.9, "fx": 500.0}
 
 SCRATCH = {}
 
@@ -45,30 +52,32 @@ _decl("cpi gpi thi s2i s2m", "sbuf", [128, V], "int32")
 _decl("rfi", "sbuf", [128, 64], "int32")
 _decl("pcol pand", "sbuf", [128, 8], "int32")
 _decl("rf16", "sbuf", [128, 64], "uint16")
-_decl("L L2", "sbuf", [128, V], "uint16")
+_decl("L", "sbuf", [128, V], "uint16")
 _decl("tab0 tab1 tab2", "sbuf", [128, TW + 256], "bfloat16")
 _decl("P CM", "sbuf", [128, 16 * V], "bfloat16")
 _decl("M", "sbuf", [128, 8 * V], "bfloat16")
 _decl("rst", "sbuf", [128, 1024], "bfloat16")
-_decl("nog S16 hT h21 h22", "sbuf", [128, V], "float16")
+_decl("nog S16 h21 h22", "sbuf", [128, V], "float16")
 _decl("ycb ypt cpb nth sg run any0 any1 any2 Y h1 qr", "sbuf", [128, V], "bfloat16")
 _decl("FM00 FM01 FM10 FM11 FM20 FM21", "sbuf", [128, V], "bfloat16")
 _decl("ygb Gw Hw Y2 S1", "sbuf", [128, V], "float32")
 _decl("lo", "sbuf", [128, 512], "bfloat16")
 _decl("I nI I2 I3 I256 nI256 n2I nBI tri0 tri sh Dm Z", "sbuf", [128, 128], "bfloat16")
-_decl("ones J", "sbuf", [128, 160], "bfloat16")
+_decl("J", "sbuf", [128, 160], "bfloat16")
+_decl("ones", "sbuf", [128, 256], "bfloat16")
 _decl("J0 J1", "sbuf", [128, 160], "float16")
 _decl("ntri16 I16", "sbuf", [128, 128], "float16")
 _decl("r16", "sbuf", [128, 256], "bfloat16")
 _decl("hv", "sbuf", [128, 8], "bfloat16")
-_decl("kcol wb wc", "sbuf", [128, 24], "float32")
-_decl("B0 B1", "psum", [128, 8, 64], "float32")
+_decl("kcol", "sbuf", [128, 8], "float32")
+_decl("wb", "sbuf", [128, 64, 16], "bfloat16")
+_decl("B0 B1", "psum", [128, 32, 16], "float32")
 _decl("B2 B3 B4 B5 B6 B7", "psum", [128, 512], "float32")
-_decl("ST", "sbuf", [128, 16, 64], "float32")
-_decl("I32", "sbuf", [128, 128], "float32")
+_decl("hT0 hT1 hT2", "sbuf", [128, 32, 32], "float16")
+_decl("L2", "sbuf", [128, 4, 256], "uint16")
 _decl("cw", "sbuf", [128, 4 * V], "bfloat16")
 
-SEMAPHORES = (["sV", "sA", "sP", "sG", "c0a", "c0b", "cp0", "cp1", "gp0", "gp1", "rfs", "ths", "outs",
+SEMAPHORES = (["sV", "sA", "sP", "sG", "c0a", "c0b", "cp0", "cp1", "gp0", "gp1", "gp2", "rfs", "ths", "outs",
                "arr0", "arr1", "arr2", "loc", "fl0", "fl1", "fl2"]
               + ["f%d_%d" % (r, u) for r in range(RO) for u in range(len(CFG["folds"]))]
               + ["yb%d" % j for j in range(len(CFG["reg"]))])
@@ -87,24 +96,26 @@ def build(rank, par, cfg):
     def reg(name, lo, hi, step=1):
         return (name, lo, hi, step)
 
-    def box(name, ra, rb, ca, cb):
+    def box(name, ra, rb, ca, cb, step=1):
         w = SCRATCH[name][1][2]
-        return (name, ra * w + ca, (rb - 1) * w + cb, (ra, rb, ca, cb))
+        return (name, ra * w + ca, (rb - 1) * w + cb, (ra, rb, ca, cb, step))
 
     def ap(T, r):
         name, lo, hi, step = r
         if isinstance(step, tuple):
-            return T[name][:, step[0]:step[1], step[2]:step[3]]
+            if step[1] - step[0] == 1:
+                return T[name][:, step[0], step[2]:step[3]]
+            return T[name][:, step[0]:step[1], step[2]:step[3]:step[4]]
         if len(SCRATCH[name][1]) == 3:
             w = SCRATCH[name][1][2]
             if lo // w == (hi - 1) // w:
                 return T[name][:, lo // w, lo % w:(hi - 1) % w + 1:step]
-            return T[name][:, lo // w:hi // w, :]
+            return T[name][:, lo // w:hi // w, lo % w::step]
         return T[name][:, lo:hi:step] if step != 1 else T[name][:, lo:hi]
 
     def cnt(r):
         if isinstance(r[3], tuple):
-            return (r[3][1] - r[3][0]) * (r[3][3] - r[3][2])
+            return (r[3][1] - r[3][0]) * ((r[3][3] - r[3][2] + r[3][4] - 1) // r[3][4])
         return (r[2] - r[1] + r[3] - 1) // r[3]
 
     def memset(o, c, half=True):
@@ -175,10 +186,8 @@ def build(rank, par, cfg):
             rows=128 * (NR - 1))
 
     own0, par0 = V * rank, V * par
-    r0, r1 = cfg["lm"]
-    nb = (r1 - r0) // 16
+    r0, ends = cfg["lm"]
     nat, units = cfg["nat"], cfg["units"]
-    natr = [(a, b) for a, b in ((0, r0), (r1, V)) if a < b]
     ca = cfg["c0a"]
     ubase, at = [], 16 * r0
     for u in units:
@@ -186,130 +195,125 @@ def build(rank, par, cfg):
         at += 8 * (u[3] - u[2])
 
     def ulist(u, ka, kb):
-        m = (units[u][3] - units[u][2]) // 16
-        return reg("L2", ubase[u] // 16 - r0 + ka * m, ubase[u] // 16 - r0 + kb * m)
+        c, at = (units[u][2] - r0) // 256, 128 * units[u][1]
+        return box("L2", c, c + 1, at + 16 * ka, at + 16 * kb)
 
     def mcol(v):
-        return 16 * (v if v <= r0 else v - r1 + r0)
+        return 16 * (v if v < r0 else v - ends[-1] + r0)
 
     def signset(c0):
         return tuple((8 * b + 8 - w, 8 * b + 8) for e, b, v0, v1, w in units if w and v0 <= c0 < v1)
 
-    sets = sorted(set(signset(c0) for c0, c1 in cfg["cnt"]) - {()})
+    sets = sorted(set(signset(c0) for c0 in range(0, V, 128)) - {()})
 
     loads = {"c0a": ("tab0", "c0", 0, ca, own0, 2), "c0b": ("tab0", "c0", ca, V, own0 + ca, 2),
              "cp0": ("cpi", "cp", 0, 512, 0, 4), "cp1": ("cpi", "cp", 512, V, 512, 4),
-             "gp0": ("gpi", "gp", 0, 512, 0, 4), "gp1": ("gpi", "gp", 512, V, 512, 4),
              "rfs": ("rfi", "rf", 0, 64, 0, 4)}
+    for j, (a, b) in enumerate(cfg["gaps"]):
+        loads["gp%d" % j] = ("gpi", "gp", a, b, a, 4)
     for s in cfg["loads"]:
         load("S", *loads[s][:5], s, loads[s][5])
-    memset(reg("ones", 0, 160), 1.0)
-    add("G", lambda g, T: g.affine_select(T.J[:], T.ones[:], [[-1, 160]], ALU.is_equal, 0.0, 16, 1),
+    memset(reg("ones", 0, 256), 1.0)
+    add("G", lambda g, T: g.affine_select(T.J[:], T.ones[:, 0:160], [[-1, 160]], ALU.is_equal, 0.0, 16, 1),
         [reg("ones", 0, 160)], [reg("J", 0, 160)], "g", 160)
     add("G", lambda g, T: g.affine_select(T.tri0[:], T.ones[:, 0:128], [[1, 128]], ALU.is_ge, 0.0, 0, -1),
         [full("ones")], [full("tri0")], "g", 128)
     add("G", lambda g, T: g.affine_select(T.tri[:], T.tri0[:], [[-16, 8], [0, 16]], ALU.is_ge, 0.0, 0, 1),
         [full("tri0")], [full("tri")], "g", 128)
-    add("G", lambda g, T: g.iota(T.lo[:], [[0, 2], [1, 256]], 0, 0, allow_small_or_imprecise_dtypes=True),
-        [], [reg("lo", 0, 512)], "g", 512)
-    send(0, own0, own0 + ca)
-    ops[-1]["first"] = True
-    send(0, own0 + ca, own0 + V)
     add("G", lambda g, T: g.iota(T.pcol[:, 0:1], [[0, 1]], 0, 1), [], [reg("pcol", 0, 1)], "g", 1)
     add("G", lambda g, T: g.affine_select(T.sh[:], T.tri[:], [[1, 128]], ALU.is_equal, 0.0, -1, -1),
         [full("tri")], [full("sh")], "g", 128)
-    load("S", "thi", "th", 0, V, 0, "ths", 4, extra=[reg("far0", 0, 999)])
+    send(0, own0, own0 + ca)
+    ops[-1]["first"] = True
+    ops[-1]["rd"] += [full("tri"), full("J"), reg("pcol", 0, 1)]
+    send(0, own0 + ca, own0 + V)
+    for a in (0, 256):
+        add("V", lambda g, T, a=a: g.vector.tensor_tensor_scan(T.lo[:, a:a + 256], T.ones[:], T.ones[:], -1.0, ALU.mult,
+                                                               ALU.add), [reg("ones", 0, 256)], [reg("lo", a, a + 256)],
+            "v", 128)
+    load("S", "thi", "th", 0, V, 0, "ths", 4, extra=[reg(*cfg["thwait"])])
     eye = reg("J", 16, 144)
     tscal(full("ntri16"), full("tri"), -1.0, None, ALU.mult, half=True)
-    for name, c in (("nBI", -4 * BIG), ("I16", 1.0), ("I32", 1.0), ("nI", -1.0), ("I256", 256.0), ("nI256", -256.0),
+    for name, c in (("nBI", -4 * BIG), ("I16", 1.0), ("nI", -1.0), ("I256", 256.0), ("nI256", -256.0), ("n2I", -2.0),
                     ("I2", 2.0), ("I3", 3.0), ("Z", 0.0)):
         tscal(full(name), eye, c, None, ALU.mult, half=True)
     memset(reg("rst", 0, 1024), 1.0)
     memset(reg("rst", 0, 1024, 8), 0.0)
     memset(reg("hv", 0, 8), 0.5)
-    memset(reg("r16", 0, 256), -1.0)
-    memset(reg("r16", 0, 256, 16), 1.0)
-    tscal(reg("pand", 0, 1), reg("pcol", 0, 1), 15, None, ALU.bitwise_and)
-    tscal(reg("kcol", 0, 1), reg("pand", 0, 1), 1.0, None, ALU.add)
+    memset(reg("r16", 0, 256), 1.0)
+    memset(reg("r16", 0, 256, 16), 0.0)
     tscal(reg("pand", 1, 2), reg("pcol", 0, 1), 16, None, ALU.bitwise_and)
     tscal(reg("kcol", 1, 2), reg("pand", 1, 2), 8.0, None, ALU.is_lt)
     tscal(reg("kcol", 2, 3), reg("pand", 1, 2), 8.0, None, ALU.is_gt)
     for j in range(2):
         tscal(reg("J%d" % j, 0, 160), reg("J", 0, 160), reg("kcol", 1 + j, 2 + j), None, ALU.mult, half=True)
-    nw = [0]
     for si, st in enumerate(sets):
-        cur = 0.0
+        memset(reg("wb", 128 * si, 128 * si + 128), 0.0)
         for k0, k1 in st:
-            a, b, c = reg("wc", nw[0], nw[0] + 1), reg("wc", nw[0] + 1, nw[0] + 2), reg("wc", nw[0] + 2, nw[0] + 3)
-            nw[0] += 3
-            tscal(a, reg("kcol", 0, 1), k0 + 0.5, 64.0, ALU.is_gt, ALU.mult)
-            tscal(b, reg("kcol", 0, 1), k1 + 0.5, -64.0, ALU.is_gt, ALU.mult)
-            o = reg("wb", si, si + 1) if (k0, k1) == st[-1] else c
-            tscal(o, a, b, cur, ALU.add, ALU.add)
-            cur = o
+            memset(box("wb", 8 * si, 8 * si + 8, k0, k1), 0.5)
     tt(full("Dm"), eye, full("sh"), ALU.subtract, 2)
     vcopy(reg("rf16", 0, 64), reg("rfi", 0, 64))
 
-    def turn(src, first):
-        n = r1 - r0
-        add("V", lambda g, T: g.vector.transpose(T.hT[:, 0:n], T[src][:, r0:r1]), [reg(src, r0, r1)],
-            [reg("hT", 0, n)], "v", n * 0.5)
+    def turn(src, r):
+        nb = (ends[0] - r0) // 32
+        out = reg("hT%d" % r, 0, 32 * nb)
+        add("V", lambda g, T: g.vector.transpose(ap(T, out), T[src][:, r0:ends[0]]), [reg(src, r0, ends[0])], [out],
+            "v", 16 * nb)
         for h in cfg["turn"]:
-            bank = "B%d" % h
-            if first:
-                mm(box(bank, 0, 8, 0, nb), full("Z"), reg("lo", 0, 8 * nb), True, False)
-            else:
-                mm(box(bank, 0, 8, 0, nb), full("I32"), box("ST", 8 * h, 8 * h + 8, 0, nb), True, False)
-                ops[-1]["n"] *= 4
+            terms = [(j, d, c) for j in range(r + 1) for d in range(2) for c in range(2)]
+            for j, d, c in terms:
+                mm(box("B%d" % h, 0, nb, 8 * d, 8 * d + 8), reg("J%d" % d, 16 + 16 * (d - c), 144 + 16 * (d - c)),
+                   box("hT%d" % j, 0, nb, 16 * c + 8 * h, 16 * c + 8 * h + 8), (j, d, c) == terms[0],
+                   (j, d, c) == terms[-1])
             for kk in range(8):
-                for d in range(2):
-                    for c in range(2):
-                        w = reg("J%d" % d, 16 + 16 * (d - c), 144 + 16 * (d - c))
-                        mm(reg(bank, kk * 64 + d, kk * 64 + nb, 2), w, reg("hT", 16 * c + 8 * h + kk, n, 32), False,
-                           (kk, d, c) == (7, 1, 1))
-            for u, (eng, blk, v0, v1, w) in enumerate(units):
-                if blk == h:
-                    tscal(ulist(u, 0, 8), box(bank, 0, 8, (v0 - r0) // 16, (v1 - r0) // 16), TW / 2, None, ALU.add)
+                at = 128 * h + 16 * kk
+                tscal(box("L2", 0, nb // 8, at, at + 16), box("B%d" % h, 0, nb, kk, 16, 8), TW / 2, None, ALU.add)
 
     for h in range(2):
-        a, b = 512 * h, 512 * h + 512
-        nown, z1, z2 = reg("B%d" % (4 + h), 0, 512), reg("B%d" % (6 + h), 0, 512), reg("B%d" % (2 + h), 0, 512)
-        tscal(nown, reg("cpi", a, b), -1.0, None, ALU.add)
-        act(reg("cpb", a, b), nown, AF.Identity, bias=1.0)
-        tt(reg("nog", a, b), reg("gpi", a, b), nown, ALU.mult)
-        mm(z1, eye, reg("lo", 0, 512), True, False)
-        mm(z1, full("ntri16"), reg("nog", a, b), False, True)
-        mm(z2, eye, reg("lo", 0, 512), True, False)
+        a = 512 * h
+        vcopy(reg("cpb", a, a + 512), reg("cpi", a, a + 512))
+        mm(reg("B%d" % (4 + h), 0, 512), eye, reg("cpb", a, a + 512), True, False)
+        for j in (0, 256):
+            mm(reg("B%d" % (4 + h), j, j + 256), full("nI"), reg("ones", 0, 256), False, j == 256)
+    for h, (a, b) in enumerate(cfg["gaps"]):
+        n = b - a
+        z1, z2 = reg("B%d" % (6 + h % 2), 0, n), reg("B" + "230"[h], 0, n)
+        tt(reg("nog", a, b), reg("gpi", a, b), reg("B%d" % (4 + a // 512), a % 512, a % 512 + n), ALU.mult)
+        mm(z2, eye, reg("lo", 0, n), True, False)
         mm(z2, full("nBI"), reg("cpb", a, b), False, False)
         mm(z2, full("ntri16"), reg("nog", a, b), False, True)
-        for j in range(2):
-            act(reg("Gw", a + 256 * j, a + 256 * j + 256), reg(z1[0], 256 * j, 256 * j + 256), AF.Identity,
-                bias=float(own0 + a + 256 * j))
-        for j in range(2):
-            tscal(reg("Hw", a + 256 * j, a + 256 * j + 256), reg(z2[0], 256 * j, 256 * j + 256),
-                  float(own0 + a + 256 * j) + BIG, 0.0, ALU.add, ALU.max)
-        for j in range(2):
-            act(reg("Y2", a + 256 * j, a + 256 * j + 256), reg(z2[0], 256 * j, 256 * j + 256), AF.Relu,
-                bias=float(own0 + a + 256 * j) + 2 * BIG)
+        mm(z1, eye, reg("lo", 0, n), True, False)
+        mm(z1, full("ntri16"), reg("nog", a, b), False, True)
+        for j in range(0, n, 256):
+            act(reg("Gw", a + j, a + j + 256), reg(z1[0], j, j + 256), AF.Identity, bias=float(own0 + a + j))
+        for j in range(0, n, 256):
+            tscal(reg("Hw", a + j, a + j + 256), reg(z2[0], j, j + 256), float(own0 + a + j) + BIG, 0.0, ALU.add, ALU.max)
+        for j in range(0, n, 256):
+            act(reg("Y2", a + j, a + j + 256), reg(z2[0], j, j + 256), AF.Relu, bias=float(own0 + a + j) + 2 * BIG)
     hop("S1", "Gw", "Hw", 0, 512, ALU.max)
     hop("S1", "Gw", "Hw", 512, V, ALU.max)
-    for v0, v1 in natr[:1] + [(r0, r1)] + natr[1:]:
+    cuts = [0, r0, ends[0], V]
+    for j, (v0, v1) in enumerate(zip(cuts, cuts[1:])):
         hop("s2i", "S1", "Y2", v0, v1, ALU.max)
+        if j:
+            ops[-1]["rd"].append(reg("s2m", cuts[j - 1], v0))
         tscal(reg("s2m", v0, v1), reg("s2i", v0, v1), TW - 1, None, ALU.bitwise_and)
-        if v0 == r0:
+        if r0 <= v0 < ends[0]:
             tscal(reg("S16", v0, v1), reg("s2m", v0, v1), -TW / 2, None, ALU.add)
-            turn("S16", True)
+            turn("S16", 0)
         else:
             vcopy(reg("L", v0, v1), reg("s2m", v0, v1))
             tscal(reg("S16", v0, v1), reg("L", v0, v1), -TW / 2, None, ALU.add, half=True)
     for h in range(2):
         a, b = 512 * h, 512 * h + 512
-        mm(reg("B%d" % (4 + h), 0, 512), full("I256"), reg("cpb", a, b), True, True, boost=0)
+        lift = [c for c in range(a, b, 128) if signset(c)]
+        mm(reg("B%d" % (4 + h), 0, 512), full("I256"), reg("cpb", a, b), True, not lift, boost=0)
+        for c in lift:
+            si = sets.index(signset(c))
+            mm(reg("B%d" % (4 + h), c - a, c - a + 128), reg("wb", 128 * si, 128 * si + 128), full("ones"), False,
+               c == lift[-1], boost=0)
         tt(reg("nth", a, b), reg("B%d" % (4 + h), 0, 512), reg("thi", a, b), ALU.subtract)
-    for c0, c1 in cfg["cnt"]:
-        if signset(c0):
-            j = sets.index(signset(c0))
-            tscal(reg("nth", c0, c1), reg("nth", c0, c1), reg("wb", j, j + 1), None, ALU.add, half=True)
+        ops[-1]["rd"].append(reg(*cfg["nthwait"]))
 
     nd, nc, nf = [0], [0], [0]
     for r in range(RO):
@@ -317,41 +321,41 @@ def build(rank, par, cfg):
         win = reg(tab, 0, TW if r == 0 else TW + 8)
         far = [reg("far%d" % r, 0, 999)]
         last = r == RO - 1
+        r1 = ends[r]
         if r > 0:
             for v0, v1 in cfg["hop1"]:
                 hop("h1", "any%d" % (r - 1), "Y", v0, v1, ALU.is_ge)
-            for j, (v0, v1) in enumerate(natr[:1] + [(r0, r1)] + natr[1:]):
-                hop("h2%d" % r, "h1", "Y", v0, v1, ALU.is_ge)
+            for v0, v1 in [(0, r0), (r0, r1)] + ([(r1, V)] if r1 < V else []):
                 if v0 == r0:
-                    turn("h2%d" % r, False)
+                    hop("h2%d" % r, "h1", "Y", v0, v0 + cfg["cut"], ALU.is_ge)
+                    hop("h2%d" % r, "h1", "Y", v0 + cfg["cut"], v1, ALU.is_ge)
+                    ops[-1]["rd"].append(reg("L", 0, r0))
+                    turn("h2%d" % r, r)
                     continue
-                o = reg("B%d" % (6 + j // 2), 0, v1 - v0)
+                hop("h2%d" % r, "h1", "Y", v0, v1, ALU.is_ge)
+                o = reg("B7", 0, v1 - v0)
                 mm(o, full("I16"), reg("S16", v0, v1), True, False)
                 for rr in range(1, r + 1):
                     mm(o, full("I16"), reg("h2%d" % rr, v0, v1), False, rr == r)
                 tscal(reg("L", v0, v1), o, TW / 2, None, ALU.add)
 
-        def keep(h):
-            if not last:
-                act(box("ST", 8 * h, 8 * h + 8, 0, nb), box("B%d" % h, 0, 8, 0, nb), AF.Identity)
-
         def natural(j):
-            v0, v1, eng = nat[j]
+            v0, v1, eng, w = nat[j]
             for a in range(v0, v1, 64):
                 pr = reg("P", 16 * a, 16 * a + 1024)
-                gather(eng, pr, win, reg("L", a, a + 64), far)
+                gather(eng[(a - v0) // 64], pr, win, reg("L", a, a + 64), far)
                 mo = reg("M", mcol(a), mcol(a) + 1024)
                 add("V", lambda g, T, pr=pr, mo=mo: g.vector.tensor_tensor_scan(
                     ap(T, mo), T.rst[:], ap(T, pr), 0.0, ALU.mult, ALU.max), [pr, reg("rst", 0, 1024)], [mo], "v", 512)
 
         def unit(u):
             eng, blk, v0, v1, w = units[u]
-            n = v1 - v0
-            per = cfg["links"][eng]
+            n, eng = v1 - v0, eng[r]
+            per = min(cfg["links"][eng], cfg["call"][eng] // n)
             if eng == "V":
                 src = reg(tab, own0 + v0, own0 + v1)
                 for j in range(per):
-                    cw = reg("cw", per * v0 + j * n, per * v0 + (j + 1) * n)
+                    cw = reg("cw", 4 * v0 + j * n, 4 * v0 + (j + 1) * n)
                     add("G", lambda g, T, cw=cw: g.affine_select(ap(T, cw), ap(T, src), [[0, n]], ALU.is_ge, 0.0, 0, 0),
                         [src] + far, [cw], "g", n)
             for kk in range(0, 8, per):
@@ -359,7 +363,7 @@ def build(rank, par, cfg):
                 if eng == "A":
                     gather("A", o, win, ulist(u, kk, kk + per), far)
                 else:
-                    fused(o, win, ulist(u, kk, kk + per), reg("cw", per * v0, per * v1), ALU.subtract, far)
+                    fused(o, win, ulist(u, kk, kk + per), reg("cw", 4 * v0, 4 * v0 + per * n), ALU.subtract, far)
 
         def fold(j):
             moves = []
@@ -373,32 +377,40 @@ def build(rank, par, cfg):
 
         def compare(kind, j):
             if kind == "n":
-                v0, v1 = nat[j][:2]
-                n, w, base = v1 - v0, 0, 16 * v0
-                src = [reg("P", base + k, 16 * v1, 16) for k in range(16)]
-            else:
-                eng, blk, v0, v1, w = units[j]
-                n, base = v1 - v0, ubase[j]
-                if eng == "V":
-                    for h in range(2):
-                        a, b = base + 4 * n * h, base + 4 * n * (h + 1)
-                        tscal(reg("CM", a, b), reg("P", a, b), 0.0, None, ALU.is_gt, half=True)
-                    return
-                src = [reg("P", base + k * n, base + (k + 1) * n) for k in range(8)]
+                v0, v1, eng, m = nat[j]
+                cb = "B%d" % (2 + nc[0] % 2)
+                nc[0] += 1
+                for i in range(4):
+                    mm(reg(cb, i, 512, 4), eye, reg(tab, own0 + v0, own0 + v1), True, True, far)
+                for a in range(0, 128, m):
+                    for i in range(4):
+                        at = 16 * v0 + 512 * i + 4 * a
+                        tt(reg("CM", at, at + 4 * m), reg("P", 16 * (v0 + a) + i, 16 * (v0 + a + m), 4),
+                           reg(cb, 4 * a, 4 * (a + m)), ALU.is_gt)
+                return
+            eng, blk, v0, v1, w = units[j]
+            n, base = v1 - v0, ubase[j]
+            if eng[r] == "V":
+                for k in range(0, 8 - w, 4):
+                    a, b = base + k * n, base + min(k + 4, 8 - w) * n
+                    tscal(reg("CM", a, b), reg("P", a, b), 0.0, None, ALU.is_gt, half=True)
+                for k in range(8 - w, 8, 2):
+                    a, b = base + k * n, base + min(k + 2, 8) * n
+                    act(reg("CM", a, b), reg("P", a, b), AF.Sign, bias=-0.5, boost=5)
+                return
             cown = reg(tab, own0 + v0, own0 + v1)
-            nv = len(src) - w
-            per = 1 if kind == "n" else min(8, 512 // n)
+            nv = 8 - w
+            per = min(8, 512 // n)
             if nv:
                 cb = "B%d" % (2 + nc[0] % 2)
                 nc[0] += 1
                 for i in range(min(per, nv)):
                     mm(reg(cb, i * n, (i + 1) * n), eye, cown, True, True, far)
             for k in range(0, nv, per):
-                m = min(per, nv - k)
-                tt(reg("CM", base + k * n, base + (k + m) * n),
-                   src[k] if kind == "n" else reg("P", base + k * n, base + (k + m) * n), reg(cb, 0, m * n), ALU.is_gt)
-            for k0 in range(nv, len(src), per):
-                k1 = min(len(src), k0 + per)
+                a, b = base + k * n, base + min(k + per, nv) * n
+                tt(reg("CM", a, b), reg("P", a, b), reg(cb, 0, b - a), ALU.is_gt)
+            for k0 in range(nv, 8, per):
+                k1 = min(8, k0 + per)
                 db = cfg["dbanks"][nd[0] % len(cfg["dbanks"])]
                 nd[0] += 1
                 mm(reg(db, 0, (k1 - k0) * n), eye, reg("P", base + k0 * n, base + k1 * n), True, False, boost=5)
@@ -411,20 +423,22 @@ def build(rank, par, cfg):
             n = c1 - c0
             folded = r0 <= c0 < r1
             if folded:
-                nv = sum(1 for e, b, v0, v1, w in units if e == "V" and v0 <= c0 < v1)
-                three = [([eye, full("I2"), full("I3")][nv], reg(tab, par0 + c0, par0 + c1))]
-                three += [(eye, reg("FM%d%d" % (r, b), c0, c1)) for b in range(2)]
+                three = [(eye, reg("FM%d%d" % (r, b), c0, c1), 0) for b in range(2)]
+                cuts = sorted(set([c0, c1] + [x[2] for x in units if c0 < x[2] < c1]))
+                for a, b in zip(cuts, cuts[1:]):
+                    nv = sum(1 for e, blk, v0, v1, w in units if e[r] == "V" and v0 <= a < v1)
+                    three.append(([eye, full("I2"), full("I3")][nv], reg(tab, par0 + a, par0 + b), a - c0))
             else:
-                three = [(eye, reg(tab, own0 + c0, own0 + c1))]
-                three += [(eye, reg("M", mcol(c0) + 7 + 8 * b, mcol(c0) + 16 * n, 16)) for b in range(2)]
+                three = [(eye, reg(tab, own0 + c0, own0 + c1), 0)]
+                three += [(eye, reg("M", mcol(c0) + 7 + 8 * b, mcol(c0) + 16 * n, 16), 0) for b in range(2)]
             nxt = ("ypt" if folded else "ycb") if last else "tab%d" % (r + 1)
             d0 = c0 if last else (par0 if folded else own0) + c0
-            x, x2 = [reg(b, 0, n) for b in cfg["xbanks"]]
-            for i, (w, xx) in enumerate(three):
-                mm(x, w, xx, i == 0, i == 2, far)
+            x, x2 = [reg("B" + b, 0, n) for b in cfg["xbanks"][j]]
+            for i, (w, xx, a) in enumerate(three):
+                mm(reg(x[0], a, a + cnt(xx)), w, xx, i == 0, i == len(three) - 1, far)
             act(reg("qr", c0, c1), x, AF.Identity, bias=QOFF - 0.5 + 2.0 ** -9, scale=2.0 ** -8)
-            for i, (w, xx) in enumerate(three):
-                mm(x2, w, xx, i == 0, False, far)
+            for i, (w, xx, a) in enumerate(three):
+                mm(reg(x2[0], a, a + cnt(xx)), w, xx, i == 0, False, far)
             mm(x2, full("nI256"), reg("qr", c0, c1), False, True)
             act(reg(nxt, d0, d0 + n), x2, AF.Identity, bias=QOFF * 256)
             if not last:
@@ -443,48 +457,56 @@ def build(rank, par, cfg):
             fb = cfg["fbanks"][nf[0] % len(cfg["fbanks"])]
             nf[0] += 1
             F, Cc = reg(fb, 0, n), reg(fb, 256, 256 + n)
-            st = signset(c0)
             ks = []
-            for k in range(16):
-                if r0 <= c0 < r1:
-                    u = [i for i, x in enumerate(units) if x[1] == k // 8 and x[2] <= c0 < x[3]][0]
-                    a = ubase[u] + (k % 8) * (units[u][3] - units[u][2]) + c0 - units[u][2]
-                else:
-                    a = 16 * c0 + k * n
-                half = any(k0 <= k < k1 for k0, k1 in st)
-                ks.append((k, a, reg("hv", 0, 8) if half else reg("ones", 0, 8)))
+            for j in range(0, n, 128):
+                for k in range(16):
+                    if r0 <= c0 < r1:
+                        u = [i for i, x in enumerate(units) if x[1] == k // 8 and x[2] <= c0 + j < x[3]][0]
+                        a = ubase[u] + (k % 8) * (units[u][3] - units[u][2]) + c0 + j - units[u][2]
+                        cm = reg("CM", a, a + 128)
+                    else:
+                        a = 16 * c0 + 512 * (k % 4)
+                        cm = reg("CM", a + k // 4, a + 512, 4)
+                    half = any(k0 <= k < k1 for k0, k1 in signset(c0 + j))
+                    ks.append((j + k, cm, reg("hv", 0, 8) if half else reg("ones", 0, 8)))
             ks.sort(key=lambda t: max(i for i, o in enumerate(ops) if o["wr"] and o["wr"][0][0] == "CM"
-                                      and o["wr"][0][1] <= t[1] < o["wr"][0][2]))
+                                      and o["wr"][0][1] < t[1][2] <= o["wr"][0][2]))
             low = cfg["boost"]["F"]
             for j in range(0, n, 128):
                 mm(reg(fb, j, j + 128), reg("nth", c0 + j, c0 + j + 128), eye, j == 0, False, boost=low)
             for i, (k, a, x) in enumerate(ks):
-                for j in range(0, n, 128):
-                    mm(reg(fb, j + k, j + 128, 16), reg("CM", a + j, a + j + 128), x, False,
-                       i == 15 and j == n - 128, boost=low)
-            sg, run = reg("sg", c0, c1), reg("run", c0, c1)
-            act(sg, F, AF.Sign, bias=0.5)
-            add("V", lambda g, T: g.vector.tensor_tensor_scan(ap(T, run), T.r16[:, 0:n], ap(T, sg), 1.0, ALU.max, ALU.min),
-                [sg, reg("r16", 0, 256)], [run], "v", n * 0.5)
+                mm(reg(fb, k, k // 128 * 128 + 128, 16), a, x, False, i == len(ks) - 1, boost=low)
+            run = reg("run", c0, c1)
+            x = F
+            if cfg["sign"] == "A":
+                x = reg("sg", c0, c1)
+                act(x, F, AF.Copy)
+            add("V", lambda g, T: g.vector.tensor_tensor_scan(ap(T, run), T.r16[:, 0:n], ap(T, x), 0.0, ALU.mult, ALU.min),
+                [x, reg("r16", 0, 256)], [run], "v", n if x == F else n * 0.5)
             for j in range(0, n, 128):
                 mm(reg(fb, j, j + 128), reg("run", c0 + j, c0 + j + 128), eye, True, True)
-            if not last:
-                mm(Cc, full("nI"), reg("cpb", c0, c1), True, False)
-                for j in range(0, n, 128):
-                    mm(reg(fb, 256 + j, 256 + j + 128), reg("run", c0 + j, c0 + j + 128), eye, False, j == n - 128)
-            act(reg("any%d" % r, c0, c1), F, AF.Identity, bias=0.5, scale=-0.5)
+            act(reg("any%d" % r, c0, c1), F, AF.Sign, scale=-1.0)
             if last:
                 for j in range(RO):
                     mm(Cc, full("Dm"), reg("any%d" % j, c0, c1), j == 0, j == RO - 1)
                 tt(reg("ygb", c0, c1), Cc, reg("gpi", c0, c1), ALU.add)
                 store("yg", "ygb", c0, c1, 4)
             else:
-                act(reg("Y", c0, c1), Cc, AF.Abs, bias=1.0)
+                mm(Cc, full("nI"), reg("cpb", c0, c1), True, False)
+                mm(Cc, full("n2I"), reg("any%d" % r, c0, c1), False, True)
+                act(reg("Y", c0, c1), Cc, AF.Abs, bias=2.0)
 
         steps = {"gn": natural, "gu": unit, "cn": lambda j: compare("n", j), "cu": lambda j: compare("u", j),
-                 "f": lambda j: counts(*cfg["cnt"][j]), "r": registers, "o": fold, "s": keep}
-        for word in cfg["seq"].split():
+                 "f": lambda j: counts(*cfg["cnt"][j]), "r": registers, "o": fold}
+        for word in cfg["seq"][r].split():
+            at = len(ops)
             steps[word[:-1]](int(word[-1]))
+            for i in range(at, len(ops)):
+                o = ops[i]
+                if word in cfg["late"] and o["wr"] and o["wr"][0][0][:3] in ("any", "qr"):
+                    o["rd"].append(reg("after%d" % r, 0, len(ops)))
+                if o["kind"] == "ag" and word[:2] == "gu":
+                    o["wr"].append(reg("after%d" % r, i, i + 1))
     return ops
 
 
@@ -532,7 +554,7 @@ def cost(o, e):
     move = o["rows"] / 16 * e["drow"] * (e["frow"] if k == "f" else 1) + 8 * n / e["dbw"] * (e["fb"] if k == "f" else 1)
     if k == "d":
         return 60, move, e["dfix"]
-    return e["riss"] + (e["rfirst"] if o["first"] else 0), move, e["rfix"]
+    return e["riss"] + (e["rfirst"] if o["first"] else 0), move, e["rfix"] + (e["fx"] if k == "f" else 0)
 
 
 def schedule(ops, e, delta):

@@ -8,37 +8,58 @@ TW = NR * V
 BIG = 65536.0
 QOFF = 129.0
 
+QUARTERS = [(0, 256), (256, 512), (512, 768), (768, 1024)]
 CFG = {
-    "lm": (128, (896, 896, 896)),
-    "nat": [(0, 128, "AA", 128), (896, 1024, "AA", 128)],
-    "sign": "V",
-    "units": [("AAA", 0, 128, 384, 8), ("VVV", 1, 128, 384, 2), ("AAA", 0, 384, 640, 4),
-              ("VVV", 1, 384, 640, 8), ("AAA", 0, 640, 896, 0), ("VVV", 1, 640, 896, 0)],
-    "cnt": [(0, 128), (128, 384), (384, 640), (640, 896), (896, 1024)],
-    "reg": [(0, 128), (128, 384), (384, 640), (640, 896), (896, 1024)],
-    "links": {"A": 4, "V": 2},
-    "call": {"A": 1024, "V": 512},
-    "dbanks": ["B0", "B1"],
-    "fbanks": ["B4", "B5", "B6"],
-    "xbanks": ["71", "77", "77", "10", "77"],
+    "plan": [[(0, 256, "A8", "V0"), (256, 512, "A8", "V0"), (512, 768, "A4", "V0"), (768, 1024, "A0", "V0")]] * 3,
+    "dec": [[(0, 1024, "01")]] * 3,
+    "hop1": [768],
+    "hop2": [512],
+    "cnt": [QUARTERS[:3] + [(768, 896), (896, 1024)]] * 3,
+    "reg": [QUARTERS] * 3,
+    "links": {"A": 4, "V": 2, "D": 4},
+    "call": {"A": 1024, "V": 512, "D": 1024},
+    "banks": {"t": "01", "f": "765", "g": "43210"},
+    "passes": 4,
+    "topen": ("h1", 0, 16),
+    "fopen": 0,
     "thwait": ("far0", 0, 999),
-    "nthwait": ("L2", 0, 896),
-    "cut": 192,
-    "turn": [1, 0],
-    "seq": ["gu0 cu0 gu2 gn0 gu1 gu3 r0 gu4 o1 cn0 o0 o4 o3 gu5 o5 r1 f0 o2 cu2 r2 cu1 f1 gn1 cu5 r3 cu3 cu4 f2 cn1 f3 "
-            "r4 f4"] * 3,
-    "folds": [[0], [1], [2], [3], [4], [5]],
-    "hop1": [(0, 768), (768, 1024)],
+    "nthwait": ("L256", 0, 1024),
+    "seq": ["g00 g01 o00 o01 g10 g11 o10 o11 r0 g20 g21 o20 o21 r1 g30 g31 o30 o31 c00 c01 f0 r2 c10 c11 f1 r3 c20 c21 f2 "
+            "c30 c31 f3 f4"] * 3,
     "c0a": 128,
     "loads": ["c0a", "c0b", "cp0", "gp0", "cp1", "rfs", "gp1", "gp2"],
     "gaps": [(0, 512), (512, 768), (768, 1024)],
-    "late": ["f0"],
+    "hw": "V",
+    "late": [],
     "delta": 0.0,
     "boost": {"VP": 5, "VM": 5, "VCM": 5, "VST": 2, "VS16": 8, "Vnth": 6, "AP": 5, "F": 5},
 }
+CFG.update({
+    "plan": [[(0, 128, 'n', 'AA', 4), (128, 384, 'A8', 'V0'), (384, 640, 'A8', 'V0'), (640, 896, 'V4', 'V0'), (896, 1024, 'n', 'AA', 0)]] * 3,
+    "sign": [[128, 640], [896], [640, 896]],
+    "seq": ['g21 g10 g11 g30 c10 o10 g00 c00 g20 o30 g31 c20 o31 g40 o21 r0 o11 r4 o20 r3 c11 c31 f0 r1 c30 c21 f1 c40 r2 f2 f4 f3',
+            'g21 g10 g11 g30 c10 o10 g00 g20 c00 o30 g31 c20 o20 o31 g40 c31 r0 o21 o11 c11 r4 f1 r3 r1 c30 c21 c40 f3 f2 f0 f4 r2',
+            'g21 g11 g30 g10 c10 g00 o30 g20 c00 g31 c20 o20 o31 o10 r0 o21 g40 o11 c11 r3 r1 c31 r4 f0 c30 c21 c40 f1 f3 f2 f4 r2'],
+    "dec": [[(0, 128, 'n'), (128, 896, '01'), (896, 1024, 'n')]] * 3,
+    "boost": {'VP': 5, 'VM': 5, 'VCM': 4, 'VS16': 5, 'Vnth': 9, 'AP': 5, 'F': 4, 'Vrun': 6, 'ACM': 5, 'AY': 6, 'Aqr': 9, 'Gcw': 5},
+    "banks": {'t': '01', 'f': '765', 'g': '4321076'},
+    "fopen": 4, "hop1": [384, 512], "hop2": [], "hw": "A", "passes": 1,
+    "cnt": [[(0, 128), (128, 384), (384, 640), (640, 896), (896, 1024)]] * 3,
+    "reg": [[(0, 128), (128, 384), (384, 640), (640, 896), (896, 1024)]] * 3,
+    "foldeng": 16, "regv": [[], [], []], "yv": [[], [], []], "signcall": 512, "pin": True, "const": "A", "relay": [[], [], []],
+})
 EST = {"cyc": 0.9, "g": 1.56, "ov": 30.0, "oa": 30.0, "pe": 0.5, "op": 5.0, "sem": 90.0,
        "dfix": 1800.0, "drow": 14.0, "dbw": 24.0, "rfix": 2000.0, "riss": 600.0, "rfirst": 2000.0,
-       "frow": 6.0, "fb": 0.9, "fx": 500.0}
+       "frow": 6.0, "fb": 0.9, "fx": 500.0, "xiss": 1000.0, "xb": 2.0, "sx": 1.0, "ra": 1.0}
+EST.update(dict(cyc=.9, pe=.62, op=4, ov=13, oa=38, g=1.56, frow=6, fb=1.0, riss=420, rfix=1450, sem=55, dbw=27, drow=10,
+                sx=1.8, dfix=1300, rfirst=1800, fx=250))
+NOW = {'plan': [(0, 128, 'n', 'AA', 3), (128, 384, 'A8', 'V0'), (384, 640, 'A4', 'V0'), (640, 896, 'A0', 'V2'), (896, 1024, 'n', 'AA', 0)], 'seq': 'g00 g10 g21 g11 c10 o10 o11 r0 g20 c00 r1 o20 o21 g30 c20 g31 g40 r4 o31 c30 c31 f0 o30 r3 c11 c21 c40 f2 f4 f3 r2 f1', 'dec': [(0, 128, 'n'), (128, 896, '01'), (896, 1024, 'n')], 'boost': {'VP': 5, 'VM': 5, 'VCM': 5, 'VS16': 8, 'Vnth': 6, 'AP': 5, 'F': 9, 'ACM': 5, 'Gcw': 6, 'VY': 4, 'D': 9, 'Vrun': 6}, 'delta': 0.0, 'banks': {'t': '01', 'f': '765', 'g': '4321076'}, 'fopen': 0, 'hop1': [256], 'hop2': [320], 'sign': [[640], [640], [640]], 'regv': [[0, 384, 640, 896], [0, 384, 640, 896], [0, 384, 640, 896]], 'yv': [[], [], []], 'links': {'A': 4, 'V': 2, 'D': 4}, 'call': {'A': 1024, 'V': 512, 'D': 1024}, 'hw': 'V'}
+EST.update(dict(cyc=.95, pe=.62, op=2, ov=12, oa=42, g=1.4, frow=6.3, fb=1.05, riss=400, rfix=1100, sem=140, dbw=26, drow=10, sx=1.8, dfix=1400, rfirst=2000, fx=600))
+NOW = {'plan': [[(0, 128, 'n', 'AA', 3), (128, 384, 'A8', 'V4'), (384, 640, 'A4', 'V0'), (640, 896, 'A0', 'V2'), (896, 1024, 'n', 'AA', 0)], [(0, 128, 'n', 'AA', 3), (128, 384, 'A8', 'V0'), (384, 640, 'A4', 'V0'), (640, 896, 'A0', 'V4'), (896, 1024, 'n', 'AA', 0)], [(0, 128, 'n', 'AA', 3), (128, 384, 'A8', 'V0'), (384, 640, 'A4', 'V0'), (640, 896, 'A0', 'V4'), (896, 1024, 'n', 'AA', 0)]], 'seq': ['g21 g10 c10 g11 g20 g00 r0 o11 o20 o10 c00 r1 g30 f0 o30 c20 g40 o21 r4 g31 c11 c40 c30 f1 r2 f4 o31 c31 c21 r3 f3 f2', 'g00 g10 g21 g11 o10 g20 r0 c00 o21 c10 o11 g30 c21 g40 o30 f0 g31 o20 r1 r4 c20 o31 c31 c11 r3 c40 r2 c30 f3 f2 f1 f4', 'g10 g21 o10 g00 c10 g20 g11 c00 o11 o20 r1 g30 c20 o30 f0 g40 o21 c30 g31 r4 c40 c11 r0 o31 c21 c31 r3 f3 f4 f2 f1 r2'], 'dec': [[(0, 128, 'n'), (128, 896, '10'), (896, 1024, 'n')], [(0, 128, 'n'), (128, 896, '01'), (896, 1024, 'n')], [(0, 128, 'n'), (128, 896, '01'), (896, 1024, 'n')]], 'boost': {'VP': 5, 'VM': 5, 'VCM': 5, 'VS16': 9, 'Vnth': 9, 'AP': 5, 'F': 9, 'ACM': 5, 'Gcw': 9, 'VY': 2, 'D': 9, 'Vrun': 6, 'Aqr': 9, 'AY': 6}, 'delta': 0.0, 'banks': {'t': '01', 'f': '765', 'g': '4321076'}, 'fopen': 4, 'hop1': [], 'hop2': [256], 'sign': [[128, 640], [640], [640]], 'regv': [[0, 384, 640], [384, 640], [0, 384, 640, 896]], 'yv': [[128, 384], [128, 384], []], 'hw': 'A', 'relay': [[0, 128], [0, 128], []]}
+for _k in ("plan", "dec", "seq", "cnt", "reg"):
+    if _k in NOW and not isinstance(NOW[_k][0], list) and not (_k == "seq" and isinstance(NOW[_k], list)):
+        NOW[_k] = [NOW[_k]] * 3
+CFG.update(NOW)
 
 SCRATCH = {}
 
@@ -53,16 +74,16 @@ _decl("rfi", "sbuf", [128, 64], "int32")
 _decl("pcol pand", "sbuf", [128, 8], "int32")
 _decl("rf16", "sbuf", [128, 64], "uint16")
 _decl("L", "sbuf", [128, V], "uint16")
-_decl("tab0 tab1 tab2", "sbuf", [128, TW + 256], "bfloat16")
+_decl("tab0 tab1 tab2", "sbuf", [128, TW + 16], "bfloat16")
 _decl("P CM", "sbuf", [128, 16 * V], "bfloat16")
-_decl("M", "sbuf", [128, 8 * V], "bfloat16")
+_decl("M", "sbuf", [128, 4 * V], "bfloat16")
 _decl("rst", "sbuf", [128, 1024], "bfloat16")
 _decl("nog S16 h21 h22", "sbuf", [128, V], "float16")
-_decl("ycb ypt cpb nth sg run any0 any1 any2 Y h1 qr", "sbuf", [128, V], "bfloat16")
+_decl("ycb ypt cpb own4 nth any0 any1 any2 Y h1 qr", "sbuf", [128, V], "bfloat16")
 _decl("FM00 FM01 FM10 FM11 FM20 FM21", "sbuf", [128, V], "bfloat16")
 _decl("ygb Gw Hw Y2 S1", "sbuf", [128, V], "float32")
 _decl("lo", "sbuf", [128, 512], "bfloat16")
-_decl("I nI I2 I3 I256 nI256 n2I nBI tri0 tri sh Dm Z", "sbuf", [128, 128], "bfloat16")
+_decl("I nI I2 I3 I256 nI256 n2I nBI tri0 tri sh Dm K258 Khalf", "sbuf", [128, 128], "bfloat16")
 _decl("J", "sbuf", [128, 160], "bfloat16")
 _decl("ones", "sbuf", [128, 256], "bfloat16")
 _decl("J0 J1", "sbuf", [128, 160], "float16")
@@ -70,17 +91,23 @@ _decl("ntri16 I16", "sbuf", [128, 128], "float16")
 _decl("r16", "sbuf", [128, 256], "bfloat16")
 _decl("hv", "sbuf", [128, 8], "bfloat16")
 _decl("kcol", "sbuf", [128, 8], "float32")
-_decl("wb", "sbuf", [128, 64, 16], "bfloat16")
+_decl("wb", "sbuf", [128, 128, 16], "bfloat16")
 _decl("B0 B1", "psum", [128, 32, 16], "float32")
 _decl("B2 B3 B4 B5 B6 B7", "psum", [128, 512], "float32")
 _decl("hT0 hT1 hT2", "sbuf", [128, 32, 32], "float16")
-_decl("L2", "sbuf", [128, 4, 256], "uint16")
+for _n in (128, 160, 192, 224, 256, 288, 320, 384, 448, 512):
+    _decl("L%d" % _n, "sbuf", [128, V // _n + 1, _n], "uint16")
+_decl("run sg", "sbuf", [128, 2 * V], "bfloat16")
 _decl("cw", "sbuf", [128, 4 * V], "bfloat16")
 
 SEMAPHORES = (["sV", "sA", "sP", "sG", "c0a", "c0b", "cp0", "cp1", "gp0", "gp1", "gp2", "rfs", "ths", "outs",
-               "arr0", "arr1", "arr2", "loc", "fl0", "fl1", "fl2"]
-              + ["f%d_%d" % (r, u) for r in range(RO) for u in range(len(CFG["folds"]))]
-              + ["yb%d" % j for j in range(len(CFG["reg"]))])
+               "arr0", "arr1", "arr2", "head1", "head2", "loc", "fl0", "fl1", "fl2"]
+              + ["f%d_%d%d" % (r, j, b) for r in range(RO) for j, c in enumerate(CFG["plan"][r]) for b in range(2)
+                 if c[2] != "n"]
+              + ["%s%d_%d%d" % (x, r, j, b) for r in range(RO) for j, c in enumerate(CFG["plan"][r]) for b in range(2)
+                 for x in "wx" if c[2 + b][0] == "D"]
+              + ["via%d_%d" % (r, j) for r in range(RO - 1) for j, c in enumerate(CFG["reg"][r]) if c[0] in CFG["relay"][r]]
+              + ["yb%d" % j for j in range(len(CFG["reg"][-1]))])
 ENGSEM = {"V": "sV", "A": "sA", "P": "sP", "G": "sG"}
 
 
@@ -97,14 +124,21 @@ def build(rank, par, cfg):
         return (name, lo, hi, step)
 
     def box(name, ra, rb, ca, cb, step=1):
-        w = SCRATCH[name][1][2]
+        w = 16 if name[0] == "#" else SCRATCH[name][1][2]
         return (name, ra * w + ca, (rb - 1) * w + cb, (ra, rb, ca, cb, step))
+
+    nbank = [0]
+
+    def bank(kind="g"):
+        nbank[0] += 1
+        return "#%s%d" % (kind, nbank[0])
 
     def ap(T, r):
         name, lo, hi, step = r
+        name = BANK.get(name, name)
         if isinstance(step, tuple):
             if step[1] - step[0] == 1:
-                return T[name][:, step[0], step[2]:step[3]]
+                return T[name][:, step[0], step[2]:step[3]:step[4]] if step[4] != 1 else T[name][:, step[0], step[2]:step[3]]
             return T[name][:, step[0]:step[1], step[2]:step[3]:step[4]]
         if len(SCRATCH[name][1]) == 3:
             w = SCRATCH[name][1][2]
@@ -134,6 +168,10 @@ def build(rank, par, cfg):
     def vcopy(o, i):
         add("V", lambda g, T: g.vector.tensor_copy(ap(T, o), ap(T, i)), [i], [o], "v", cnt(o))
 
+    def gcopy(o, i, extra):
+        add("G", lambda g, T: g.affine_select(ap(T, o), ap(T, i), [[0, cnt(o)]], ALU.is_ge, 0.0, 0, 0), [i] + extra, [o],
+            "g", cnt(o))
+
     def tt(o, a, b, op, w=1):
         add("V", lambda g, T: g.vector.tensor_tensor(ap(T, o), ap(T, a), ap(T, b), op), [a, b], [o], "v", cnt(o) * w)
 
@@ -141,12 +179,14 @@ def build(rank, par, cfg):
         add("V", lambda g, T: g.vector.tensor_tensor(ap(T, o), ap(T, w).indirect(ap(T, off)), ap(T, y), op),
             [w, off, y] + list(extra), [o], "vg", cnt(o))
 
-    def hop(o, win, y, v0, v1, op):
-        fused(reg(o, v0, v1), reg(win, 0, V), reg("rf16", v0 // 16, v1 // 16), reg(y, v0, v1), op)
+    def hop(o, win, y, v0, v1, op, stops=()):
+        at = [v0] + [v for v in stops if v0 < v < v1] + [v1]
+        for a, b in zip(at, at[1:]):
+            fused(reg(o, a, b), reg(win, 0, V), reg("rf16", a // 16, b // 16), reg(y, a, b), op)
 
-    def gather(eng, o, w, off, extra):
+    def gather(eng, o, w, off, extra, scale=1.0):
         if eng == "A":
-            add("A", lambda g, T: g.scalar.activation(ap(T, o), ap(T, w).indirect(ap(T, off)), AF.Copy),
+            add("A", lambda g, T: g.scalar.activation(ap(T, o), ap(T, w).indirect(ap(T, off)), AF.Copy, scale=scale),
                 [w, off] + extra, [o], "ag", cnt(o))
         else:
             add("V", lambda g, T: g.vector.tensor_copy(ap(T, o), ap(T, w).indirect(ap(T, off))),
@@ -177,34 +217,41 @@ def build(rank, par, cfg):
 
     nsend = [0]
 
-    def send(r, s0, s1, behind=False):
-        tab = "tab%d" % r
+    def send(r, s0, s1, relay=None):
+        x = reg("tab%d" % r, s0, s1)
         nsend[0] += 1
-        dsts = [reg(tab, s0, s1)] + ([reg(tab, TW, TW + s1 - s0)] if behind else [])
-        add("G", ([([reg(tab, s0, s1)], dsts)], "all", "loc"), [reg(tab, s0, s1)],
-            [reg("far%d" % r, nsend[0], nsend[0] + 1)], "r", (s1 - s0) * 2 * (NR - 1), sig=("arr%d" % r, None),
-            rows=128 * (NR - 1))
+        head = r > 0 and s0 % V == 0
+        done = reg("far%d" % r, 0, 1) if head else reg("far%d" % r, nsend[0], nsend[0] + 1)
+        sig, size = (("head%d" if head else "arr%d") % r, None), (s1 - s0) * 2
+        if relay:
+            add("G", ([([x], [x])], "aide", "loc", 0), [x], [reg(relay, 0, 1)], "r", size, sig=(relay, None), rows=128)
+            add("H", ([([x], [x])], "all", "loc", 0), [reg(relay, 0, 1)], [done], "h", size * (NR - 1), sig=sig)
+            ops[-1]["first"] = not any(p["kind"] == "h" for p in ops[:-1])
+            return
+        add("G", ([([x], [x])], "all", "loc", 0), [x], [done], "r", size * (NR - 1), sig=sig, rows=128 * (NR - 1))
 
     own0, par0 = V * rank, V * par
-    r0, ends = cfg["lm"]
-    nat, units = cfg["nat"], cfg["units"]
+    plan = cfg["plan"]
     ca = cfg["c0a"]
-    ubase, at = [], 16 * r0
-    for u in units:
-        ubase.append(at)
-        at += 8 * (u[3] - u[2])
 
-    def ulist(u, ka, kb):
-        c, at = (units[u][2] - r0) // 256, 128 * units[u][1]
-        return box("L2", c, c + 1, at + 16 * ka, at + 16 * kb)
+    def chunk(r, v):
+        return [c for c in plan[r] if c[0] <= v < c[1]][0]
 
-    def mcol(v):
-        return 16 * (v if v < r0 else v - ends[-1] + r0)
+    def signset(r, v):
+        c = chunk(r, v)
+        if c[2] == "n":
+            return tuple((i, 16, 4) for i in range(4 - c[4], 4))
+        return tuple((8 * b + 8 - int(c[2 + b][1]), 8 * b + 8, 1) for b in range(2) if int(c[2 + b][1]))
 
-    def signset(c0):
-        return tuple((8 * b + 8 - w, 8 * b + 8) for e, b, v0, v1, w in units if w and v0 <= c0 < v1)
+    def blocks(c0, c1):
+        return [c0] + ([c1 - 128] if c1 - c0 > 128 else [])
 
-    sets = sorted(set(signset(c0) for c0 in range(0, V, 128)) - {()})
+    sets = sorted(set(signset(r, v) for r in range(RO) for v in range(0, V, 32)) - {()})
+    loose = {v for v in range(0, V, 32) if len(set(signset(r, v) for r in range(RO))) > 1}
+    for _ in range(V // 32):
+        for v in (v for r in range(RO) for c in cfg["cnt"][r] for v in blocks(*c)):
+            if loose & set(range(v, v + 128, 32)):
+                loose |= set(range(v, v + 128, 32))
 
     loads = {"c0a": ("tab0", "c0", 0, ca, own0, 2), "c0b": ("tab0", "c0", ca, V, own0 + ca, 2),
              "cp0": ("cpi", "cp", 0, 512, 0, 4), "cp1": ("cpi", "cp", 512, V, 512, 4),
@@ -213,6 +260,8 @@ def build(rank, par, cfg):
         loads["gp%d" % j] = ("gpi", "gp", a, b, a, 4)
     for s in cfg["loads"]:
         load("S", *loads[s][:5], s, loads[s][5])
+        if cfg["pin"]:
+            ops[-1]["pin"] = len(ops)
     memset(reg("ones", 0, 256), 1.0)
     add("G", lambda g, T: g.affine_select(T.J[:], T.ones[:, 0:160], [[-1, 160]], ALU.is_equal, 0.0, 16, 1),
         [reg("ones", 0, 160)], [reg("J", 0, 160)], "g", 160)
@@ -234,51 +283,95 @@ def build(rank, par, cfg):
     load("S", "thi", "th", 0, V, 0, "ths", 4, extra=[reg(*cfg["thwait"])])
     eye = reg("J", 16, 144)
     tscal(full("ntri16"), full("tri"), -1.0, None, ALU.mult, half=True)
-    for name, c in (("nBI", -4 * BIG), ("I16", 1.0), ("nI", -1.0), ("I256", 256.0), ("nI256", -256.0), ("n2I", -2.0),
-                    ("I2", 2.0), ("I3", 3.0), ("Z", 0.0)):
-        tscal(full(name), eye, c, None, ALU.mult, half=True)
-    memset(reg("rst", 0, 1024), 1.0)
-    memset(reg("rst", 0, 1024, 8), 0.0)
-    memset(reg("hv", 0, 8), 0.5)
-    memset(reg("r16", 0, 256), 1.0)
-    memset(reg("r16", 0, 256, 16), 0.0)
+    tscal(full("I16"), eye, 1.0, None, ALU.mult, half=True)
+    first_const = len(ops)
+
+    onv = cfg["const"] == "V"
+
+    def fill(o, c):
+        if onv:
+            return memset(o, c)
+        act(o, reg("ones", 0, cnt(o)), AF.Copy, scale=c)
+
+    for name, c in (("nI", -1.0), ("nBI", -4 * BIG), ("I256", 256.0), ("nI256", -256.0), ("n2I", -2.0), ("I2", 2.0),
+                    ("I3", 3.0)):
+        if onv:
+            tscal(full(name), eye, c, None, ALU.mult, half=True)
+        else:
+            act(full(name), eye, AF.Copy, scale=c)
+    for a in range(0, 1024, 1024 if onv else 256):
+        fill(reg("rst", a, a + (1024 if onv else 256)), 1.0)
+    fill(reg("rst", 0, 1024, 8), 0.0)
+    fill(full("K258"), 258.0)
+    fill(reg("hv", 0, 8), 0.5)
+    fill(reg("r16", 0, 256), -1024.0)
+    fill(reg("r16", 0, 256, 16), 0.5)
+    fill(full("Khalf"), 2.0 ** -8)
+    for a in range(0, 128 * len(sets), 256):
+        fill(reg("wb", a, a + 256), 0.0)
+    for si, st in enumerate(sets):
+        for k0, k1, dk in st:
+            fill(box("wb", 8 * si, 8 * si + 8, k0, k1, dk), 0.5)
+    if onv:
+        tt(full("Dm"), eye, full("sh"), ALU.subtract, 2)
+    else:
+        dm = full(bank())
+        mm(dm, eye, eye, True, False, [full("sh")])
+        mm(dm, full("nI"), full("sh"), False, True)
+        act(full("Dm"), dm, AF.Copy)
+    last_const = len(ops)
     tscal(reg("pand", 1, 2), reg("pcol", 0, 1), 16, None, ALU.bitwise_and)
     tscal(reg("kcol", 1, 2), reg("pand", 1, 2), 8.0, None, ALU.is_lt)
     tscal(reg("kcol", 2, 3), reg("pand", 1, 2), 8.0, None, ALU.is_gt)
     for j in range(2):
         tscal(reg("J%d" % j, 0, 160), reg("J", 0, 160), reg("kcol", 1 + j, 2 + j), None, ALU.mult, half=True)
-    for si, st in enumerate(sets):
-        memset(reg("wb", 128 * si, 128 * si + 128), 0.0)
-        for k0, k1 in st:
-            memset(box("wb", 8 * si, 8 * si + 8, k0, k1), 0.5)
-    tt(full("Dm"), eye, full("sh"), ALU.subtract, 2)
     vcopy(reg("rf16", 0, 64), reg("rfi", 0, 64))
 
-    def turn(src, r):
-        nb = (ends[0] - r0) // 32
-        out = reg("hT%d" % r, 0, 32 * nb)
-        add("V", lambda g, T: g.vector.transpose(ap(T, out), T[src][:, r0:ends[0]]), [reg(src, r0, ends[0])], [out],
-            "v", 16 * nb)
-        for h in cfg["turn"]:
-            terms = [(j, d, c) for j in range(r + 1) for d in range(2) for c in range(2)]
-            for j, d, c in terms:
-                mm(box("B%d" % h, 0, nb, 8 * d, 8 * d + 8), reg("J%d" % d, 16 + 16 * (d - c), 144 + 16 * (d - c)),
-                   box("hT%d" % j, 0, nb, 16 * c + 8 * h, 16 * c + 8 * h + 8), (j, d, c) == terms[0],
-                   (j, d, c) == terms[-1])
-            for kk in range(8):
-                at = 128 * h + 16 * kk
-                tscal(box("L2", 0, nb // 8, at, at + 16), box("B%d" % h, 0, nb, kk, 16, 8), TW / 2, None, ALU.add)
+    def flip(src, r, v0, v1):
+        out = reg("hT%d" % r, v0, v1)
+        add("V", lambda g, T: g.vector.transpose(ap(T, out), T[src][:, v0:v1]), [reg(src, v0, v1)], [out], "v",
+            (v1 - v0) / 2)
 
+    def turn(src, r, v0, v1, blocks):
+        flip(src, r, v0, v1)
+        nb, b0 = (v1 - v0) // 32, v0 // 32
+        runs = []
+        for c in plan[r]:
+            if v0 <= c[0] < v1:
+                if runs and runs[-1][2] == c[1] - c[0]:
+                    runs[-1][1] = c[1]
+                else:
+                    runs.append([c[0], c[1], c[1] - c[0]])
+        for h in map(int, blocks):
+            terms = [(j, d, c) for j in range(r + 1) for d in range(2) for c in range(2)]
+            tb = bank("t")
+            for j, d, c in terms:
+                mm(box(tb, 0, nb, 8 * d, 8 * d + 8), reg("J%d" % d, 16 + 16 * (d - c), 144 + 16 * (d - c)),
+                   box("hT%d" % j, b0, b0 + nb, 16 * c + 8 * h, 16 * c + 8 * h + 8), (j, d, c) == terms[0],
+                   (j, d, c) == terms[-1], [reg(*cfg["topen"], 1)] if r and (j, d, c) == terms[0] else [])
+            for a, b, n in runs:
+                for kk in range(8):
+                    at = (8 * h + kk) * n // 16
+                    tscal(box("L%d" % n, a // n, a // n + (b - a) // n, at, at + n // 16),
+                          box(tb, (a - v0) // 32, (b - v0) // 32, kk, 16, 8), TW / 2, None, ALU.add)
+
+    def spare(src, r):
+        for c in plan[r]:
+            if c[2] == "n" and any(chunk(rr, v)[2] != "n" for rr in range(r + 1, RO) for v in range(c[0], c[1], 32)):
+                flip(src, r, c[0], c[1])
+                ops[-1]["boost"] = 1
+
+    less = [bank("f"), bank("f")]
     for h in range(2):
         a = 512 * h
         vcopy(reg("cpb", a, a + 512), reg("cpi", a, a + 512))
-        mm(reg("B%d" % (4 + h), 0, 512), eye, reg("cpb", a, a + 512), True, False)
+        mm(reg(less[h], 0, 512), eye, reg("cpb", a, a + 512), True, False)
         for j in (0, 256):
-            mm(reg("B%d" % (4 + h), j, j + 256), full("nI"), reg("ones", 0, 256), False, j == 256)
+            mm(reg(less[h], j, j + 256), full("nI"), reg("ones", 0, 256), False, j == 256)
     for h, (a, b) in enumerate(cfg["gaps"]):
         n = b - a
-        z1, z2 = reg("B%d" % (6 + h % 2), 0, n), reg("B" + "230"[h], 0, n)
-        tt(reg("nog", a, b), reg("gpi", a, b), reg("B%d" % (4 + a // 512), a % 512, a % 512 + n), ALU.mult)
+        z1, z2 = reg(bank(), 0, n), reg(bank(), 0, n)
+        tt(reg("nog", a, b), reg("gpi", a, b), reg(less[a // 512], a % 512, a % 512 + n), ALU.mult)
         mm(z2, eye, reg("lo", 0, n), True, False)
         mm(z2, full("nBI"), reg("cpb", a, b), False, False)
         mm(z2, full("ntri16"), reg("nog", a, b), False, True)
@@ -287,227 +380,308 @@ def build(rank, par, cfg):
         for j in range(0, n, 256):
             act(reg("Gw", a + j, a + j + 256), reg(z1[0], j, j + 256), AF.Identity, bias=float(own0 + a + j))
         for j in range(0, n, 256):
-            tscal(reg("Hw", a + j, a + j + 256), reg(z2[0], j, j + 256), float(own0 + a + j) + BIG, 0.0, ALU.add, ALU.max)
+            if cfg["hw"] == "V":
+                tscal(reg("Hw", a + j, a + j + 256), reg(z2[0], j, j + 256), float(own0 + a + j) + BIG, 0.0, ALU.add, ALU.max)
+            else:
+                act(reg("Hw", a + j, a + j + 256), reg(z2[0], j, j + 256), AF.Relu, bias=float(own0 + a + j) + BIG)
         for j in range(0, n, 256):
             act(reg("Y2", a + j, a + j + 256), reg(z2[0], j, j + 256), AF.Relu, bias=float(own0 + a + j) + 2 * BIG)
-    hop("S1", "Gw", "Hw", 0, 512, ALU.max)
-    hop("S1", "Gw", "Hw", 512, V, ALU.max)
-    cuts = [0, r0, ends[0], V]
-    for j, (v0, v1) in enumerate(zip(cuts, cuts[1:])):
-        hop("s2i", "S1", "Y2", v0, v1, ALU.max)
-        if j:
-            ops[-1]["rd"].append(reg("s2m", cuts[j - 1], v0))
-        tscal(reg("s2m", v0, v1), reg("s2i", v0, v1), TW - 1, None, ALU.bitwise_and)
-        if r0 <= v0 < ends[0]:
-            tscal(reg("S16", v0, v1), reg("s2m", v0, v1), -TW / 2, None, ALU.add)
-            turn("S16", 0)
+    hop("S1", "Gw", "Hw", 0, V, ALU.max, [512])
+    for v0, v1, how in cfg["dec"][0]:
+        at = [v0] + [v for v in cfg["hop2"] if v0 < v < v1] + [v1]
+        for a, b in zip(at, at[1:]):
+            hop("s2i", "S1", "Y2", a, b, ALU.max)
+            tscal(reg("s2m", a, b), reg("s2i", a, b), TW - 1, None, ALU.bitwise_and)
+            if how != "n":
+                tscal(reg("S16", a, b), reg("s2m", a, b), -TW / 2, None, ALU.add)
+                ops[-1]["boost"] = 9
+        if how != "n":
+            turn("S16", 0, v0, v1, how)
         else:
             vcopy(reg("L", v0, v1), reg("s2m", v0, v1))
             tscal(reg("S16", v0, v1), reg("L", v0, v1), -TW / 2, None, ALU.add, half=True)
+    spare("S16", 0)
     for h in range(2):
         a, b = 512 * h, 512 * h + 512
-        lift = [c for c in range(a, b, 128) if signset(c)]
-        mm(reg("B%d" % (4 + h), 0, 512), full("I256"), reg("cpb", a, b), True, not lift, boost=0)
-        for c in lift:
-            si = sets.index(signset(c))
-            mm(reg("B%d" % (4 + h), c - a, c - a + 128), reg("wb", 128 * si, 128 * si + 128), full("ones"), False,
-               c == lift[-1], boost=0)
-        tt(reg("nth", a, b), reg("B%d" % (4 + h), 0, 512), reg("thi", a, b), ALU.subtract)
+        lift = []
+        for c in range(a, b, 32):
+            if signset(0, c) and c not in loose:
+                if lift and lift[-1][1] == c and signset(0, c) == signset(0, c - 32) and c - lift[-1][0] < 256:
+                    lift[-1][1] = c + 32
+                else:
+                    lift.append([c, c + 32])
+        nb = bank("f")
+        mm(reg(nb, 0, 512), full("I256"), reg("cpb", a, b), True, False, [reg("S1", 0, V)], boost=0)
+        for j in (0, 256):
+            mm(reg(nb, j, j + 256), full("Khalf"), reg("ones", 0, 256), False, j > 0 and not lift, boost=0)
+        if any(cfg["yv"]):
+            tscal(reg("own4", a, b), reg("cpb", a, b), -4.0, 4.0, ALU.mult, ALU.add, half=True)
+            ops[-1]["boost"] = 1
+        for c, d in lift:
+            si = sets.index(signset(0, c))
+            mm(reg(nb, c - a, d - a), reg("wb", 128 * si, 128 * si + 128), reg("ones", 0, d - c), False,
+               c == lift[-1][0], boost=0)
+        tt(reg("nth", a, b), reg(nb, 0, 512), reg("thi", a, b), ALU.subtract)
         ops[-1]["rd"].append(reg(*cfg["nthwait"]))
 
-    nd, nc, nf = [0], [0], [0]
+    mid = cfg["boost"].get("D", 5)
     for r in range(RO):
         tab = "tab%d" % r
-        win = reg(tab, 0, TW if r == 0 else TW + 8)
+        win = reg(tab, 0, TW if r == 0 else TW + 16)
         far = [reg("far%d" % r, 0, 999)]
         last = r == RO - 1
-        r1 = ends[r]
+        chunks = plan[r]
+        mcol, at = {}, 0
+        for c in chunks:
+            if c[2] == "n":
+                mcol[c[0]] = at
+                at += 16 * (c[1] - c[0])
         if r > 0:
-            for v0, v1 in cfg["hop1"]:
-                hop("h1", "any%d" % (r - 1), "Y", v0, v1, ALU.is_ge)
-            for v0, v1 in [(0, r0), (r0, r1)] + ([(r1, V)] if r1 < V else []):
-                if v0 == r0:
-                    hop("h2%d" % r, "h1", "Y", v0, v0 + cfg["cut"], ALU.is_ge)
-                    hop("h2%d" % r, "h1", "Y", v0 + cfg["cut"], v1, ALU.is_ge)
-                    ops[-1]["rd"].append(reg("L", 0, r0))
-                    turn("h2%d" % r, r)
+            gcopy(reg(tab, TW, TW + 16), reg(tab, 0, 16), [reg("far%d" % r, 0, 1)])
+            def step(o, win, v0, v1, stops):
+                runs = []
+                for a, b in sorted(cfg["cnt"][r - 1]):
+                    op = ALU.is_gt if a in cfg["yv"][r - 1] else ALU.is_ge
+                    if runs and runs[-1][2] == op:
+                        runs[-1][1] = b
+                    else:
+                        runs.append([a, b, op])
+                for a, b, op in runs:
+                    if max(a, v0) < min(b, v1):
+                        hop(o, win, "Y", max(a, v0), min(b, v1), op, stops)
+
+            step("h1", "any%d" % (r - 1), 0, V, cfg["hop1"])
+            for v0, v1, how in cfg["dec"][r]:
+                step("h2%d" % r, "h1", v0, v1, cfg["hop2"])
+                if how != "n":
+                    turn("h2%d" % r, r, v0, v1, how)
                     continue
-                hop("h2%d" % r, "h1", "Y", v0, v1, ALU.is_ge)
-                o = reg("B7", 0, v1 - v0)
-                mm(o, full("I16"), reg("S16", v0, v1), True, False)
+                o = reg(bank(), 0, v1 - v0)
+                mm(o, full("I16"), reg("S16", v0, v1), True, False, [reg(*cfg["topen"], 1)])
                 for rr in range(1, r + 1):
                     mm(o, full("I16"), reg("h2%d" % rr, v0, v1), False, rr == r)
                 tscal(reg("L", v0, v1), o, TW / 2, None, ALU.add)
+            spare("h2%d" % r, r)
+        copies = {}
 
-        def natural(j):
-            v0, v1, eng, w = nat[j]
-            for a in range(v0, v1, 64):
-                pr = reg("P", 16 * a, 16 * a + 1024)
-                gather(eng[(a - v0) // 64], pr, win, reg("L", a, a + 64), far)
-                mo = reg("M", mcol(a), mcol(a) + 1024)
-                add("V", lambda g, T, pr=pr, mo=mo: g.vector.tensor_tensor_scan(
-                    ap(T, mo), T.rst[:], ap(T, pr), 0.0, ALU.mult, ALU.max), [pr, reg("rst", 0, 1024)], [mo], "v", 512)
+        def repeat(v0, v1, per):
+            n = v1 - v0
+            for j in range(copies.get(v0, 0), per):
+                gcopy(reg("cw", 4 * v0 + j * n, 4 * v0 + (j + 1) * n), reg(tab, own0 + v0, own0 + v1), far)
+            copies[v0] = max(per, copies.get(v0, 0))
+            return reg("cw", 4 * v0, 4 * v0 + per * n)
 
-        def unit(u):
-            eng, blk, v0, v1, w = units[u]
-            n, eng = v1 - v0, eng[r]
-            per = min(cfg["links"][eng], cfg["call"][eng] // n)
-            if eng == "V":
-                src = reg(tab, own0 + v0, own0 + v1)
-                for j in range(per):
-                    cw = reg("cw", 4 * v0 + j * n, 4 * v0 + (j + 1) * n)
-                    add("G", lambda g, T, cw=cw: g.affine_select(ap(T, cw), ap(T, src), [[0, n]], ALU.is_ge, 0.0, 0, 0),
-                        [src] + far, [cw], "g", n)
-            for kk in range(0, 8, per):
-                o = reg("P", ubase[u] + kk * n, ubase[u] + (kk + per) * n)
-                if eng == "A":
-                    gather("A", o, win, ulist(u, kk, kk + per), far)
-                else:
-                    fused(o, win, ulist(u, kk, kk + per), reg("cw", 4 * v0, 4 * v0 + per * n), ALU.subtract, far)
-
-        def fold(j):
-            moves = []
-            for u in cfg["folds"][j]:
-                eng, blk, v0, v1, w = units[u]
-                n = v1 - v0
-                moves.append(([reg("P", ubase[u] + kk * n, ubase[u] + (kk + 1) * n) for kk in range(8)],
-                              [reg("FM%d%d" % (r, blk), v0, v1)]))
-            add("G", (moves, "par", "fl%d" % r), [x for m in moves for x in m[0]], [m[1][0] for m in moves], "f",
-                16 * n * len(moves), sig=("f%d_%d" % (r, j), None), rows=128 * len(moves))
-
-        def compare(kind, j):
-            if kind == "n":
-                v0, v1, eng, m = nat[j]
-                cb = "B%d" % (2 + nc[0] % 2)
-                nc[0] += 1
-                for i in range(4):
-                    mm(reg(cb, i, 512, 4), eye, reg(tab, own0 + v0, own0 + v1), True, True, far)
-                for a in range(0, 128, m):
-                    for i in range(4):
-                        at = 16 * v0 + 512 * i + 4 * a
-                        tt(reg("CM", at, at + 4 * m), reg("P", 16 * (v0 + a) + i, 16 * (v0 + a + m), 4),
-                           reg(cb, 4 * a, 4 * (a + m)), ALU.is_gt)
+        def unit(j, blk):
+            v0, v1 = chunks[j][:2]
+            n = v1 - v0
+            if chunks[j][2] == "n":
+                if blk:
+                    return
+                for a in range(v0, v1, 64):
+                    pr = reg("P", 16 * a, 16 * a + 1024)
+                    gather(chunks[j][3][(a - v0) // 64], pr, win, reg("L", a, a + 64), far)
+                    mo = reg("M", mcol[v0] + 16 * (a - v0), mcol[v0] + 16 * (a - v0) + 1024)
+                    add("V", lambda g, T, pr=pr, mo=mo: g.vector.tensor_tensor_scan(
+                        ap(T, mo), T.rst[:], ap(T, pr), 0.0, ALU.mult, ALU.max), [pr, reg("rst", 0, 1024)], [mo], "v", 512)
                 return
-            eng, blk, v0, v1, w = units[j]
-            n, base = v1 - v0, ubase[j]
-            if eng[r] == "V":
-                for k in range(0, 8 - w, 4):
-                    a, b = base + k * n, base + min(k + 4, 8 - w) * n
-                    tscal(reg("CM", a, b), reg("P", a, b), 0.0, None, ALU.is_gt, half=True)
-                for k in range(8 - w, 8, 2):
-                    a, b = base + k * n, base + min(k + 2, 8) * n
-                    act(reg("CM", a, b), reg("P", a, b), AF.Sign, bias=-0.5, boost=5)
+            eng, base = chunks[j][2 + blk][0], 16 * v0 + 8 * n * blk
+            per = max(1, min(cfg["links"][eng], cfg["call"][eng] // n))
+            if eng == "V":
+                cw = repeat(v0, v1, per)
+            if eng == "D":
+                own = reg(tab, own0 + v0, own0 + v1)
+                for kk in range(8):
+                    o = reg("CM", base + kk * n, base + (kk + 1) * n)
+                    add("S", lambda g, T, o=o: g.sync.dma_start(ap(T, o), ap(T, own)), [own] + far, [o], "d", 2 * n,
+                        sig=("w%d_%d%d" % (r, j, blk), None), rows=128)
+            for kk in range(0, 8, per):
+                o = reg("P", base + kk * n, base + (kk + per) * n)
+                k = 8 * blk + kk
+                off = box("L%d" % n, v0 // n, v0 // n + 1, k * n // 16, (k + per) * n // 16)
+                if eng == "V":
+                    fused(o, win, off, cw, ALU.subtract, far)
+                    continue
+                gather("A", o, win, off, far, -1.0 if eng == "D" else 1.0)
+            if eng == "D":
+                o, x = reg("CM", base, base + 8 * n), reg("P", base, base + 8 * n)
+                add("G", lambda g, T: g.dma_start(ap(T, o), ap(T, x), accum_op=ALU.add), [o, x], [o], "x", 16 * n,
+                    sig=("x%d_%d%d" % (r, j, blk), None), rows=128)
+                ops[-1]["first"] = not any(p["kind"] == "x" for p in ops[:-1])
+
+        def fold(j, blk):
+            v0, v1 = chunks[j][:2]
+            if chunks[j][2] == "n":
+                return
+            n = v1 - v0
+            base = 16 * v0 + 8 * n * blk
+            srcs = [reg("P", base + kk * n, base + (kk + 1) * n) for kk in range(8)]
+            dst = reg("FM%d%d" % (r, blk), v0, v1)
+            add("G", ([(srcs, [dst])], "par", "fl%d" % r, 3 if chunks[j][2 + blk][0] == "D" else 2), srcs, [dst], "f",
+                16 * n, sig=("f%d_%d%d" % (r, j, blk), None), rows=128)
+
+        def compare(j, blk):
+            v0, v1 = chunks[j][:2]
+            n = v1 - v0
+            if chunks[j][2] == "n":
+                if blk:
+                    return
+                for u in range(v0, v1, 128):
+                    cown, nv = reg(tab, own0 + u, own0 + u + 128), 4 - chunks[j][4]
+                    cb = bank()
+                    for i in range(4 if nv else 0):
+                        mm(reg(cb, i, 512, 4), eye, cown, True, True, far + [reg("P", 16 * u, 16 * u + 16)])
+                    for i in range(4):
+                        out, quarter = reg("CM", 16 * u + 512 * i, 16 * u + 512 * i + 512), reg("P", 16 * u + i, 16 * (u + 128), 4)
+                        if i < nv:
+                            tt(out, quarter, reg(cb, 0, 512), ALU.is_gt)
+                            continue
+                        db = bank()
+                        mm(reg(db, 0, 512), eye, quarter, True, False, boost=mid)
+                        for x in range(4):
+                            mm(reg(db, x, 512, 4), full("nI"), cown, False, x == 3, far, boost=mid)
+                        act(out, reg(db, 0, 512), AF.Sign, bias=-0.5)
+                return
+            eng, w = chunks[j][2 + blk][0], int(chunks[j][2 + blk][1])
+            base = 16 * v0 + 8 * n * blk
+            if eng != "A":
+                per, src = max(1, 1024 // n), "P" if eng == "V" else "CM"
+                for k in range(0, 8 - w, per):
+                    a, b = base + k * n, base + min(k + per, 8 - w) * n
+                    tscal(reg("CM", a, b), reg(src, a, b), 0.0, None, ALU.is_gt if eng == "V" else ALU.is_lt, half=True)
+                per = max(1, cfg["signcall"] // n)
+                for k in range(8 - w, 8, per):
+                    a, b = base + k * n, base + min(k + per, 8) * n
+                    act(reg("CM", a, b), reg(src, a, b), AF.Sign, bias=-0.5, scale=1.0 if eng == "V" else -1.0)
                 return
             cown = reg(tab, own0 + v0, own0 + v1)
             nv = 8 - w
             per = min(8, 512 // n)
             if nv:
-                cb = "B%d" % (2 + nc[0] % 2)
-                nc[0] += 1
+                cb = bank()
                 for i in range(min(per, nv)):
-                    mm(reg(cb, i * n, (i + 1) * n), eye, cown, True, True, far)
+                    mm(reg(cb, i * n, (i + 1) * n), eye, cown, True, True, far + [reg("P", base, base + 16)])
             for k in range(0, nv, per):
                 a, b = base + k * n, base + min(k + per, nv) * n
                 tt(reg("CM", a, b), reg("P", a, b), reg(cb, 0, b - a), ALU.is_gt)
             for k0 in range(nv, 8, per):
                 k1 = min(8, k0 + per)
-                db = cfg["dbanks"][nd[0] % len(cfg["dbanks"])]
-                nd[0] += 1
-                mm(reg(db, 0, (k1 - k0) * n), eye, reg("P", base + k0 * n, base + k1 * n), True, False, boost=5)
+                db = bank()
+                mm(reg(db, 0, (k1 - k0) * n), eye, reg("P", base + k0 * n, base + k1 * n), True, False, boost=mid)
                 for k in range(k0, k1):
-                    mm(reg(db, (k - k0) * n, (k - k0 + 1) * n), full("nI"), cown, False, k == k1 - 1, far, boost=5)
-                act(reg("CM", base + k0 * n, base + k1 * n), reg(db, 0, (k1 - k0) * n), AF.Sign, bias=-0.5, boost=5)
+                    mm(reg(db, (k - k0) * n, (k - k0 + 1) * n), full("nI"), cown, False, k == k1 - 1, far, boost=mid)
+                act(reg("CM", base + k0 * n, base + k1 * n), reg(db, 0, (k1 - k0) * n), AF.Sign, bias=-0.5)
 
         def registers(j):
-            c0, c1 = cfg["reg"][j]
+            c0, c1 = cfg["reg"][r][j]
             n = c1 - c0
-            folded = r0 <= c0 < r1
+            folded = chunk(r, c0)[2] != "n"
+            terms = []
             if folded:
-                three = [(eye, reg("FM%d%d" % (r, b), c0, c1), 0) for b in range(2)]
-                cuts = sorted(set([c0, c1] + [x[2] for x in units if c0 < x[2] < c1]))
-                for a, b in zip(cuts, cuts[1:]):
-                    nv = sum(1 for e, blk, v0, v1, w in units if e[r] == "V" and v0 <= a < v1)
-                    three.append(([eye, full("I2"), full("I3")][nv], reg(tab, par0 + a, par0 + b), a - c0))
+                for c in chunks:
+                    a, b = max(c0, c[0]), min(c1, c[1])
+                    if a < b:
+                        nv = sum(1 for u in c[2:4] if u[0] == "V")
+                        terms.append(([eye, full("I2"), full("I3")][nv], reg(tab, par0 + a, par0 + b), a - c0))
+                        terms += [(full("nI") if c[2 + blk][0] == "D" else eye, reg("FM%d%d" % (r, blk), a, b), a - c0)
+                                  for blk in range(2)]
             else:
-                three = [(eye, reg(tab, own0 + c0, own0 + c1), 0)]
-                three += [(eye, reg("M", mcol(c0) + 7 + 8 * b, mcol(c0) + 16 * n, 16), 0) for b in range(2)]
+                m0 = mcol[chunk(r, c0)[0]] + 16 * (c0 - chunk(r, c0)[0])
+                terms = [(eye, reg(tab, own0 + c0, own0 + c1), 0)]
+                terms += [(eye, reg("M", m0 + 7 + 8 * b, m0 + 16 * n, 16), 0) for b in range(2)]
             nxt = ("ypt" if folded else "ycb") if last else "tab%d" % (r + 1)
             d0 = c0 if last else (par0 if folded else own0) + c0
-            x, x2 = [reg("B" + b, 0, n) for b in cfg["xbanks"][j]]
-            for i, (w, xx, a) in enumerate(three):
-                mm(reg(x[0], a, a + cnt(xx)), w, xx, i == 0, i == len(three) - 1, far)
-            act(reg("qr", c0, c1), x, AF.Identity, bias=QOFF - 0.5 + 2.0 ** -9, scale=2.0 ** -8)
-            for i, (w, xx, a) in enumerate(three):
-                mm(reg(x2[0], a, a + cnt(xx)), w, xx, i == 0, False, far)
-            mm(x2, full("nI256"), reg("qr", c0, c1), False, True)
-            act(reg(nxt, d0, d0 + n), x2, AF.Identity, bias=QOFF * 256)
+            x = reg(bank(), 0, n)
+            lifted = c0 in cfg["regv"][r]
+            if lifted:
+                terms.insert(0, (full("K258"), reg("ones", 0, n), 0))
+            terms.reverse()
+            for i, (w, xx, a) in enumerate(terms):
+                mm(reg(x[0], a, a + cnt(xx)), w, xx, i == 0, i == len(terms) - 1, far + [t[1] for t in terms])
+            if lifted:
+                act(reg("qr", c0, c1), x, AF.Identity, bias=-127.5)
+                tt(reg(nxt, d0, d0 + n), x, reg("qr", c0, c1), ALU.subtract)
+                ops[-1]["boost"] = 9
+            else:
+                x2 = reg(bank(), 0, n)
+                ops[-1]["wr"].append(reg("open" + x[0], 0, 1))
+                act(reg("qr", c0, c1), x, AF.Identity, bias=QOFF - 0.5 + 2.0 ** -9, scale=2.0 ** -8)
+                for i, (w, xx, a) in enumerate(terms):
+                    mm(reg(x2[0], a, a + cnt(xx)), w, xx, i == 0, False, far + [reg("open" + x[0], 0, 1)])
+                mm(x2, full("nI256"), reg("qr", c0, c1), False, True)
+                act(reg(nxt, d0, d0 + n), x2, AF.Identity, bias=QOFF * 256)
             if not last:
-                send(r + 1, d0, d0 + n, rank == 0 and c0 == 0)
-                if c0 == 0:
-                    act(reg(nxt, TW, TW + 8), reg(x2[0], 0, 8), AF.Identity, bias=QOFF * 256)
-                    ops[-1]["only0"] = True
+                send(r + 1, d0, d0 + n, "via%d_%d" % (r, j) if c0 in cfg["relay"][r] else None)
                 return
             if folded:
                 src, dst = reg("ypt", c0, c1), reg("ycb", c0, c1)
-                add("G", ([([src], [dst])], "par", "loc"), [src], [dst], "r", 2 * n, sig=("yb%d" % j, None), rows=128)
+                add("G", ([([src], [dst])], "par", "loc", 0), [src], [dst], "r", 2 * n, sig=("yb%d" % j, None), rows=128)
             store("yc", "ycb", c0, c1, 2)
 
         def counts(c0, c1):
             n = c1 - c0
-            fb = cfg["fbanks"][nf[0] % len(cfg["fbanks"])]
-            nf[0] += 1
-            F, Cc = reg(fb, 0, n), reg(fb, 256, 256 + n)
+            fb = bank("f")
+            at = list(enumerate(blocks(c0, c1)))
+            m = 128 * len(at)
+            F, Cc = reg(fb, 0, m), reg(fb, 256, 256 + n)
             ks = []
-            for j in range(0, n, 128):
+            for j, v in at:
+                c = chunk(r, v)
                 for k in range(16):
-                    if r0 <= c0 < r1:
-                        u = [i for i, x in enumerate(units) if x[1] == k // 8 and x[2] <= c0 + j < x[3]][0]
-                        a = ubase[u] + (k % 8) * (units[u][3] - units[u][2]) + c0 + j - units[u][2]
+                    if c[2] != "n":
+                        a = 16 * c[0] + k * (c[1] - c[0]) + v - c[0]
                         cm = reg("CM", a, a + 128)
                     else:
-                        a = 16 * c0 + 512 * (k % 4)
+                        a = 16 * v + 512 * (k % 4)
                         cm = reg("CM", a + k // 4, a + 512, 4)
-                    half = any(k0 <= k < k1 for k0, k1 in signset(c0 + j))
-                    ks.append((j + k, cm, reg("hv", 0, 8) if half else reg("ones", 0, 8)))
-            ks.sort(key=lambda t: max(i for i, o in enumerate(ops) if o["wr"] and o["wr"][0][0] == "CM"
-                                      and o["wr"][0][1] < t[1][2] <= o["wr"][0][2]))
+                    half = any(k in range(*x) for x in signset(r, v))
+                    ks.append((128 * j + k, cm, reg("hv", 0, 8) if half else reg("ones", 0, 8)))
+            made = [(i, o["wr"][0]) for i, o in enumerate(ops) if o["wr"] and o["wr"][0][0] == "CM"]
+            ks.sort(key=lambda t: max(i for i, w in made if w[1] < t[1][2] <= w[2]))
             low = cfg["boost"]["F"]
-            for j in range(0, n, 128):
-                mm(reg(fb, j, j + 128), reg("nth", c0 + j, c0 + j + 128), eye, j == 0, False, boost=low)
+            for j, v in at:
+                mm(reg(fb, 128 * j, 128 * j + 128), reg("nth", v, v + 128), eye, j == 0, False, [ks[cfg["fopen"]][1]],
+                   boost=low)
+                if signset(r, v) and v in loose:
+                    si = sets.index(signset(r, v))
+                    mm(reg(fb, 128 * j, 128 * j + 128), full("ones"), reg("wb", 128 * si, 128 * si + 128), False, False,
+                       boost=low)
             for i, (k, a, x) in enumerate(ks):
                 mm(reg(fb, k, k // 128 * 128 + 128, 16), a, x, False, i == len(ks) - 1, boost=low)
-            run = reg("run", c0, c1)
+            run = reg("run", 2 * c0, 2 * c0 + m)
             x = F
-            if cfg["sign"] == "A":
-                x = reg("sg", c0, c1)
+            if c0 in cfg["sign"][r]:
+                x = reg("sg", 2 * c0, 2 * c0 + m)
                 act(x, F, AF.Copy)
-            add("V", lambda g, T: g.vector.tensor_tensor_scan(ap(T, run), T.r16[:, 0:n], ap(T, x), 0.0, ALU.mult, ALU.min),
-                [x, reg("r16", 0, 256)], [run], "v", n if x == F else n * 0.5)
-            for j in range(0, n, 128):
-                mm(reg(fb, j, j + 128), reg("run", c0 + j, c0 + j + 128), eye, True, True)
-            act(reg("any%d" % r, c0, c1), F, AF.Sign, scale=-1.0)
+            add("V", lambda g, T: g.vector.tensor_tensor_scan(ap(T, run), T.r16[:, 0:m], ap(T, x), 0.5, ALU.max, ALU.min),
+                [x, reg("r16", 0, 256)], [run], "v", m if x == F else m / 2)
+            for j, v in at:
+                mm(reg(fb, v - c0, v - c0 + 128), reg("run", 2 * c0 + 128 * j, 2 * c0 + 128 * j + 128), eye, True, True)
+            act(reg("any%d" % r, c0, c1), reg(fb, 0, n), AF.Sign, bias=0.5, scale=-1.0)
             if last:
                 for j in range(RO):
                     mm(Cc, full("Dm"), reg("any%d" % j, c0, c1), j == 0, j == RO - 1)
                 tt(reg("ygb", c0, c1), Cc, reg("gpi", c0, c1), ALU.add)
                 store("yg", "ygb", c0, c1, 4)
+            elif c0 in cfg["yv"][r]:
+                tt(reg("Y", c0, c1), reg(fb, 0, n), reg("own4", c0, c1), ALU.mult)
             else:
                 mm(Cc, full("nI"), reg("cpb", c0, c1), True, False)
                 mm(Cc, full("n2I"), reg("any%d" % r, c0, c1), False, True)
                 act(reg("Y", c0, c1), Cc, AF.Abs, bias=2.0)
 
-        steps = {"gn": natural, "gu": unit, "cn": lambda j: compare("n", j), "cu": lambda j: compare("u", j),
-                 "f": lambda j: counts(*cfg["cnt"][j]), "r": registers, "o": fold}
+        steps = {"g": unit, "c": compare, "o": fold, "f": lambda j: counts(*cfg["cnt"][r][j]), "r": registers}
         for word in cfg["seq"][r].split():
             at = len(ops)
-            steps[word[:-1]](int(word[-1]))
+            steps[word[0]](*map(int, word[1:]))
             for i in range(at, len(ops)):
                 o = ops[i]
+                o["word"] = "%d%s" % (r, word)
                 if word in cfg["late"] and o["wr"] and o["wr"][0][0][:3] in ("any", "qr"):
                     o["rd"].append(reg("after%d" % r, 0, len(ops)))
-                if o["kind"] == "ag" and word[:2] == "gu":
+                if o["kind"] == "ag":
                     o["wr"].append(reg("after%d" % r, i, i + 1))
-    return ops
+    read = {x[0] for o in ops for x in o["rd"]}
+    return [o for i, o in enumerate(ops) if not first_const <= i < last_const or o["wr"][0][0] in read]
 
 
 def link(ops):
@@ -516,23 +690,23 @@ def link(ops):
         pre = {}
         for rs, iswr in ((o["rd"], False), (o["wr"], True)):
             for name, lo, hi, step in rs:
-                for j, a, b, w, st in hist.get(name, []):
-                    if isinstance(st, tuple) and isinstance(step, tuple) and (st[3] <= step[2] or step[3] <= st[2]):
-                        continue
-                    if (w or iswr) and a < hi and lo < b and j != i:
+                for j, a, b, st in hist.get((name, True), []) + (hist.get((name, False), []) if iswr else []):
+                    if a < hi and lo < b and j != i:
+                        if isinstance(st, tuple) and isinstance(step, tuple) and (st[3] <= step[2] or step[3] <= st[2]):
+                            continue
                         both_pe = ops[j]["q"] == "P" and o["q"] == "P"
                         pre[j] = pre.get(j, False) or not both_pe
-                if name[0] == "B" and len(name) == 2:
+                if name[0] == "#":
                     j = bank.get(name)
                     if j is not None and j != i:
                         pre[j] = pre.get(j, False) or ops[j]["q"] != o["q"]
                     bank[name] = i
         for rs, iswr in ((o["rd"], False), (o["wr"], True)):
             for name, lo, hi, step in rs:
-                h = hist.setdefault(name, [])
                 if iswr and step == 1:
-                    h[:] = [e for e in h if not (lo <= e[1] and e[2] <= hi)]
-                h.append((i, lo, hi, iswr, step))
+                    for w in (True, False):
+                        hist[name, w] = [e for e in hist.get((name, w), []) if not (lo <= e[1] and e[2] <= hi)]
+                hist.setdefault((name, iswr), []).append((i, lo, hi, step))
         o["pre"] = pre
     return ops
 
@@ -544,45 +718,86 @@ def cost(o, e):
     if k == "vg":
         return 50 + n * e["g"] * e["cyc"], 0, 0
     if k == "a":
-        return e["oa"] + max(64, n) * e["cyc"], 0, 0
+        return e["oa"] + max(64, n) * e["cyc"] * e["ra"], 0, 0
     if k == "ag":
-        return 65 + n * e["g"] * e["cyc"], 0, 0
+        return 65 + n * e["g"] * e["cyc"] * e["ra"], 0, 0
     if k == "p":
         return e["op"] + n * e["pe"], 0, 0
     if k == "g":
         return 170 + 2 * n * e["cyc"], 0, 0
-    move = o["rows"] / 16 * e["drow"] * (e["frow"] if k == "f" else 1) + 8 * n / e["dbw"] * (e["fb"] if k == "f" else 1)
+    if k == "h":
+        return (e["riss"] + e["rfix"] + (e["rfirst"] if o["first"] else 0) + 8 * (NR - 1) * e["drow"]
+                + 8 * n / e["dbw"] * e["sx"]), 0, 0
+    move = (o["rows"] / 16 * e["drow"] * (e["frow"] if k == "f" else 1)
+            + 8 * n / e["dbw"] * {"f": e["fb"], "x": e["xb"], "r": e["sx"] if o["rows"] > 128 else 1}.get(k, 1))
     if k == "d":
         return 60, move, e["dfix"]
+    if k == "x":
+        return e["xiss"] + (e["rfirst"] if o["first"] else 0), move, e["dfix"]
     return e["riss"] + (e["rfirst"] if o["first"] else 0), move, e["rfix"] + (e["fx"] if k == "f" else 0)
 
 
-def schedule(ops, e, delta):
+def schedule(ops, e, cfg):
+    key, best = [(-o["boost"], i) for i, o in enumerate(ops)], None
+    for _ in range(cfg["passes"]):
+        start, banks, waits = greedy(ops, e, key, cfg)
+        end, at, key = justify(hand_over(ops, waits), e, start)
+        if best is None or end < best[0]:
+            best = (end, at, banks, waits)
+    at = best[1]
+    LAST[:] = [at]
+    return {q: sorted((i for i, o in enumerate(ops) if o["q"] == q), key=lambda i: (at[i], i)) for q in "VAPGSH"}, best[2], best[3]
+
+
+def hand_over(ops, waits):
+    ops = list(ops)
+    for i, j in waits:
+        ops[i] = dict(ops[i], pre=dict(ops[i]["pre"]))
+        ops[i]["pre"][j] = ops[i]["pre"].get(j, False) or ops[j]["q"] != ops[i]["q"]
+    return ops
+
+
+def greedy(ops, e, key, cfg):
     n = len(ops)
     succ = [[] for _ in range(n)]
+    opens, closes = {}, {}
     for i, o in enumerate(ops):
         for j in o["pre"]:
             succ[j].append(i)
-    prio = [o["boost"] for o in ops]
+        for x in o["rd"] + o["wr"]:
+            if x[0][0] == "#":
+                opens.setdefault(x[0], i)
+                closes[x[0]] = i
+    opens = {i: x for x, i in opens.items()}
+    shut = {i: x for x, i in closes.items()}
+    held = {b: (0.0, None) for b in "01234567"}
+    banks, waits = {}, []
     left = [len(o["pre"]) for o in ops]
     fin, ready = [0.0] * n, [0.0] * n
-    cand = {q: [] for q in "VAPGS"}
-    free = {q: 0.0 for q in "VAPGS"}
+    cand = {q: [] for q in "VAPGSH"}
+    free = {q: 0.0 for q in "VAPGSH"}
     start = [0.0] * n
     dma = [0.0]
     for i in range(n):
         if left[i] == 0:
             cand[ops[i]["q"]].append(i)
     for _ in range(n):
-        t, q = min((max(free[q], min(ready[i] for i in cand[q])), q) for q in "VAPGS" if cand[q])
-        isdma = [i for i in cand[q] if ops[i]["kind"] == "d" and ready[i] <= t]
-        if isdma:
-            i = min(isdma)
-        else:
-            i = max((i for i in cand[q] if ready[i] <= t + delta), key=lambda i: (prio[i], -i))
+        soon = {k: min((held[b][0] for b in v if held[b]), default=1e18) for k, v in cfg["banks"].items()}
+        when = {i: max(ready[i], soon[opens[i][1]]) if i in opens else ready[i] for q in cand for i in cand[q]}
+        t, q = min((max(free[q], min(when[i] for i in cand[q])), q) for q in cand if cand[q])
+        assert t < 1e17
+        i = min((i for i in cand[q] if when[i] <= t + cfg["delta"]), key=lambda i: key[i])
         cand[q].remove(i)
         a, b, c = cost(ops[i], e)
-        st = max(free[q], ready[i])
+        st = max(free[q], when[i])
+        if i in opens:
+            bk = [x for x in cfg["banks"][opens[i][1]] if held[x] and held[x][0] <= st][0]
+            if held[bk][1] is not None:
+                waits.append((i, held[bk][1]))
+            banks[opens[i]] = "B" + bk
+            held[bk] = None
+        if i in shut:
+            held[banks[shut[i]][1]] = (st + a + e["sem"], i)
         start[i] = st
         free[q] = st + a
         if b:
@@ -595,10 +810,10 @@ def schedule(ops, e, delta):
             left[j] -= 1
             if left[j] == 0:
                 cand[ops[j]["q"]].append(j)
-    return justify(ops, e, start)
+    return start, banks, waits
 
 
-def justify(ops, e, start, rounds=6):
+def justify(ops, e, start, rounds=2):
     n = len(ops)
     res, dur, pre = [o["q"] for o in ops], [cost(o, e)[0] for o in ops], [[] for o in ops]
     out, key = list(range(n)), list(start)
@@ -620,12 +835,10 @@ def justify(ops, e, start, rounds=6):
 
     def place(before, after, rank):
         left, ready, at = [len(x) for x in before], [0.0] * m, [0.0] * m
-        busy = {q: [] for q in "VAPGSD"}
-        cand = [(rank[i], i) for i in range(m) if not left[i]]
+        busy = {q: [] for q in "VAPGSHD"}
+        cand = sorted(((rank[i], i) for i in range(m) if not left[i]), reverse=True)
         while cand:
-            pick = min(cand)
-            cand.remove(pick)
-            i = pick[1]
+            i = cand.pop()[1]
             b, t = busy[res[i]], ready[i]
             p = len(b)
             while p and b[p - 1][1] > t:
@@ -640,43 +853,68 @@ def justify(ops, e, start, rounds=6):
                 left[j] -= 1
                 if not left[j]:
                     cand.append((rank[j], j))
+                    cand.sort(reverse=True)
         return at
 
     best = None
     for _ in range(rounds):
+        for i, o in enumerate(ops):
+            if "pin" in o:
+                key[i] = key[out[i]] = o["pin"] - 1e9
         at = place(pre, suc, key)
         end = max(at[i] + dur[i] for i in range(m))
         if best is None or end < best[0]:
             best = (end, at)
         back = place(suc, pre, [-(at[i] + dur[i]) for i in range(m)])
         key = [-(back[i] + dur[i]) for i in range(m)]
-    return {q: sorted((i for i in range(n) if res[i] == q), key=lambda i: (best[1][i], i)) for q in "VAPGS"}
+    return best[0], best[1][:n], key[:n]
 
 
 ORDER = []
+BANK = {}
+LAST = []
 
 
 def rank_program(g, core, T, topo):
-    rank = T.rank_of(core)
-    if rank is None:
-        return
     by_die = sorted(range(NR), key=lambda q: (topo.die(T.cores[q]), q))
+    spare = sorted((c for c in topo.cores_of(T.cores[0]) if c not in T.cores), key=lambda c: (topo.die(c), c))
+    rank = T.rank_of(core)
+    if rank is None and not (core in spare and any(CFG["relay"])):
+        return
+    aide = rank is None
+    if aide:
+        rank = by_die[spare.index(core)]
     par = by_die[by_die.index(rank) ^ 1]
     if not ORDER:
-        ORDER.append(schedule(link(build(0, 1, CFG)), EST, CFG["delta"]))
+        ORDER.extend(schedule(link(build(0, 1, CFG)), EST, CFG))
+        BANK.update(ORDER[1])
     order = ORDER[0]
-    every = build(rank, par, CFG)
-    keep = [i for i, o in enumerate(every) if rank == 0 or not o.get("only0")]
-    where = {i: j for j, i in enumerate(keep)}
-    order = {q: [where[i] for i in order[q] if i in where] for q in order}
-    ops = link([every[i] for i in keep])
-    dests = {"all": [c for c in T.cores if c != core], "par": [T.cores[par]]}
+    ops = hand_over(link(build(rank, par, CFG)), ORDER[2])
+    dests = {"all": [c for c in T.cores if c != T.cores[rank]], "par": [T.cores[par]], "aide": [spare[by_die.index(rank)]]}
     engines = [e for e in topo.engines(core, T.cores[par]) if all(e in topo.engines(core, c) for c in dests["all"])]
     neng = len(engines)
+
+    def remote(o, eng):
+        moves, to, loc, alu = o["fn"]
+        ids = [DstId(rid=topo.addr(c)[0], pnc=topo.addr(c)[1]) for c in dests[to]]
+        g.remote_dma_fused([RemoteDMATransfer(
+            dst_ids=[d for x in dsts for d in ids], dma_engine_mask=sum(1 << e for e in eng),
+            remote_sem=T.sem[o["sig"][0]], srcs=[T[x[0]][:, x[1]:x[2]] for x in srcs],
+            dsts=[T[x[0]][:, x[1]:x[2]] for x in dsts for d in ids], alu_op=alu)
+            for srcs, dsts in moves], local_sem=T.sem[loc])
+
+    if aide:
+        for i in order["H"]:
+            for j in ops[i]["pre"]:
+                g.wait_ge(T.sem[ops[j]["sig"][0]], neng)
+            remote(ops[i], engines)
+        g.wait_ge(T.sem["loc"], neng * len(order["H"]))
+        return
     total = {s: 0 for s in SEMAPHORES}
     total["arr0"] = 2 * (NR - 1) * neng
     for r in range(1, RO):
-        total["arr%d" % r] = (len(CFG["reg"]) * (NR - 1) + (1 if rank else 0)) * neng
+        total["arr%d" % r] = (len(CFG["reg"][r - 1]) - 1) * (NR - 1) * neng
+        total["head%d" % r] = (NR - 1) * neng
     for q in "VAPGS":
         k = 0
         for i in order[q]:
@@ -686,14 +924,16 @@ def rank_program(g, core, T, topo):
                 o["sig"] = (ENGSEM[q], k)
                 total[ENGSEM[q]] = k
             elif o["kind"] in "rf":
+                o["eng"] = engines[:CFG["foldeng"]] if o["kind"] == "f" else engines
                 if o["fn"][1] == "par":
-                    total[o["sig"][0]] = neng
+                    total[o["sig"][0]] = len(o["eng"])
                 o["sig"] = (o["sig"][0], total[o["sig"][0]])
-                total[o["fn"][2]] += neng
-            elif o["sig"][0] == "outs":
-                total["outs"] += 16
+                total[o["fn"][2]] += len(o["eng"])
             else:
-                total[o["sig"][0]] = 16
+                total[o["sig"][0]] += 16
+    for o in ops:
+        if o["kind"] in "dxh":
+            o["sig"] = (o["sig"][0], total[o["sig"][0]])
     queue = {"V": g.vector, "A": g.scalar, "P": g.tensor, "G": g, "S": g.sync}
     for q in "VAPGS":
         seen = {}
@@ -712,17 +952,9 @@ def rank_program(g, core, T, topo):
                     queue[q].wait_ge(T.sem[s], need[s])
                     seen[s] = need[s]
             if o["kind"] in "rf":
-                moves, to, loc = o["fn"]
-                ids = [DstId(rid=topo.addr(c)[0], pnc=topo.addr(c)[1]) for c in dests[to]]
-                share = neng // len(moves)
-                g.remote_dma_fused([RemoteDMATransfer(
-                    dst_ids=[d for x in dsts for d in ids],
-                    dma_engine_mask=sum(1 << e for e in engines[share * m:share * (m + 1)]),
-                    remote_sem=T.sem[o["sig"][0]], srcs=[T[x[0]][:, x[1]:x[2]] for x in srcs],
-                    dsts=[T[x[0]][:, x[1]:x[2]] for x in dsts for d in ids], alu_op=2 if len(srcs) > 1 else 0)
-                    for m, (srcs, dsts) in enumerate(moves)], local_sem=T.sem[loc])
+                remote(o, o["eng"])
             else:
-                o["fn"](g, T).then_inc(T.sem[o["sig"][0]], 16 if o["kind"] == "d" else 1)
+                o["fn"](g, T).then_inc(T.sem[o["sig"][0]], 16 if o["kind"] in "dx" else 1)
     for s in SEMAPHORES:
         if total[s]:
             g.sync.wait_ge(T.sem[s], total[s])

@@ -6,6 +6,7 @@ NR = 4
 RO = 3
 TW = NR * V
 BIG = 65536.0
+OWN = 16 * BIG
 QOFF = 129.0
 
 QUARTERS = [(0, 256), (256, 512), (512, 768), (768, 1024)]
@@ -46,16 +47,22 @@ CFG.update({
     "fopen": 4, "hop1": [384, 512], "hop2": [], "hw": "A", "passes": 1,
     "cnt": [[(0, 128), (128, 384), (384, 640), (640, 896), (896, 1024)]] * 3,
     "reg": [[(0, 128), (128, 384), (384, 640), (640, 896), (896, 1024)]] * 3,
-    "foldeng": 16, "regv": [[], [], []], "yv": [[], [], []], "signcall": 512, "pin": True, "const": "A", "relay": [[], [], []],
+    "foldeng": 16, "regv": [[], [], []], "yv": [[], [], []], "signcall": 512, "onv": [], "quick": [], "short": [], "route": ["aaddd", "aaddd"], "first": [(0, 128, "d"), (128, 1024, "d")], "less": True, "mod": "A", "cwfar": False, "sums": [(0, 512), (512, 1024)], "hop0": [512], "cut0": [512], "via0": False, "pin": True, "const": "A", "relay": [[], [], []],
 })
 EST = {"cyc": 0.9, "g": 1.56, "ov": 30.0, "oa": 30.0, "pe": 0.5, "op": 5.0, "sem": 90.0,
        "dfix": 1800.0, "drow": 14.0, "dbw": 24.0, "rfix": 2000.0, "riss": 600.0, "rfirst": 2000.0,
-       "frow": 6.0, "fb": 0.9, "fx": 500.0, "xiss": 1000.0, "xb": 2.0, "sx": 1.0, "ra": 1.0}
+       "frow": 6.0, "fb": 0.9, "fx": 500.0, "xiss": 1000.0, "xb": 2.0, "sx": 1.0, "ra": 1.0, "rw": 0.0}
 EST.update(dict(cyc=.9, pe=.62, op=4, ov=13, oa=38, g=1.56, frow=6, fb=1.0, riss=420, rfix=1450, sem=55, dbw=27, drow=10,
                 sx=1.8, dfix=1300, rfirst=1800, fx=250))
 NOW = {'plan': [(0, 128, 'n', 'AA', 3), (128, 384, 'A8', 'V0'), (384, 640, 'A4', 'V0'), (640, 896, 'A0', 'V2'), (896, 1024, 'n', 'AA', 0)], 'seq': 'g00 g10 g21 g11 c10 o10 o11 r0 g20 c00 r1 o20 o21 g30 c20 g31 g40 r4 o31 c30 c31 f0 o30 r3 c11 c21 c40 f2 f4 f3 r2 f1', 'dec': [(0, 128, 'n'), (128, 896, '01'), (896, 1024, 'n')], 'boost': {'VP': 5, 'VM': 5, 'VCM': 5, 'VS16': 8, 'Vnth': 6, 'AP': 5, 'F': 9, 'ACM': 5, 'Gcw': 6, 'VY': 4, 'D': 9, 'Vrun': 6}, 'delta': 0.0, 'banks': {'t': '01', 'f': '765', 'g': '4321076'}, 'fopen': 0, 'hop1': [256], 'hop2': [320], 'sign': [[640], [640], [640]], 'regv': [[0, 384, 640, 896], [0, 384, 640, 896], [0, 384, 640, 896]], 'yv': [[], [], []], 'links': {'A': 4, 'V': 2, 'D': 4}, 'call': {'A': 1024, 'V': 512, 'D': 1024}, 'hw': 'V'}
 EST.update(dict(cyc=.95, pe=.62, op=2, ov=12, oa=42, g=1.4, frow=6.3, fb=1.05, riss=400, rfix=1100, sem=140, dbw=26, drow=10, sx=1.8, dfix=1400, rfirst=2000, fx=600))
 NOW = {'plan': [[(0, 128, 'n', 'AA', 3), (128, 384, 'A8', 'V4'), (384, 640, 'A4', 'V0'), (640, 896, 'A0', 'V2'), (896, 1024, 'n', 'AA', 0)], [(0, 128, 'n', 'AA', 3), (128, 384, 'A8', 'V0'), (384, 640, 'A4', 'V0'), (640, 896, 'A0', 'V4'), (896, 1024, 'n', 'AA', 0)], [(0, 128, 'n', 'AA', 3), (128, 384, 'A8', 'V0'), (384, 640, 'A4', 'V0'), (640, 896, 'A0', 'V4'), (896, 1024, 'n', 'AA', 0)]], 'seq': ['g21 g10 c10 g11 g20 g00 r0 o11 o20 o10 c00 r1 g30 f0 o30 c20 g40 o21 r4 g31 c11 c40 c30 f1 r2 f4 o31 c31 c21 r3 f3 f2', 'g00 g10 g21 g11 o10 g20 r0 c00 o21 c10 o11 g30 c21 g40 o30 f0 g31 o20 r1 r4 c20 o31 c31 c11 r3 c40 r2 c30 f3 f2 f1 f4', 'g10 g21 o10 g00 c10 g20 g11 c00 o11 o20 r1 g30 c20 o30 f0 g40 o21 c30 g31 r4 c40 c11 r0 o31 c21 c31 r3 f3 f4 f2 f1 r2'], 'dec': [[(0, 128, 'n'), (128, 896, '10'), (896, 1024, 'n')], [(0, 128, 'n'), (128, 896, '01'), (896, 1024, 'n')], [(0, 128, 'n'), (128, 896, '01'), (896, 1024, 'n')]], 'boost': {'VP': 5, 'VM': 5, 'VCM': 5, 'VS16': 9, 'Vnth': 9, 'AP': 5, 'F': 9, 'ACM': 5, 'Gcw': 9, 'VY': 2, 'D': 9, 'Vrun': 6, 'Aqr': 9, 'AY': 6}, 'delta': 0.0, 'banks': {'t': '01', 'f': '765', 'g': '4321076'}, 'fopen': 4, 'hop1': [], 'hop2': [256], 'sign': [[128, 640], [640], [640]], 'regv': [[0, 384, 640], [384, 640], [0, 384, 640, 896]], 'yv': [[128, 384], [128, 384], []], 'hw': 'A', 'relay': [[0, 128], [0, 128], []]}
+NOW.update(cut0=[512], mod="V", hw="V", sums=[(0, 512), (512, 768), (768, 1024)], loads=['c0a', 'c0b', 'cp0', 'cp1', 'gp0', 'gp1', 'gp2', 'rfs'],
+           first=[(0, 512, "m"), (512, 1024, "m")], c0a=512, route=["aaddd", "aaddd"], less=True)
+NOW.update({'plan': [(0, 128, 'n', 'AAAV', 3), (128, 384, 'A8', 'V0'), (384, 640, 'A2', 'V0'), (640, 896, 'A2', 'V4'), (896, 1024, 'n', 'AA', 0)], 'seq': ['g00 g21 g10 g11 c00 c10 o11 c11 g20 r0 o10 c21 o21 g30 o30 o20 g31 c20 f2 c31 f1 r1 c30 r2 g40 f0 c40 f4 f3 o31 r4 r3', 'g10 g21 g00 c00 g11 c10 o21 c11 o11 r0 g20 c21 g30 o20 o30 g31 o10 g40 c20 f2 r2 c31 f1 c30 r1 f0 c40 o31 f3 f4 r3 r4', 'g10 g21 g00 c00 g11 c10 o11 c11 c21 r0 g20 g30 o21 o20 o30 g31 o10 c20 r2 o31 f1 f2 r1 c31 f0 c30 g40 c40 f4 r4 r3 f3'], 'dec': [(0, 128, 'n'), (128, 896, '01'), (896, 1024, 'n')], 'boost': {'VP': 5, 'VM': 5, 'VCM': 5, 'VS16': 5, 'Vnth': 6, 'AP': 5, 'F': 9, 'ACM': 5, 'Gcw': 6, 'VY': 2, 'D': 9, 'Vrun': 6, 'Aqr': 9, 'AY': 9}, 'fopen': 4, 'hop1': [256, 640], 'hop2': [384], 'sign': [[384, 640], [], [640]], 'regv': [[384, 640, 896], [384, 640, 896], [0, 384, 640, 896]], 'yv': [[384], [], []], 'route': ['fafdd', 'aafdd'], 'links': {'A': 8, 'V': 4, 'D': 4}, 'call': {'A': 2048, 'V': 1024, 'D': 1024}, 'hw': 'V', 'loads': ['cp0', 'c0a', 'cp1', 'gp0', 'c0b', 'gp1', 'gp2', 'rfs'], 'mod': 'A', 'cut0': [320, 640], 'sums': [(0, 512), (512, 1024)], 'signcall': 512, 'quick': [0], 'short': []})
+EST.update({'sem': 200, 'riss': 440.0, 'drow': 11.0, 'dbw': 23.4, 'fb': 0.84, 'rfix': 1089.0, 'rfirst': 1800.0})
+NOW.update({'seq': ['g10 g00 g21 g11 c00 c10 c11 o11 g20 c21 r0 g30 g31 o20 c20 o30 o10 f2 c31 o21 g40 f1 r1 c30 r2 f0 c40 o31 f3 f4 r4 r3', 'g21 g10 g00 c00 g11 c10 o21 o11 r0 c11 g20 o20 g30 c21 g31 g40 c20 o10 f1 c31 r2 o30 c30 r1 c40 o31 f4 f2 f3 r3 r4 f0', 'g11 o11 g21 g00 g10 c00 c10 c11 g20 c21 r0 g30 o30 o20 o21 g31 o31 o10 c20 r2 r1 f1 f2 r3 c31 f0 g40 c40 c30 r4 f3 f4'], 'boost': {'VP': 5, 'VM': 5, 'VCM': 5, 'VS16': 6, 'Vnth': 5, 'AP': 5, 'F': 9, 'ACM': 5, 'Gcw': 2, 'VY': 2, 'D': 9, 'Vrun': 6, 'Aqr': 9, 'AY': 9}, 'hop2': [256], 'yv': [[], [], []], 'loads': ['cp0', 'cp1', 'c0a', 'gp0', 'gp1', 'gp2', 'rfs', 'c0b'], 'onv': ['I2', 'K258', 'r16']})
+EST.update({'drow': 9.9, 'sx': 1.62, 'dfix': 1120.0})
 for _k in ("plan", "dec", "seq", "cnt", "reg"):
     if _k in NOW and not isinstance(NOW[_k][0], list) and not (_k == "seq" and isinstance(NOW[_k], list)):
         NOW[_k] = [NOW[_k]] * 3
@@ -79,15 +86,16 @@ _decl("P CM", "sbuf", [128, 16 * V], "bfloat16")
 _decl("M", "sbuf", [128, 4 * V], "bfloat16")
 _decl("rst", "sbuf", [128, 1024], "bfloat16")
 _decl("nog S16 h21 h22", "sbuf", [128, V], "float16")
-_decl("ycb ypt cpb own4 nth any0 any1 any2 Y h1 qr", "sbuf", [128, V], "bfloat16")
+_decl("ycb ypt own nth any0 any1 any2 Y h1 qr", "sbuf", [128, V], "bfloat16")
 _decl("FM00 FM01 FM10 FM11 FM20 FM21", "sbuf", [128, V], "bfloat16")
-_decl("ygb Gw Hw Y2 S1", "sbuf", [128, V], "float32")
+_decl("ygb Gw Hw Y2 S1 S2", "sbuf", [128, V], "float32")
 _decl("lo", "sbuf", [128, 512], "bfloat16")
-_decl("I nI I2 I3 I256 nI256 n2I nBI tri0 tri sh Dm K258 Khalf", "sbuf", [128, 128], "bfloat16")
+_decl("now back", "sbuf", [128, 272 * 5], "bfloat16")
+_decl("nI I2 I3 nY nTW nI256 n2I BI tri0 sh Dm K258 Klift", "sbuf", [128, 128], "bfloat16")
 _decl("J", "sbuf", [128, 160], "bfloat16")
 _decl("ones", "sbuf", [128, 256], "bfloat16")
 _decl("J0 J1", "sbuf", [128, 160], "float16")
-_decl("ntri16 I16", "sbuf", [128, 128], "float16")
+_decl("tri16 I16", "sbuf", [128, 128], "float16")
 _decl("r16", "sbuf", [128, 256], "bfloat16")
 _decl("hv", "sbuf", [128, 8], "bfloat16")
 _decl("kcol", "sbuf", [128, 8], "float32")
@@ -95,7 +103,7 @@ _decl("wb", "sbuf", [128, 128, 16], "bfloat16")
 _decl("B0 B1", "psum", [128, 32, 16], "float32")
 _decl("B2 B3 B4 B5 B6 B7", "psum", [128, 512], "float32")
 _decl("hT0 hT1 hT2", "sbuf", [128, 32, 32], "float16")
-for _n in (128, 160, 192, 224, 256, 288, 320, 384, 448, 512):
+for _n in {c[1] - c[0] for p in CFG["plan"] for c in p if c[2] != "n"}:
     _decl("L%d" % _n, "sbuf", [128, V // _n + 1, _n], "uint16")
 _decl("run sg", "sbuf", [128, 2 * V], "bfloat16")
 _decl("cw", "sbuf", [128, 4 * V], "bfloat16")
@@ -106,12 +114,16 @@ SEMAPHORES = (["sV", "sA", "sP", "sG", "c0a", "c0b", "cp0", "cp1", "gp0", "gp1",
                  if c[2] != "n"]
               + ["%s%d_%d%d" % (x, r, j, b) for r in range(RO) for j, c in enumerate(CFG["plan"][r]) for b in range(2)
                  for x in "wx" if c[2 + b][0] == "D"]
-              + ["via%d_%d" % (r, j) for r in range(RO - 1) for j, c in enumerate(CFG["reg"][r]) if c[0] in CFG["relay"][r]]
+              + ["via%d_%d" % (r, j) for r in range(RO - 1) for j, c in enumerate(CFG["route"][r]) if c != "d"]
+              + ["via%d" % j for j, c in enumerate(CFG["first"]) if c[2] != "d"]
               + ["yb%d" % j for j in range(len(CFG["reg"][-1]))])
 ENGSEM = {"V": "sV", "A": "sA", "P": "sP", "G": "sG"}
 
 
-def build(rank, par, cfg):
+WAYS = {"all": (1, 2, 3), "par": (1, 0, 1), "aide": (1, 0, 0), "mir": (0, 1, 1), "faraide": (0, 1, 0), "pair": (2, 0, 2)}
+
+
+def build(rank, ring, cfg):
     ops = []
 
     def add(q, fn, rd, wr, kind, n, sig=None, rows=0, boost=None):
@@ -217,20 +229,34 @@ def build(rank, par, cfg):
 
     nsend = [0]
 
-    def send(r, s0, s1, relay=None):
-        x = reg("tab%d" % r, s0, s1)
-        nsend[0] += 1
-        head = r > 0 and s0 % V == 0
-        done = reg("far%d" % r, 0, 1) if head else reg("far%d" % r, nsend[0], nsend[0] + 1)
-        sig, size = (("head%d" if head else "arr%d") % r, None), (s1 - s0) * 2
-        if relay:
-            add("G", ([([x], [x])], "aide", "loc", 0), [x], [reg(relay, 0, 1)], "r", size, sig=(relay, None), rows=128)
-            add("H", ([([x], [x])], "all", "loc", 0), [reg(relay, 0, 1)], [done], "h", size * (NR - 1), sig=sig)
-            ops[-1]["first"] = not any(p["kind"] == "h" for p in ops[:-1])
-            return
-        add("G", ([([x], [x])], "all", "loc", 0), [x], [done], "r", size * (NR - 1), sig=sig, rows=128 * (NR - 1))
+    def write(q, src, dst, to, rd, wr, sem):
+        kind = "h" if q == "H" else "r"
+        add(q, ([([src], [dst])], to, "loc", 0), rd, wr, kind, 2 * cnt(src), sig=(sem, None),
+            rows=128 * sum(WAYS[to][:2]) if q == "G" else 0)
+        ops[-1]["first"] = not any(p["kind"] == kind for p in ops[:-1])
 
-    own0, par0 = V * rank, V * par
+    def send(r, who, c0, c1, route, via):
+        x, y = [reg("tab%d" % r, V * ring[seat ^ who ^ m] + c0, V * ring[seat ^ who ^ m] + c1) for m in (0, 2)]
+        head = r > 0 and c0 == 0
+        nsend[0] += 4
+        done = [reg("far%d" % r, j + (0 if head else nsend[0]), j + 1 + (0 if head else nsend[0])) for j in range(3)]
+        sem, mid = ("head%d" if head else "arr%d") % r, reg(via, 0, 1)
+        if route == "d":
+            write("G", x, x, "all", [x], [done[0]], sem)
+        elif route == "a":
+            write("G", x, x, "aide", [x], [mid], via)
+            write("H", x, x, "all", [mid], [done[0]], sem)
+        elif route == "f":
+            write("G", x, x, "faraide", [x], [mid], via)
+            write("G", x, x, "par", [x], [done[0]], sem)
+            write("H", y, y, "pair", [mid], [done[1]], sem)
+        else:
+            write("G", x, x, "mir", [x], [mid, done[2]], via)
+            write("G", x, x, "par", [x], [done[0]], sem)
+            write("G", y, y, "par", [mid], [done[1]], sem)
+
+    seat = ring.index(rank)
+    own0, par0 = V * rank, V * ring[seat ^ 1]
     plan = cfg["plan"]
     ca = cfg["c0a"]
 
@@ -263,50 +289,67 @@ def build(rank, par, cfg):
         if cfg["pin"]:
             ops[-1]["pin"] = len(ops)
     memset(reg("ones", 0, 256), 1.0)
-    add("G", lambda g, T: g.affine_select(T.J[:], T.ones[:, 0:160], [[-1, 160]], ALU.is_equal, 0.0, 16, 1),
-        [reg("ones", 0, 160)], [reg("J", 0, 160)], "g", 160)
-    add("G", lambda g, T: g.affine_select(T.tri0[:], T.ones[:, 0:128], [[1, 128]], ALU.is_ge, 0.0, 0, -1),
-        [full("ones")], [full("tri0")], "g", 128)
-    add("G", lambda g, T: g.affine_select(T.tri[:], T.tri0[:], [[-16, 8], [0, 16]], ALU.is_ge, 0.0, 0, 1),
-        [full("tri0")], [full("tri")], "g", 128)
-    add("G", lambda g, T: g.iota(T.pcol[:, 0:1], [[0, 1]], 0, 1), [], [reg("pcol", 0, 1)], "g", 1)
-    add("G", lambda g, T: g.affine_select(T.sh[:], T.tri[:], [[1, 128]], ALU.is_equal, 0.0, -1, -1),
-        [full("tri")], [full("sh")], "g", 128)
-    send(0, own0, own0 + ca)
-    ops[-1]["first"] = True
-    ops[-1]["rd"] += [full("tri"), full("J"), reg("pcol", 0, 1)]
-    send(0, own0 + ca, own0 + V)
+    add("G", lambda g, T: g.iota(T.pcol[:, 0:4], [[16, 2], [1, 2]], 0, 1), [], [reg("pcol", 0, 4)], "g", 4)
+    if cfg.get("oldpro"):
+        add("G", None, [], [reg("pcol", 4, 5)], "g", 820)
+        ops[-1]["pin"] = 0
+    mark = len(ops)
+    for j, (a, b, route) in enumerate(cfg["first"]):
+        send(0, 0, a, b, route, "via%d" % j)
+    ops[mark]["rd"].append(reg("pcol", 0, 5 if cfg.get("oldpro") else 4))
+    rest = sorted(ops[mark + 1:], key=lambda o: (WAYS[o["fn"][1]][1] == 0) + (o["rd"][0][0][:3] == "via"))
+    ops[mark + 1:] = rest
+    for j, o in enumerate(ops[mark:]):
+        o["pin"] = mark + j
     for a in (0, 256):
         add("V", lambda g, T, a=a: g.vector.tensor_tensor_scan(T.lo[:, a:a + 256], T.ones[:], T.ones[:], -1.0, ALU.mult,
                                                                ALU.add), [reg("ones", 0, 256)], [reg("lo", a, a + 256)],
             "v", 128)
     load("S", "thi", "th", 0, V, 0, "ths", 4, extra=[reg(*cfg["thwait"])])
     eye = reg("J", 16, 144)
-    tscal(full("ntri16"), full("tri"), -1.0, None, ALU.mult, half=True)
+
+    def col(j):
+        return reg("kcol", j, j + 1)
+
+    vcopy(reg("kcol", 0, 4), reg("pcol", 0, 4))
+    for j, bits in enumerate((112, 15, 16)):
+        tscal(reg("pand", j, j + 1), reg("pcol", 0, 1), bits, None, ALU.bitwise_and)
+    tscal(reg("J", 0, 160), reg("lo", 0, 160), col(2), None, ALU.is_equal, half=True)
+    tscal(col(4), reg("pand", 0, 1), 15.0, None, ALU.add)
+    tscal(full("tri0"), full("lo"), col(0), col(4), ALU.max, ALU.min, half=True)
+    tt(full("tri16"), full("tri0"), full("lo"), ALU.is_equal, 2)
+    tscal(col(5), reg("pand", 1, 2), 15.0, None, ALU.is_lt)
+    tscal(full("sh"), full("lo"), col(1), col(5), ALU.is_equal, ALU.mult, half=True)
+    tscal(col(6), reg("pand", 2, 3), 8.0, None, ALU.is_lt)
+    tscal(col(7), reg("pand", 2, 3), 8.0, None, ALU.is_gt)
     tscal(full("I16"), eye, 1.0, None, ALU.mult, half=True)
     first_const = len(ops)
 
     onv = cfg["const"] == "V"
 
     def fill(o, c):
-        if onv:
+        if onv or o[0] in cfg["onv"]:
             return memset(o, c)
         act(o, reg("ones", 0, cnt(o)), AF.Copy, scale=c)
 
-    for name, c in (("nI", -1.0), ("nBI", -4 * BIG), ("I256", 256.0), ("nI256", -256.0), ("n2I", -2.0), ("I2", 2.0),
+    for name, c in (("BI", OWN), ("nTW", -float(TW)), ("nI", -1.0), ("nI256", -256.0), ("n2I", -2.0), ("I2", 2.0), ("nY", -0.375),
                     ("I3", 3.0)):
-        if onv:
+        if onv or name in cfg["onv"]:
             tscal(full(name), eye, c, None, ALU.mult, half=True)
         else:
             act(full(name), eye, AF.Copy, scale=c)
-    for a in range(0, 1024, 1024 if onv else 256):
-        fill(reg("rst", a, a + (1024 if onv else 256)), 1.0)
+    wide = 1024 if onv or "rst" in cfg["onv"] else 256
+    for a in range(0, 1024, wide):
+        fill(reg("rst", a, a + wide), 1.0)
     fill(reg("rst", 0, 1024, 8), 0.0)
+    for j in range(len(cfg["short"])):
+        fill(reg("now", 272 * j, 272 * j + 16), 0.0)
+        fill(reg("back", 272 * j + 16, 272 * j + 272), 0.0)
     fill(full("K258"), 258.0)
     fill(reg("hv", 0, 8), 0.5)
     fill(reg("r16", 0, 256), -1024.0)
     fill(reg("r16", 0, 256, 16), 0.5)
-    fill(full("Khalf"), 2.0 ** -8)
+    act(full("Klift"), eye, AF.Identity, bias=2.0, scale=0.5)
     for a in range(0, 128 * len(sets), 256):
         fill(reg("wb", a, a + 256), 0.0)
     for si, st in enumerate(sets):
@@ -320,11 +363,8 @@ def build(rank, par, cfg):
         mm(dm, full("nI"), full("sh"), False, True)
         act(full("Dm"), dm, AF.Copy)
     last_const = len(ops)
-    tscal(reg("pand", 1, 2), reg("pcol", 0, 1), 16, None, ALU.bitwise_and)
-    tscal(reg("kcol", 1, 2), reg("pand", 1, 2), 8.0, None, ALU.is_lt)
-    tscal(reg("kcol", 2, 3), reg("pand", 1, 2), 8.0, None, ALU.is_gt)
     for j in range(2):
-        tscal(reg("J%d" % j, 0, 160), reg("J", 0, 160), reg("kcol", 1 + j, 2 + j), None, ALU.mult, half=True)
+        tscal(reg("J%d" % j, 0, 160), reg("J", 0, 160), col(6 + j), None, ALU.mult, half=True)
     vcopy(reg("rf16", 0, 64), reg("rfi", 0, 64))
 
     def flip(src, r, v0, v1):
@@ -364,32 +404,47 @@ def build(rank, par, cfg):
     less = [bank("f"), bank("f")]
     for h in range(2):
         a = 512 * h
-        vcopy(reg("cpb", a, a + 512), reg("cpi", a, a + 512))
-        mm(reg(less[h], 0, 512), eye, reg("cpb", a, a + 512), True, False)
-        for j in (0, 256):
-            mm(reg(less[h], j, j + 256), full("nI"), reg("ones", 0, 256), False, j == 256)
-    for h, (a, b) in enumerate(cfg["gaps"]):
-        n = b - a
-        z1, z2 = reg(bank(), 0, n), reg(bank(), 0, n)
-        tt(reg("nog", a, b), reg("gpi", a, b), reg(less[a // 512], a % 512, a % 512 + n), ALU.mult)
-        mm(z2, eye, reg("lo", 0, n), True, False)
-        mm(z2, full("nBI"), reg("cpb", a, b), False, False)
-        mm(z2, full("ntri16"), reg("nog", a, b), False, True)
-        mm(z1, eye, reg("lo", 0, n), True, False)
-        mm(z1, full("ntri16"), reg("nog", a, b), False, True)
-        for j in range(0, n, 256):
-            act(reg("Gw", a + j, a + j + 256), reg(z1[0], j, j + 256), AF.Identity, bias=float(own0 + a + j))
-        for j in range(0, n, 256):
-            if cfg["hw"] == "V":
-                tscal(reg("Hw", a + j, a + j + 256), reg(z2[0], j, j + 256), float(own0 + a + j) + BIG, 0.0, ALU.add, ALU.max)
+        tscal(reg("own", a, a + 512), reg("cpi", a, a + 512), -1.0, 1.0, ALU.mult, ALU.add)
+        if cfg["less"]:
+            mm(reg(less[h], 0, 512), eye, reg("own", a, a + 512), True, True)
+            if cfg.get("oldpro"):
+                mm(reg(less[h], 0, 512), eye, reg("own", a, a + 512), True, True)
+    floors = cfg["mod"] == "A"
+    base = own0 + (QOFF * TW - TW / 2 if floors else 0.0)
+    for a, b in cfg["sums"]:
+        z1, z2 = bank(), bank()
+        parts = [(max(a, x), min(b, y)) for x, y in cfg["gaps"] if x < b and a < y]
+        for z in (z1, z2):
+            mm(reg(z, 0, b - a), eye, reg("lo", a % 256, a % 256 + b - a), True, False,
+               [reg("gpi", a, b)] if cfg.get("oldpro") else [])
+        mm(reg(z2, 0, b - a), full("BI"), reg("own", a, b), False, False)
+        for x, y in parts:
+            if cfg["less"]:
+                tt(reg("nog", x, y), reg("gpi", x, y), reg(less[x // 512], x % 512, x % 512 + y - x), ALU.mult)
             else:
-                act(reg("Hw", a + j, a + j + 256), reg(z2[0], j, j + 256), AF.Relu, bias=float(own0 + a + j) + BIG)
-        for j in range(0, n, 256):
-            act(reg("Y2", a + j, a + j + 256), reg(z2[0], j, j + 256), AF.Relu, bias=float(own0 + a + j) + 2 * BIG)
-    hop("S1", "Gw", "Hw", 0, V, ALU.max, [512])
+                tt(reg("nog", x, y), reg("gpi", x, y), reg("own", x, y), ALU.mult, 2)
+            for z in (z1, z2):
+                mm(reg(z, x - a, y - a), full("tri16"), reg("nog", x, y), False, y == b)
+        at = [a] + [v for v in range(0, V, 256) if a < v < b] + [b]
+        for name, z, func, lift in (("Gw", z1, AF.Identity, 0.0), ("Hw", z2, AF.Relu, BIG - OWN), ("Y2", z2, AF.Relu, 2 * BIG - OWN)):
+            for x, y in zip(at, at[1:]):
+                if name == "Hw" and cfg["hw"] == "V":
+                    tscal(reg(name, x, y), reg(z, x - a, y - a), base + x // 256 * 256 + lift, 0.0, ALU.add, ALU.max)
+                else:
+                    act(reg(name, x, y), reg(z, x - a, y - a), func, bias=base + x // 256 * 256 + lift)
+    hop("S1", "Gw", "Hw", 0, V, ALU.max, cfg["hop0"])
     for v0, v1, how in cfg["dec"][0]:
-        at = [v0] + [v for v in cfg["hop2"] if v0 < v < v1] + [v1]
+        at = [v0] + [v for v in cfg["cut0"] if v0 < v < v1] + [v1]
         for a, b in zip(at, at[1:]):
+            if floors:
+                hop("S2", "S1", "Y2", a, b, ALU.max)
+                act(reg("qr", a, b), reg("S2", a, b), AF.Identity, bias=QOFF - 0.5 + 0.5 / TW - (base - own0) / TW,
+                    scale=1.0 / TW)
+                x = reg(bank(), 0, b - a)
+                mm(x, full("nTW"), reg("qr", a, b), True, True)
+                tt(reg("S16", a, b), reg("S2", a, b), x, ALU.add)
+                ops[-1]["boost"] = 9
+                continue
             hop("s2i", "S1", "Y2", a, b, ALU.max)
             tscal(reg("s2m", a, b), reg("s2i", a, b), TW - 1, None, ALU.bitwise_and)
             if how != "n":
@@ -397,6 +452,8 @@ def build(rank, par, cfg):
                 ops[-1]["boost"] = 9
         if how != "n":
             turn("S16", 0, v0, v1, how)
+        elif floors:
+            tscal(reg("L", v0, v1), reg("S16", v0, v1), TW / 2, None, ALU.add, half=True)
         else:
             vcopy(reg("L", v0, v1), reg("s2m", v0, v1))
             tscal(reg("S16", v0, v1), reg("L", v0, v1), -TW / 2, None, ALU.add, half=True)
@@ -411,12 +468,9 @@ def build(rank, par, cfg):
                 else:
                     lift.append([c, c + 32])
         nb = bank("f")
-        mm(reg(nb, 0, 512), full("I256"), reg("cpb", a, b), True, False, [reg("S1", 0, V)], boost=0)
+        mm(reg(nb, 0, 512), full("nI256"), reg("own", a, b), True, False, [reg("S1", 0, V)], boost=0)
         for j in (0, 256):
-            mm(reg(nb, j, j + 256), full("Khalf"), reg("ones", 0, 256), False, j > 0 and not lift, boost=0)
-        if any(cfg["yv"]):
-            tscal(reg("own4", a, b), reg("cpb", a, b), -4.0, 4.0, ALU.mult, ALU.add, half=True)
-            ops[-1]["boost"] = 1
+            mm(reg(nb, j, j + 256), full("Klift"), reg("ones", 0, 256), False, j > 0 and not lift, boost=0)
         for c, d in lift:
             si = sets.index(signset(0, c))
             mm(reg(nb, c - a, d - a), reg("wb", 128 * si, 128 * si + 128), reg("ones", 0, d - c), False,
@@ -437,7 +491,7 @@ def build(rank, par, cfg):
                 mcol[c[0]] = at
                 at += 16 * (c[1] - c[0])
         if r > 0:
-            gcopy(reg(tab, TW, TW + 16), reg(tab, 0, 16), [reg("far%d" % r, 0, 1)])
+            gcopy(reg(tab, TW, TW + 16), reg(tab, 0, 16), [reg("far%d" % r, 0, 4)])
             def step(o, win, v0, v1, stops):
                 runs = []
                 for a, b in sorted(cfg["cnt"][r - 1]):
@@ -452,6 +506,12 @@ def build(rank, par, cfg):
 
             step("h1", "any%d" % (r - 1), 0, V, cfg["hop1"])
             for v0, v1, how in cfg["dec"][r]:
+                if v0 in cfg["quick"]:
+                    hop("Gw", "h1", "Hw", v0, v1, ALU.add)
+                    tscal(reg("L", v0, v1), reg("Gw", v0, v1), 0.25, None, ALU.mult)
+                    if not last:
+                        tscal(reg("S16", v0, v1), reg("L", v0, v1), -TW / 2, None, ALU.add, half=True)
+                    continue
                 step("h2%d" % r, "h1", v0, v1, cfg["hop2"])
                 if how != "n":
                     turn("h2%d" % r, r, v0, v1, how)
@@ -467,7 +527,8 @@ def build(rank, par, cfg):
         def repeat(v0, v1, per):
             n = v1 - v0
             for j in range(copies.get(v0, 0), per):
-                gcopy(reg("cw", 4 * v0 + j * n, 4 * v0 + (j + 1) * n), reg(tab, own0 + v0, own0 + v1), far)
+                gcopy(reg("cw", 4 * v0 + j * n, 4 * v0 + (j + 1) * n), reg(tab, own0 + v0, own0 + v1),
+                      far if r or cfg.get("oldpro") else [])
             copies[v0] = max(per, copies.get(v0, 0))
             return reg("cw", 4 * v0, 4 * v0 + per * n)
 
@@ -477,9 +538,11 @@ def build(rank, par, cfg):
             if chunks[j][2] == "n":
                 if blk:
                     return
+                m = n // len(chunks[j][3])
+                for a in range(v0, v1, m):
+                    gather(chunks[j][3][(a - v0) // m], reg("P", 16 * a, 16 * (a + m)), win, reg("L", a, a + m), far)
                 for a in range(v0, v1, 64):
                     pr = reg("P", 16 * a, 16 * a + 1024)
-                    gather(chunks[j][3][(a - v0) // 64], pr, win, reg("L", a, a + 64), far)
                     mo = reg("M", mcol[v0] + 16 * (a - v0), mcol[v0] + 16 * (a - v0) + 1024)
                     add("V", lambda g, T, pr=pr, mo=mo: g.vector.tensor_tensor_scan(
                         ap(T, mo), T.rst[:], ap(T, pr), 0.0, ALU.mult, ALU.max), [pr, reg("rst", 0, 1024)], [mo], "v", 512)
@@ -610,11 +673,11 @@ def build(rank, par, cfg):
                 mm(x2, full("nI256"), reg("qr", c0, c1), False, True)
                 act(reg(nxt, d0, d0 + n), x2, AF.Identity, bias=QOFF * 256)
             if not last:
-                send(r + 1, d0, d0 + n, "via%d_%d" % (r, j) if c0 in cfg["relay"][r] else None)
+                send(r + 1, int(folded), c0, c1, cfg["route"][r][j], "via%d_%d" % (r, j))
                 return
             if folded:
                 src, dst = reg("ypt", c0, c1), reg("ycb", c0, c1)
-                add("G", ([([src], [dst])], "par", "loc", 0), [src], [dst], "r", 2 * n, sig=("yb%d" % j, None), rows=128)
+                write("G", src, dst, "par", [src], [dst], "yb%d" % j)
             store("yc", "ycb", c0, c1, 2)
 
         def counts(c0, c1):
@@ -654,20 +717,43 @@ def build(rank, par, cfg):
                 act(x, F, AF.Copy)
             add("V", lambda g, T: g.vector.tensor_tensor_scan(ap(T, run), T.r16[:, 0:m], ap(T, x), 0.5, ALU.max, ALU.min),
                 [x, reg("r16", 0, 256)], [run], "v", m if x == F else m / 2)
+            if last and c0 in cfg["short"]:
+                a = 272 * cfg["short"].index(c0) + 16
+                tscal(reg("now", a, a + m), run, 0.0, None, ALU.is_lt, half=True)
+                tscal(reg("back", a + 16, a + m, 16), reg("run", 2 * c0 + 15, 2 * c0 + m - 16, 16), 0.0, None, ALU.is_lt,
+                      half=True)
+                Cc = reg(bank(), 0, n)
+                for j in range(RO - 1):
+                    mm(Cc, full("Dm"), reg("any%d" % j, c0, c1), j == 0, False, [ks[-1][1]])
+                for j, v in at:
+                    s, b = 0 if j == 0 else 256 - n, a + 128 * j
+                    plus, minus = reg("J", 16 + s, 144), reg("nI", s, 128)
+                    for x, w in ((reg("now", b, b + 128), plus), (reg("now", b - 1, b + 127), minus),
+                                 (reg("back", b, b + 128), plus)):
+                        mm(reg(Cc[0], v - c0 + s, v - c0 + 128), x, w, False, j == len(at) - 1 and x[0] == "back")
+                tt(reg("ygb", c0, c1), Cc, reg("gpi", c0, c1), ALU.add)
+                store("yg", "ygb", c0, c1, 4)
+                return
             for j, v in at:
-                mm(reg(fb, v - c0, v - c0 + 128), reg("run", 2 * c0 + 128 * j, 2 * c0 + 128 * j + 128), eye, True, True)
-            act(reg("any%d" % r, c0, c1), reg(fb, 0, n), AF.Sign, bias=0.5, scale=-1.0)
+                mm(reg(fb, v - c0, v - c0 + 128), reg("run", 2 * c0 + 128 * j, 2 * c0 + 128 * j + 128), full("I2"), True,
+                   True)
+            act(reg("any%d" % r, c0, c1), reg(fb, 0, n), AF.Sign, bias=1.0, scale=-1.0)
             if last:
                 for j in range(RO):
                     mm(Cc, full("Dm"), reg("any%d" % j, c0, c1), j == 0, j == RO - 1)
                 tt(reg("ygb", c0, c1), Cc, reg("gpi", c0, c1), ALU.add)
                 store("yg", "ygb", c0, c1, 4)
             elif c0 in cfg["yv"][r]:
-                tt(reg("Y", c0, c1), reg(fb, 0, n), reg("own4", c0, c1), ALU.mult)
+                tt(reg("Y", c0, c1), reg(fb, 0, n), reg("own", c0, c1), ALU.mult)
             else:
-                mm(Cc, full("nI"), reg("cpb", c0, c1), True, False)
+                mm(Cc, eye, reg("own", c0, c1), True, False)
                 mm(Cc, full("n2I"), reg("any%d" % r, c0, c1), False, True)
-                act(reg("Y", c0, c1), Cc, AF.Abs, bias=2.0)
+                act(reg("Y", c0, c1), Cc, AF.Abs, bias=1.0)
+                if c0 in cfg["quick"]:
+                    z = reg(bank(), 0, n)
+                    mm(z, full("nY"), reg("Y", c0, c1), True, False)
+                    mm(z, full("I16"), reg("S16", c0, c1), False, True)
+                    act(reg("Hw", c0, c1), z, AF.Identity, bias=2.0 * TW + 3.0, scale=4.0)
 
         steps = {"g": unit, "c": compare, "o": fold, "f": lambda j: counts(*cfg["cnt"][r][j]), "r": registers}
         for word in cfg["seq"][r].split():
@@ -725,16 +811,19 @@ def cost(o, e):
         return e["op"] + n * e["pe"], 0, 0
     if k == "g":
         return 170 + 2 * n * e["cyc"], 0, 0
-    if k == "h":
-        return (e["riss"] + e["rfix"] + (e["rfirst"] if o["first"] else 0) + 8 * (NR - 1) * e["drow"]
-                + 8 * n / e["dbw"] * e["sx"]), 0, 0
-    move = (o["rows"] / 16 * e["drow"] * (e["frow"] if k == "f" else 1)
-            + 8 * n / e["dbw"] * {"f": e["fb"], "x": e["xb"], "r": e["sx"] if o["rows"] > 128 else 1}.get(k, 1))
+    if k in "rh":
+        near, far = WAYS[o["fn"][1]][:2]
+        move = 8 * (near + far) * e["drow"] + 8 * n / e["dbw"] * (near + far * (3 * e["sx"] - 1) / 2)
+        if k == "h":
+            return e["riss"] + e["rfix"] + (e["rfirst"] if o["first"] else 0) + move, 0, 0
+    else:
+        move = (o["rows"] / 16 * e["drow"] * (e["frow"] if k == "f" else 1)
+                + 8 * n / e["dbw"] * {"f": e["fb"], "x": e["xb"]}.get(k, 1))
     if k == "d":
         return 60, move, e["dfix"]
     if k == "x":
         return e["xiss"] + (e["rfirst"] if o["first"] else 0), move, e["dfix"]
-    return e["riss"] + (e["rfirst"] if o["first"] else 0), move, e["rfix"] + (e["fx"] if k == "f" else 0)
+    return e["riss"] + e["rw"] * (o["rows"] / 128 if k == "r" else 1) + (e["rfirst"] if o["first"] else 0), move, e["rfix"] + (e["fx"] if k == "f" else 0)
 
 
 def schedule(ops, e, cfg):
@@ -827,6 +916,11 @@ def justify(ops, e, start, rounds=2):
             key.append(start[i])
     for i, o in enumerate(ops):
         pre[i] = [(out[j], e["sem"] if w else 0.0) for j, w in o["pre"].items()]
+    for q in "GS":
+        pinned = [i for i, o in enumerate(ops) if "pin" in o and o["q"] == q]
+        for j, i in zip(pinned, pinned[1:]):
+            pre[i].append((j, 0.0))
+            pre[out[i]].append((out[j], 0.0))
     m = len(res)
     suc = [[] for _ in range(m)]
     for i in range(m):
@@ -879,18 +973,20 @@ def rank_program(g, core, T, topo):
     by_die = sorted(range(NR), key=lambda q: (topo.die(T.cores[q]), q))
     spare = sorted((c for c in topo.cores_of(T.cores[0]) if c not in T.cores), key=lambda c: (topo.die(c), c))
     rank = T.rank_of(core)
-    if rank is None and not (core in spare and any(CFG["relay"])):
+    if rank is None and core not in spare:
         return
     aide = rank is None
     if aide:
         rank = by_die[spare.index(core)]
-    par = by_die[by_die.index(rank) ^ 1]
+    at = by_die.index(rank)
+    par = by_die[at ^ 1]
     if not ORDER:
-        ORDER.extend(schedule(link(build(0, 1, CFG)), EST, CFG))
+        ORDER.extend(schedule(link(build(by_die[0], by_die, CFG)), EST, CFG))
         BANK.update(ORDER[1])
     order = ORDER[0]
-    ops = hand_over(link(build(rank, par, CFG)), ORDER[2])
-    dests = {"all": [c for c in T.cores if c != T.cores[rank]], "par": [T.cores[par]], "aide": [spare[by_die.index(rank)]]}
+    ops = hand_over(link(build(rank, by_die, CFG)), ORDER[2])
+    dests = {"all": [c for c in T.cores if c != T.cores[rank]], "par": [T.cores[par]], "aide": [spare[at]],
+             "mir": [T.cores[by_die[at ^ 2]]], "faraide": [spare[at ^ 2]], "pair": [T.cores[rank], T.cores[par]]}
     engines = [e for e in topo.engines(core, T.cores[par]) if all(e in topo.engines(core, c) for c in dests["all"])]
     neng = len(engines)
 
@@ -908,13 +1004,13 @@ def rank_program(g, core, T, topo):
             for j in ops[i]["pre"]:
                 g.wait_ge(T.sem[ops[j]["sig"][0]], neng)
             remote(ops[i], engines)
-        g.wait_ge(T.sem["loc"], neng * len(order["H"]))
+        if order["H"]:
+            g.wait_ge(T.sem["loc"], neng * len(order["H"]))
         return
     total = {s: 0 for s in SEMAPHORES}
-    total["arr0"] = 2 * (NR - 1) * neng
-    for r in range(1, RO):
-        total["arr%d" % r] = (len(CFG["reg"][r - 1]) - 1) * (NR - 1) * neng
-        total["head%d" % r] = (NR - 1) * neng
+    for o in ops:
+        if o["kind"] in "rfh":
+            total[o["sig"][0]] += WAYS[o["fn"][1]][2] * neng
     for q in "VAPGS":
         k = 0
         for i in order[q]:
@@ -924,11 +1020,9 @@ def rank_program(g, core, T, topo):
                 o["sig"] = (ENGSEM[q], k)
                 total[ENGSEM[q]] = k
             elif o["kind"] in "rf":
-                o["eng"] = engines[:CFG["foldeng"]] if o["kind"] == "f" else engines
-                if o["fn"][1] == "par":
-                    total[o["sig"][0]] = len(o["eng"])
+                o["eng"] = engines
                 o["sig"] = (o["sig"][0], total[o["sig"][0]])
-                total[o["fn"][2]] += len(o["eng"])
+                total[o["fn"][2]] += neng
             else:
                 total[o["sig"][0]] += 16
     for o in ops:

from concourse.bass import DstId, RemoteDMATransfer
from concourse.mybir import AluOpType as ALU, ActivationFunctionType as AF

V = 1024
NR = 4
RO = 3
TW = NR * V
BIG = 65536.0
OWN = 16 * BIG
QOFF = 129.0

QUARTERS = [(0, 256), (256, 512), (512, 768), (768, 1024)]
CFG = {
    "plan": [[(0, 256, "A8", "V0"), (256, 512, "A8", "V0"), (512, 768, "A4", "V0"), (768, 1024, "A0", "V0")]] * 3,
    "dec": [[(0, 1024, "01")]] * 3,
    "hop1": [768],
    "hop2": [512],
    "cnt": [QUARTERS[:3] + [(768, 896), (896, 1024)]] * 3,
    "reg": [QUARTERS] * 3,
    "links": {"A": 4, "V": 2, "D": 4},
    "call": {"A": 1024, "V": 512, "D": 1024},
    "banks": {"t": "01", "f": "765", "g": "43210"},
    "passes": 4,
    "topen": ("h1", 0, 16),
    "fopen": 0,
    "thwait": ("far0", 0, 999),
    "nthwait": ("L256", 0, 1024),
    "seq": ["g00 g01 o00 o01 g10 g11 o10 o11 r0 g20 g21 o20 o21 r1 g30 g31 o30 o31 c00 c01 f0 r2 c10 c11 f1 r3 c20 c21 f2 "
            "c30 c31 f3 f4"] * 3,
    "c0a": 128,
    "loads": ["c0a", "c0b", "cp0", "gp0", "cp1", "rfs", "gp1", "gp2"],
    "gaps": [(0, 512), (512, 768), (768, 1024)],
    "hw": "V",
    "late": [],
    "delta": 0.0,
    "boost": {"VP": 5, "VM": 5, "VCM": 5, "VST": 2, "VS16": 8, "Vnth": 6, "AP": 5, "F": 5},
}
CFG.update({
    "plan": [[(0, 128, 'n', 'AA', 4), (128, 384, 'A8', 'V0'), (384, 640, 'A8', 'V0'), (640, 896, 'V4', 'V0'), (896, 1024, 'n', 'AA', 0)]] * 3,
    "sign": [[128, 640], [896], [640, 896]],
    "seq": ['g21 g10 g11 g30 c10 o10 g00 c00 g20 o30 g31 c20 o31 g40 o21 r0 o11 r4 o20 r3 c11 c31 f0 r1 c30 c21 f1 c40 r2 f2 f4 f3',
            'g21 g10 g11 g30 c10 o10 g00 g20 c00 o30 g31 c20 o20 o31 g40 c31 r0 o21 o11 c11 r4 f1 r3 r1 c30 c21 c40 f3 f2 f0 f4 r2',
            'g21 g11 g30 g10 c10 g00 o30 g20 c00 g31 c20 o20 o31 o10 r0 o21 g40 o11 c11 r3 r1 c31 r4 f0 c30 c21 c40 f1 f3 f2 f4 r2'],
    "dec": [[(0, 128, 'n'), (128, 896, '01'), (896, 1024, 'n')]] * 3,
    "boost": {'VP': 5, 'VM': 5, 'VCM': 4, 'VS16': 5, 'Vnth': 9, 'AP': 5, 'F': 4, 'Vrun': 6, 'ACM': 5, 'AY': 6, 'Aqr': 9, 'Gcw': 5},
    "banks": {'t': '01', 'f': '765', 'g': '4321076'},
    "fopen": 4, "hop1": [384, 512], "hop2": [], "hw": "A", "passes": 1,
    "cnt": [[(0, 128), (128, 384), (384, 640), (640, 896), (896, 1024)]] * 3,
    "reg": [[(0, 128), (128, 384), (384, 640), (640, 896), (896, 1024)]] * 3,
    "foldeng": 16, "regv": [[], [], []], "yv": [[], [], []], "signcall": 512, "onv": [], "quick": [], "short": [], "route": ["aaddd", "aaddd"], "first": [(0, 128, "d"), (128, 1024, "d")], "less": True, "mod": "A", "cwfar": False, "sums": [(0, 512), (512, 1024)], "hop0": [512], "cut0": [512], "via0": False, "pin": True, "const": "A", "relay": [[], [], []],
})
EST = {"cyc": 0.9, "g": 1.56, "ov": 30.0, "oa": 30.0, "pe": 0.5, "op": 5.0, "sem": 90.0,
       "dfix": 1800.0, "drow": 14.0, "dbw": 24.0, "rfix": 2000.0, "riss": 600.0, "rfirst": 2000.0,
       "frow": 6.0, "fb": 0.9, "fx": 500.0, "xiss": 1000.0, "xb": 2.0, "sx": 1.0, "ra": 1.0, "rw": 0.0}
EST.update(dict(cyc=.9, pe=.62, op=4, ov=13, oa=38, g=1.56, frow=6, fb=1.0, riss=420, rfix=1450, sem=55, dbw=27, drow=10,
                sx=1.8, dfix=1300, rfirst=1800, fx=250))
NOW = {'plan': [(0, 128, 'n', 'AA', 3), (128, 384, 'A8', 'V0'), (384, 640, 'A4', 'V0'), (640, 896, 'A0', 'V2'), (896, 1024, 'n', 'AA', 0)], 'seq': 'g00 g10 g21 g11 c10 o10 o11 r0 g20 c00 r1 o20 o21 g30 c20 g31 g40 r4 o31 c30 c31 f0 o30 r3 c11 c21 c40 f2 f4 f3 r2 f1', 'dec': [(0, 128, 'n'), (128, 896, '01'), (896, 1024, 'n')], 'boost': {'VP': 5, 'VM': 5, 'VCM': 5, 'VS16': 8, 'Vnth': 6, 'AP': 5, 'F': 9, 'ACM': 5, 'Gcw': 6, 'VY': 4, 'D': 9, 'Vrun': 6}, 'delta': 0.0, 'banks': {'t': '01', 'f': '765', 'g': '4321076'}, 'fopen': 0, 'hop1': [256], 'hop2': [320], 'sign': [[640], [640], [640]], 'regv': [[0, 384, 640, 896], [0, 384, 640, 896], [0, 384, 640, 896]], 'yv': [[], [], []], 'links': {'A': 4, 'V': 2, 'D': 4}, 'call': {'A': 1024, 'V': 512, 'D': 1024}, 'hw': 'V'}
EST.update(dict(cyc=.95, pe=.62, op=2, ov=12, oa=42, g=1.4, frow=6.3, fb=1.05, riss=400, rfix=1100, sem=140, dbw=26, drow=10, sx=1.8, dfix=1400, rfirst=2000, fx=600))
NOW = {'plan': [[(0, 128, 'n', 'AA', 3), (128, 384, 'A8', 'V4'), (384, 640, 'A4', 'V0'), (640, 896, 'A0', 'V2'), (896, 1024, 'n', 'AA', 0)], [(0, 128, 'n', 'AA', 3), (128, 384, 'A8', 'V0'), (384, 640, 'A4', 'V0'), (640, 896, 'A0', 'V4'), (896, 1024, 'n', 'AA', 0)], [(0, 128, 'n', 'AA', 3), (128, 384, 'A8', 'V0'), (384, 640, 'A4', 'V0'), (640, 896, 'A0', 'V4'), (896, 1024, 'n', 'AA', 0)]], 'seq': ['g21 g10 c10 g11 g20 g00 r0 o11 o20 o10 c00 r1 g30 f0 o30 c20 g40 o21 r4 g31 c11 c40 c30 f1 r2 f4 o31 c31 c21 r3 f3 f2', 'g00 g10 g21 g11 o10 g20 r0 c00 o21 c10 o11 g30 c21 g40 o30 f0 g31 o20 r1 r4 c20 o31 c31 c11 r3 c40 r2 c30 f3 f2 f1 f4', 'g10 g21 o10 g00 c10 g20 g11 c00 o11 o20 r1 g30 c20 o30 f0 g40 o21 c30 g31 r4 c40 c11 r0 o31 c21 c31 r3 f3 f4 f2 f1 r2'], 'dec': [[(0, 128, 'n'), (128, 896, '10'), (896, 1024, 'n')], [(0, 128, 'n'), (128, 896, '01'), (896, 1024, 'n')], [(0, 128, 'n'), (128, 896, '01'), (896, 1024, 'n')]], 'boost': {'VP': 5, 'VM': 5, 'VCM': 5, 'VS16': 9, 'Vnth': 9, 'AP': 5, 'F': 9, 'ACM': 5, 'Gcw': 9, 'VY': 2, 'D': 9, 'Vrun': 6, 'Aqr': 9, 'AY': 6}, 'delta': 0.0, 'banks': {'t': '01', 'f': '765', 'g': '4321076'}, 'fopen': 4, 'hop1': [], 'hop2': [256], 'sign': [[128, 640], [640], [640]], 'regv': [[0, 384, 640], [384, 640], [0, 384, 640, 896]], 'yv': [[128, 384], [128, 384], []], 'hw': 'A', 'relay': [[0, 128], [0, 128], []]}
NOW.update(cut0=[512], mod="V", hw="V", sums=[(0, 512), (512, 768), (768, 1024)], loads=['c0a', 'c0b', 'cp0', 'cp1', 'gp0', 'gp1', 'gp2', 'rfs'],
           first=[(0, 512, "m"), (512, 1024, "m")], c0a=512, route=["aaddd", "aaddd"], less=True)
NOW.update({'plan': [(0, 128, 'n', 'AAAV', 3), (128, 384, 'A8', 'V0'), (384, 640, 'A2', 'V0'), (640, 896, 'A2', 'V4'), (896, 1024, 'n', 'AA', 0)], 'seq': ['g00 g21 g10 g11 c00 c10 o11 c11 g20 r0 o10 c21 o21 g30 o30 o20 g31 c20 f2 c31 f1 r1 c30 r2 g40 f0 c40 f4 f3 o31 r4 r3', 'g10 g21 g00 c00 g11 c10 o21 c11 o11 r0 g20 c21 g30 o20 o30 g31 o10 g40 c20 f2 r2 c31 f1 c30 r1 f0 c40 o31 f3 f4 r3 r4', 'g10 g21 g00 c00 g11 c10 o11 c11 c21 r0 g20 g30 o21 o20 o30 g31 o10 c20 r2 o31 f1 f2 r1 c31 f0 c30 g40 c40 f4 r4 r3 f3'], 'dec': [(0, 128, 'n'), (128, 896, '01'), (896, 1024, 'n')], 'boost': {'VP': 5, 'VM': 5, 'VCM': 5, 'VS16': 5, 'Vnth': 6, 'AP': 5, 'F': 9, 'ACM': 5, 'Gcw': 6, 'VY': 2, 'D': 9, 'Vrun': 6, 'Aqr': 9, 'AY': 9}, 'fopen': 4, 'hop1': [256, 640], 'hop2': [384], 'sign': [[384, 640], [], [640]], 'regv': [[384, 640, 896], [384, 640, 896], [0, 384, 640, 896]], 'yv': [[384], [], []], 'route': ['fafdd', 'aafdd'], 'links': {'A': 8, 'V': 4, 'D': 4}, 'call': {'A': 2048, 'V': 1024, 'D': 1024}, 'hw': 'V', 'loads': ['cp0', 'c0a', 'cp1', 'gp0', 'c0b', 'gp1', 'gp2', 'rfs'], 'mod': 'A', 'cut0': [320, 640], 'sums': [(0, 512), (512, 1024)], 'signcall': 512, 'quick': [0], 'short': []})
EST.update({'sem': 200, 'riss': 440.0, 'drow': 11.0, 'dbw': 23.4, 'fb': 0.84, 'rfix': 1089.0, 'rfirst': 1800.0})
NOW.update({'seq': ['g10 g00 g21 g11 c00 c10 c11 o11 g20 c21 r0 g30 g31 o20 c20 o30 o10 f2 c31 o21 g40 f1 r1 c30 r2 f0 c40 o31 f3 f4 r4 r3', 'g21 g10 g00 c00 g11 c10 o21 o11 r0 c11 g20 o20 g30 c21 g31 g40 c20 o10 f1 c31 r2 o30 c30 r1 c40 o31 f4 f2 f3 r3 r4 f0', 'g11 o11 g21 g00 g10 c00 c10 c11 g20 c21 r0 g30 o30 o20 o21 g31 o31 o10 c20 r2 r1 f1 f2 r3 c31 f0 g40 c40 c30 r4 f3 f4'], 'boost': {'VP': 5, 'VM': 5, 'VCM': 5, 'VS16': 6, 'Vnth': 5, 'AP': 5, 'F': 9, 'ACM': 5, 'Gcw': 2, 'VY': 2, 'D': 9, 'Vrun': 6, 'Aqr': 9, 'AY': 9}, 'hop2': [256], 'yv': [[], [], []], 'loads': ['cp0', 'cp1', 'c0a', 'gp0', 'gp1', 'gp2', 'rfs', 'c0b'], 'onv': ['I2', 'K258', 'r16']})
EST.update({'drow': 9.9, 'sx': 1.62, 'dfix': 1120.0})
for _k in ("plan", "dec", "seq", "cnt", "reg"):
    if _k in NOW and not isinstance(NOW[_k][0], list) and not (_k == "seq" and isinstance(NOW[_k], list)):
        NOW[_k] = [NOW[_k]] * 3
CFG.update(NOW)

SCRATCH = {}


def _decl(names, where, shape, dtype):
    for n in names.split():
        SCRATCH[n] = (where, shape, dtype)


_decl("cpi gpi thi s2i s2m", "sbuf", [128, V], "int32")
_decl("rfi", "sbuf", [128, 64], "int32")
_decl("pcol pand", "sbuf", [128, 8], "int32")
_decl("rf16", "sbuf", [128, 64], "uint16")
_decl("L", "sbuf", [128, V], "uint16")
_decl("tab0 tab1 tab2", "sbuf", [128, TW + 16], "bfloat16")
_decl("P CM", "sbuf", [128, 16 * V], "bfloat16")
_decl("M", "sbuf", [128, 4 * V], "bfloat16")
_decl("rst", "sbuf", [128, 1024], "bfloat16")
_decl("nog S16 h21 h22", "sbuf", [128, V], "float16")
_decl("ycb ypt own nth any0 any1 any2 Y h1 qr", "sbuf", [128, V], "bfloat16")
_decl("FM00 FM01 FM10 FM11 FM20 FM21", "sbuf", [128, V], "bfloat16")
_decl("ygb Gw Hw Y2 S1 S2", "sbuf", [128, V], "float32")
_decl("lo", "sbuf", [128, 512], "bfloat16")
_decl("now back", "sbuf", [128, 272 * 5], "bfloat16")
_decl("nI I2 I3 nY nTW nI256 n2I BI tri0 sh Dm K258 Klift", "sbuf", [128, 128], "bfloat16")
_decl("J", "sbuf", [128, 160], "bfloat16")
_decl("ones", "sbuf", [128, 256], "bfloat16")
_decl("J0 J1", "sbuf", [128, 160], "float16")
_decl("tri16 I16", "sbuf", [128, 128], "float16")
_decl("r16", "sbuf", [128, 256], "bfloat16")
_decl("hv", "sbuf", [128, 8], "bfloat16")
_decl("kcol", "sbuf", [128, 8], "float32")
_decl("wb", "sbuf", [128, 128, 16], "bfloat16")
_decl("B0 B1", "psum", [128, 32, 16], "float32")
_decl("B2 B3 B4 B5 B6 B7", "psum", [128, 512], "float32")
_decl("hT0 hT1 hT2", "sbuf", [128, 32, 32], "float16")
for _n in {c[1] - c[0] for p in CFG["plan"] for c in p if c[2] != "n"}:
    _decl("L%d" % _n, "sbuf", [128, V // _n + 1, _n], "uint16")
_decl("run sg", "sbuf", [128, 2 * V], "bfloat16")
_decl("cw", "sbuf", [128, 4 * V], "bfloat16")

SEMAPHORES = (["sV", "sA", "sP", "sG", "c0a", "c0b", "cp0", "cp1", "gp0", "gp1", "gp2", "rfs", "ths", "outs",
               "arr0", "arr1", "arr2", "head1", "head2", "loc", "fl0", "fl1", "fl2"]
              + ["f%d_%d%d" % (r, j, b) for r in range(RO) for j, c in enumerate(CFG["plan"][r]) for b in range(2)
                 if c[2] != "n"]
              + ["%s%d_%d%d" % (x, r, j, b) for r in range(RO) for j, c in enumerate(CFG["plan"][r]) for b in range(2)
                 for x in "wx" if c[2 + b][0] == "D"]
              + ["via%d_%d" % (r, j) for r in range(RO - 1) for j, c in enumerate(CFG["route"][r]) if c != "d"]
              + ["via%d" % j for j, c in enumerate(CFG["first"]) if c[2] != "d"]
              + ["yb%d" % j for j in range(len(CFG["reg"][-1]))])
ENGSEM = {"V": "sV", "A": "sA", "P": "sP", "G": "sG"}


WAYS = {"all": (1, 2, 3), "par": (1, 0, 1), "aide": (1, 0, 0), "mir": (0, 1, 1), "faraide": (0, 1, 0), "pair": (2, 0, 2)}


def build(rank, ring, cfg):
    ops = []

    def add(q, fn, rd, wr, kind, n, sig=None, rows=0, boost=None):
        if boost is None:
            boost = cfg["boost"].get(q + (wr[0][0] if wr else ""), 9)
        ops.append({"q": q, "fn": fn, "rd": rd, "wr": wr, "kind": kind, "n": n, "sig": sig, "rows": rows,
                    "boost": boost, "first": False})

    def reg(name, lo, hi, step=1):
        return (name, lo, hi, step)

    def box(name, ra, rb, ca, cb, step=1):
        w = 16 if name[0] == "#" else SCRATCH[name][1][2]
        return (name, ra * w + ca, (rb - 1) * w + cb, (ra, rb, ca, cb, step))

    nbank = [0]

    def bank(kind="g"):
        nbank[0] += 1
        return "#%s%d" % (kind, nbank[0])

    def ap(T, r):
        name, lo, hi, step = r
        name = BANK.get(name, name)
        if isinstance(step, tuple):
            if step[1] - step[0] == 1:
                return T[name][:, step[0], step[2]:step[3]:step[4]] if step[4] != 1 else T[name][:, step[0], step[2]:step[3]]
            return T[name][:, step[0]:step[1], step[2]:step[3]:step[4]]
        if len(SCRATCH[name][1]) == 3:
            w = SCRATCH[name][1][2]
            if lo // w == (hi - 1) // w:
                return T[name][:, lo // w, lo % w:(hi - 1) % w + 1:step]
            return T[name][:, lo // w:hi // w, lo % w::step]
        return T[name][:, lo:hi:step] if step != 1 else T[name][:, lo:hi]

    def cnt(r):
        if isinstance(r[3], tuple):
            return (r[3][1] - r[3][0]) * ((r[3][3] - r[3][2] + r[3][4] - 1) // r[3][4])
        return (r[2] - r[1] + r[3] - 1) // r[3]

    def memset(o, c, half=True):
        add("V", lambda g, T: g.vector.memset(ap(T, o), c), [], [o], "v", cnt(o) * (0.5 if half else 1))

    def tscal(o, i, s1, s2, op0, op1=None, half=False):
        cols = [s for s in (s1, s2) if isinstance(s, tuple)]

        def fn(g, T):
            a, b = [ap(T, s) if isinstance(s, tuple) else s for s in (s1, s2)]
            if op1 is None:
                return g.vector.tensor_scalar(ap(T, o), ap(T, i), a, None, op0)
            return g.vector.tensor_scalar(ap(T, o), ap(T, i), a, b, op0, op1)
        add("V", fn, [i] + cols, [o], "v", cnt(o) * (0.5 if half else 1))

    def vcopy(o, i):
        add("V", lambda g, T: g.vector.tensor_copy(ap(T, o), ap(T, i)), [i], [o], "v", cnt(o))

    def gcopy(o, i, extra):
        add("G", lambda g, T: g.affine_select(ap(T, o), ap(T, i), [[0, cnt(o)]], ALU.is_ge, 0.0, 0, 0), [i] + extra, [o],
            "g", cnt(o))

    def tt(o, a, b, op, w=1):
        add("V", lambda g, T: g.vector.tensor_tensor(ap(T, o), ap(T, a), ap(T, b), op), [a, b], [o], "v", cnt(o) * w)

    def fused(o, w, off, y, op, extra=()):
        add("V", lambda g, T: g.vector.tensor_tensor(ap(T, o), ap(T, w).indirect(ap(T, off)), ap(T, y), op),
            [w, off, y] + list(extra), [o], "vg", cnt(o))

    def hop(o, win, y, v0, v1, op, stops=()):
        at = [v0] + [v for v in stops if v0 < v < v1] + [v1]
        for a, b in zip(at, at[1:]):
            fused(reg(o, a, b), reg(win, 0, V), reg("rf16", a // 16, b // 16), reg(y, a, b), op)

    def gather(eng, o, w, off, extra, scale=1.0):
        if eng == "A":
            add("A", lambda g, T: g.scalar.activation(ap(T, o), ap(T, w).indirect(ap(T, off)), AF.Copy, scale=scale),
                [w, off] + extra, [o], "ag", cnt(o))
        else:
            add("V", lambda g, T: g.vector.tensor_copy(ap(T, o), ap(T, w).indirect(ap(T, off))),
                [w, off] + extra, [o], "vg", cnt(o))

    def act(o, i, func, bias=0.0, scale=1.0, boost=None):
        col = bias if isinstance(bias, tuple) else None

        def fn(g, T):
            return g.scalar.activation(ap(T, o), ap(T, i), func, bias=(ap(T, col) if col else bias), scale=scale)
        add("A", fn, [i] + ([col] if col else []), [o], "a", cnt(o), boost=boost)

    def mm(o, w, x, start, stop, extra=(), boost=None):
        add("P", lambda g, T: g.tensor.matmul(ap(T, o), ap(T, w), ap(T, x), start, stop), [w, x] + list(extra), [o],
            "p", max(64, cnt(o)), boost=boost)

    def full(name):
        return reg(name, 0, 128)

    def load(q, name, src, c0, c1, d0, sem, size, extra=()):
        def fn(g, T):
            return (g.sync if q == "S" else g.scalar).dma_start(T[name][:, d0:d0 + c1 - c0], T[src][:, c0:c1])
        add(q, fn, list(extra), [reg(name, d0, d0 + c1 - c0)], "d", (c1 - c0) * size, sig=(sem, 16), rows=128)

    def store(dst, name, v0, v1, size):
        add("S", lambda g, T: g.sync.dma_start(T[dst][:, v0:v1], T[name][:, v0:v1]), [reg(name, v0, v1)],
            [], "d", (v1 - v0) * size, sig=("outs", None), rows=128)

    nsend = [0]

    def write(q, src, dst, to, rd, wr, sem):
        kind = "h" if q == "H" else "r"
        add(q, ([([src], [dst])], to, "loc", 0), rd, wr, kind, 2 * cnt(src), sig=(sem, None),
            rows=128 * sum(WAYS[to][:2]) if q == "G" else 0)
        ops[-1]["first"] = not any(p["kind"] == kind for p in ops[:-1])

    def send(r, who, c0, c1, route, via):
        x, y = [reg("tab%d" % r, V * ring[seat ^ who ^ m] + c0, V * ring[seat ^ who ^ m] + c1) for m in (0, 2)]
        head = r > 0 and c0 == 0
        nsend[0] += 4
        done = [reg("far%d" % r, j + (0 if head else nsend[0]), j + 1 + (0 if head else nsend[0])) for j in range(3)]
        sem, mid = ("head%d" if head else "arr%d") % r, reg(via, 0, 1)
        if route == "d":
            write("G", x, x, "all", [x], [done[0]], sem)
        elif route == "a":
            write("G", x, x, "aide", [x], [mid], via)
            write("H", x, x, "all", [mid], [done[0]], sem)
        elif route == "f":
            write("G", x, x, "faraide", [x], [mid], via)
            write("G", x, x, "par", [x], [done[0]], sem)
            write("H", y, y, "pair", [mid], [done[1]], sem)
        else:
            write("G", x, x, "mir", [x], [mid, done[2]], via)
            write("G", x, x, "par", [x], [done[0]], sem)
            write("G", y, y, "par", [mid], [done[1]], sem)

    seat = ring.index(rank)
    own0, par0 = V * rank, V * ring[seat ^ 1]
    plan = cfg["plan"]
    ca = cfg["c0a"]

    def chunk(r, v):
        return [c for c in plan[r] if c[0] <= v < c[1]][0]

    def signset(r, v):
        c = chunk(r, v)
        if c[2] == "n":
            return tuple((i, 16, 4) for i in range(4 - c[4], 4))
        return tuple((8 * b + 8 - int(c[2 + b][1]), 8 * b + 8, 1) for b in range(2) if int(c[2 + b][1]))

    def blocks(c0, c1):
        return [c0] + ([c1 - 128] if c1 - c0 > 128 else [])

    sets = sorted(set(signset(r, v) for r in range(RO) for v in range(0, V, 32)) - {()})
    loose = {v for v in range(0, V, 32) if len(set(signset(r, v) for r in range(RO))) > 1}
    for _ in range(V // 32):
        for v in (v for r in range(RO) for c in cfg["cnt"][r] for v in blocks(*c)):
            if loose & set(range(v, v + 128, 32)):
                loose |= set(range(v, v + 128, 32))

    loads = {"c0a": ("tab0", "c0", 0, ca, own0, 2), "c0b": ("tab0", "c0", ca, V, own0 + ca, 2),
             "cp0": ("cpi", "cp", 0, 512, 0, 4), "cp1": ("cpi", "cp", 512, V, 512, 4),
             "rfs": ("rfi", "rf", 0, 64, 0, 4)}
    for j, (a, b) in enumerate(cfg["gaps"]):
        loads["gp%d" % j] = ("gpi", "gp", a, b, a, 4)
    for s in cfg["loads"]:
        load("S", *loads[s][:5], s, loads[s][5])
        if cfg["pin"]:
            ops[-1]["pin"] = len(ops)
    memset(reg("ones", 0, 256), 1.0)
    add("G", lambda g, T: g.iota(T.pcol[:, 0:4], [[16, 2], [1, 2]], 0, 1), [], [reg("pcol", 0, 4)], "g", 4)
    if cfg.get("oldpro"):
        add("G", None, [], [reg("pcol", 4, 5)], "g", 820)
        ops[-1]["pin"] = 0
    mark = len(ops)
    for j, (a, b, route) in enumerate(cfg["first"]):
        send(0, 0, a, b, route, "via%d" % j)
    ops[mark]["rd"].append(reg("pcol", 0, 5 if cfg.get("oldpro") else 4))
    rest = sorted(ops[mark + 1:], key=lambda o: (WAYS[o["fn"][1]][1] == 0) + (o["rd"][0][0][:3] == "via"))
    ops[mark + 1:] = rest
    for j, o in enumerate(ops[mark:]):
        o["pin"] = mark + j
    for a in (0, 256):
        add("V", lambda g, T, a=a: g.vector.tensor_tensor_scan(T.lo[:, a:a + 256], T.ones[:], T.ones[:], -1.0, ALU.mult,
                                                               ALU.add), [reg("ones", 0, 256)], [reg("lo", a, a + 256)],
            "v", 128)
    load("S", "thi", "th", 0, V, 0, "ths", 4, extra=[reg(*cfg["thwait"])])
    eye = reg("J", 16, 144)

    def col(j):
        return reg("kcol", j, j + 1)

    vcopy(reg("kcol", 0, 4), reg("pcol", 0, 4))
    for j, bits in enumerate((112, 15, 16)):
        tscal(reg("pand", j, j + 1), reg("pcol", 0, 1), bits, None, ALU.bitwise_and)
    tscal(reg("J", 0, 160), reg("lo", 0, 160), col(2), None, ALU.is_equal, half=True)
    tscal(col(4), reg("pand", 0, 1), 15.0, None, ALU.add)
    tscal(full("tri0"), full("lo"), col(0), col(4), ALU.max, ALU.min, half=True)
    tt(full("tri16"), full("tri0"), full("lo"), ALU.is_equal, 2)
    tscal(col(5), reg("pand", 1, 2), 15.0, None, ALU.is_lt)
    tscal(full("sh"), full("lo"), col(1), col(5), ALU.is_equal, ALU.mult, half=True)
    tscal(col(6), reg("pand", 2, 3), 8.0, None, ALU.is_lt)
    tscal(col(7), reg("pand", 2, 3), 8.0, None, ALU.is_gt)
    tscal(full("I16"), eye, 1.0, None, ALU.mult, half=True)
    first_const = len(ops)

    onv = cfg["const"] == "V"

    def fill(o, c):
        if onv or o[0] in cfg["onv"]:
            return memset(o, c)
        act(o, reg("ones", 0, cnt(o)), AF.Copy, scale=c)

    for name, c in (("BI", OWN), ("nTW", -float(TW)), ("nI", -1.0), ("nI256", -256.0), ("n2I", -2.0), ("I2", 2.0), ("nY", -0.375),
                    ("I3", 3.0)):
        if onv or name in cfg["onv"]:
            tscal(full(name), eye, c, None, ALU.mult, half=True)
        else:
            act(full(name), eye, AF.Copy, scale=c)
    wide = 1024 if onv or "rst" in cfg["onv"] else 256
    for a in range(0, 1024, wide):
        fill(reg("rst", a, a + wide), 1.0)
    fill(reg("rst", 0, 1024, 8), 0.0)
    for j in range(len(cfg["short"])):
        fill(reg("now", 272 * j, 272 * j + 16), 0.0)
        fill(reg("back", 272 * j + 16, 272 * j + 272), 0.0)
    fill(full("K258"), 258.0)
    fill(reg("hv", 0, 8), 0.5)
    fill(reg("r16", 0, 256), -1024.0)
    fill(reg("r16", 0, 256, 16), 0.5)
    act(full("Klift"), eye, AF.Identity, bias=2.0, scale=0.5)
    for a in range(0, 128 * len(sets), 256):
        fill(reg("wb", a, a + 256), 0.0)
    for si, st in enumerate(sets):
        for k0, k1, dk in st:
            fill(box("wb", 8 * si, 8 * si + 8, k0, k1, dk), 0.5)
    if onv:
        tt(full("Dm"), eye, full("sh"), ALU.subtract, 2)
    else:
        dm = full(bank())
        mm(dm, eye, eye, True, False, [full("sh")])
        mm(dm, full("nI"), full("sh"), False, True)
        act(full("Dm"), dm, AF.Copy)
    last_const = len(ops)
    for j in range(2):
        tscal(reg("J%d" % j, 0, 160), reg("J", 0, 160), col(6 + j), None, ALU.mult, half=True)
    vcopy(reg("rf16", 0, 64), reg("rfi", 0, 64))

    def flip(src, r, v0, v1):
        out = reg("hT%d" % r, v0, v1)
        add("V", lambda g, T: g.vector.transpose(ap(T, out), T[src][:, v0:v1]), [reg(src, v0, v1)], [out], "v",
            (v1 - v0) / 2)

    def turn(src, r, v0, v1, blocks):
        flip(src, r, v0, v1)
        nb, b0 = (v1 - v0) // 32, v0 // 32
        runs = []
        for c in plan[r]:
            if v0 <= c[0] < v1:
                if runs and runs[-1][2] == c[1] - c[0]:
                    runs[-1][1] = c[1]
                else:
                    runs.append([c[0], c[1], c[1] - c[0]])
        for h in map(int, blocks):
            terms = [(j, d, c) for j in range(r + 1) for d in range(2) for c in range(2)]
            tb = bank("t")
            for j, d, c in terms:
                mm(box(tb, 0, nb, 8 * d, 8 * d + 8), reg("J%d" % d, 16 + 16 * (d - c), 144 + 16 * (d - c)),
                   box("hT%d" % j, b0, b0 + nb, 16 * c + 8 * h, 16 * c + 8 * h + 8), (j, d, c) == terms[0],
                   (j, d, c) == terms[-1], [reg(*cfg["topen"], 1)] if r and (j, d, c) == terms[0] else [])
            for a, b, n in runs:
                for kk in range(8):
                    at = (8 * h + kk) * n // 16
                    tscal(box("L%d" % n, a // n, a // n + (b - a) // n, at, at + n // 16),
                          box(tb, (a - v0) // 32, (b - v0) // 32, kk, 16, 8), TW / 2, None, ALU.add)

    def spare(src, r):
        for c in plan[r]:
            if c[2] == "n" and any(chunk(rr, v)[2] != "n" for rr in range(r + 1, RO) for v in range(c[0], c[1], 32)):
                flip(src, r, c[0], c[1])
                ops[-1]["boost"] = 1

    less = [bank("f"), bank("f")]
    for h in range(2):
        a = 512 * h
        tscal(reg("own", a, a + 512), reg("cpi", a, a + 512), -1.0, 1.0, ALU.mult, ALU.add)
        if cfg["less"]:
            mm(reg(less[h], 0, 512), eye, reg("own", a, a + 512), True, True)
            if cfg.get("oldpro"):
                mm(reg(less[h], 0, 512), eye, reg("own", a, a + 512), True, True)
    floors = cfg["mod"] == "A"
    base = own0 + (QOFF * TW - TW / 2 if floors else 0.0)
    for a, b in cfg["sums"]:
        z1, z2 = bank(), bank()
        parts = [(max(a, x), min(b, y)) for x, y in cfg["gaps"] if x < b and a < y]
        for z in (z1, z2):
            mm(reg(z, 0, b - a), eye, reg("lo", a % 256, a % 256 + b - a), True, False,
               [reg("gpi", a, b)] if cfg.get("oldpro") else [])
        mm(reg(z2, 0, b - a), full("BI"), reg("own", a, b), False, False)
        for x, y in parts:
            if cfg["less"]:
                tt(reg("nog", x, y), reg("gpi", x, y), reg(less[x // 512], x % 512, x % 512 + y - x), ALU.mult)
            else:
                tt(reg("nog", x, y), reg("gpi", x, y), reg("own", x, y), ALU.mult, 2)
            for z in (z1, z2):
                mm(reg(z, x - a, y - a), full("tri16"), reg("nog", x, y), False, y == b)
        at = [a] + [v for v in range(0, V, 256) if a < v < b] + [b]
        for name, z, func, lift in (("Gw", z1, AF.Identity, 0.0), ("Hw", z2, AF.Relu, BIG - OWN), ("Y2", z2, AF.Relu, 2 * BIG - OWN)):
            for x, y in zip(at, at[1:]):
                if name == "Hw" and cfg["hw"] == "V":
                    tscal(reg(name, x, y), reg(z, x - a, y - a), base + x // 256 * 256 + lift, 0.0, ALU.add, ALU.max)
                else:
                    act(reg(name, x, y), reg(z, x - a, y - a), func, bias=base + x // 256 * 256 + lift)
    hop("S1", "Gw", "Hw", 0, V, ALU.max, cfg["hop0"])
    for v0, v1, how in cfg["dec"][0]:
        at = [v0] + [v for v in cfg["cut0"] if v0 < v < v1] + [v1]
        for a, b in zip(at, at[1:]):
            if floors:
                hop("S2", "S1", "Y2", a, b, ALU.max)
                act(reg("qr", a, b), reg("S2", a, b), AF.Identity, bias=QOFF - 0.5 + 0.5 / TW - (base - own0) / TW,
                    scale=1.0 / TW)
                x = reg(bank(), 0, b - a)
                mm(x, full("nTW"), reg("qr", a, b), True, True)
                tt(reg("S16", a, b), reg("S2", a, b), x, ALU.add)
                ops[-1]["boost"] = 9
                continue
            hop("s2i", "S1", "Y2", a, b, ALU.max)
            tscal(reg("s2m", a, b), reg("s2i", a, b), TW - 1, None, ALU.bitwise_and)
            if how != "n":
                tscal(reg("S16", a, b), reg("s2m", a, b), -TW / 2, None, ALU.add)
                ops[-1]["boost"] = 9
        if how != "n":
            turn("S16", 0, v0, v1, how)
        elif floors:
            tscal(reg("L", v0, v1), reg("S16", v0, v1), TW / 2, None, ALU.add, half=True)
        else:
            vcopy(reg("L", v0, v1), reg("s2m", v0, v1))
            tscal(reg("S16", v0, v1), reg("L", v0, v1), -TW / 2, None, ALU.add, half=True)
    spare("S16", 0)
    for h in range(2):
        a, b = 512 * h, 512 * h + 512
        lift = []
        for c in range(a, b, 32):
            if signset(0, c) and c not in loose:
                if lift and lift[-1][1] == c and signset(0, c) == signset(0, c - 32) and c - lift[-1][0] < 256:
                    lift[-1][1] = c + 32
                else:
                    lift.append([c, c + 32])
        nb = bank("f")
        mm(reg(nb, 0, 512), full("nI256"), reg("own", a, b), True, False, [reg("S1", 0, V)], boost=0)
        for j in (0, 256):
            mm(reg(nb, j, j + 256), full("Klift"), reg("ones", 0, 256), False, j > 0 and not lift, boost=0)
        for c, d in lift:
            si = sets.index(signset(0, c))
            mm(reg(nb, c - a, d - a), reg("wb", 128 * si, 128 * si + 128), reg("ones", 0, d - c), False,
               c == lift[-1][0], boost=0)
        tt(reg("nth", a, b), reg(nb, 0, 512), reg("thi", a, b), ALU.subtract)
        ops[-1]["rd"].append(reg(*cfg["nthwait"]))

    mid = cfg["boost"].get("D", 5)
    for r in range(RO):
        tab = "tab%d" % r
        win = reg(tab, 0, TW if r == 0 else TW + 16)
        far = [reg("far%d" % r, 0, 999)]
        last = r == RO - 1
        chunks = plan[r]
        mcol, at = {}, 0
        for c in chunks:
            if c[2] == "n":
                mcol[c[0]] = at
                at += 16 * (c[1] - c[0])
        if r > 0:
            gcopy(reg(tab, TW, TW + 16), reg(tab, 0, 16), [reg("far%d" % r, 0, 4)])
            def step(o, win, v0, v1, stops):
                runs = []
                for a, b in sorted(cfg["cnt"][r - 1]):
                    op = ALU.is_gt if a in cfg["yv"][r - 1] else ALU.is_ge
                    if runs and runs[-1][2] == op:
                        runs[-1][1] = b
                    else:
                        runs.append([a, b, op])
                for a, b, op in runs:
                    if max(a, v0) < min(b, v1):
                        hop(o, win, "Y", max(a, v0), min(b, v1), op, stops)

            step("h1", "any%d" % (r - 1), 0, V, cfg["hop1"])
            for v0, v1, how in cfg["dec"][r]:
                if v0 in cfg["quick"]:
                    hop("Gw", "h1", "Hw", v0, v1, ALU.add)
                    tscal(reg("L", v0, v1), reg("Gw", v0, v1), 0.25, None, ALU.mult)
                    if not last:
                        tscal(reg("S16", v0, v1), reg("L", v0, v1), -TW / 2, None, ALU.add, half=True)
                    continue
                step("h2%d" % r, "h1", v0, v1, cfg["hop2"])
                if how != "n":
                    turn("h2%d" % r, r, v0, v1, how)
                    continue
                o = reg(bank(), 0, v1 - v0)
                mm(o, full("I16"), reg("S16", v0, v1), True, False, [reg(*cfg["topen"], 1)])
                for rr in range(1, r + 1):
                    mm(o, full("I16"), reg("h2%d" % rr, v0, v1), False, rr == r)
                tscal(reg("L", v0, v1), o, TW / 2, None, ALU.add)
            spare("h2%d" % r, r)
        copies = {}

        def repeat(v0, v1, per):
            n = v1 - v0
            for j in range(copies.get(v0, 0), per):
                gcopy(reg("cw", 4 * v0 + j * n, 4 * v0 + (j + 1) * n), reg(tab, own0 + v0, own0 + v1),
                      far if r or cfg.get("oldpro") else [])
            copies[v0] = max(per, copies.get(v0, 0))
            return reg("cw", 4 * v0, 4 * v0 + per * n)

        def unit(j, blk):
            v0, v1 = chunks[j][:2]
            n = v1 - v0
            if chunks[j][2] == "n":
                if blk:
                    return
                m = n // len(chunks[j][3])
                for a in range(v0, v1, m):
                    gather(chunks[j][3][(a - v0) // m], reg("P", 16 * a, 16 * (a + m)), win, reg("L", a, a + m), far)
                for a in range(v0, v1, 64):
                    pr = reg("P", 16 * a, 16 * a + 1024)
                    mo = reg("M", mcol[v0] + 16 * (a - v0), mcol[v0] + 16 * (a - v0) + 1024)
                    add("V", lambda g, T, pr=pr, mo=mo: g.vector.tensor_tensor_scan(
                        ap(T, mo), T.rst[:], ap(T, pr), 0.0, ALU.mult, ALU.max), [pr, reg("rst", 0, 1024)], [mo], "v", 512)
                return
            eng, base = chunks[j][2 + blk][0], 16 * v0 + 8 * n * blk
            per = max(1, min(cfg["links"][eng], cfg["call"][eng] // n))
            if eng == "V":
                cw = repeat(v0, v1, per)
            if eng == "D":
                own = reg(tab, own0 + v0, own0 + v1)
                for kk in range(8):
                    o = reg("CM", base + kk * n, base + (kk + 1) * n)
                    add("S", lambda g, T, o=o: g.sync.dma_start(ap(T, o), ap(T, own)), [own] + far, [o], "d", 2 * n,
                        sig=("w%d_%d%d" % (r, j, blk), None), rows=128)
            for kk in range(0, 8, per):
                o = reg("P", base + kk * n, base + (kk + per) * n)
                k = 8 * blk + kk
                off = box("L%d" % n, v0 // n, v0 // n + 1, k * n // 16, (k + per) * n // 16)
                if eng == "V":
                    fused(o, win, off, cw, ALU.subtract, far)
                    continue
                gather("A", o, win, off, far, -1.0 if eng == "D" else 1.0)
            if eng == "D":
                o, x = reg("CM", base, base + 8 * n), reg("P", base, base + 8 * n)
                add("G", lambda g, T: g.dma_start(ap(T, o), ap(T, x), accum_op=ALU.add), [o, x], [o], "x", 16 * n,
                    sig=("x%d_%d%d" % (r, j, blk), None), rows=128)
                ops[-1]["first"] = not any(p["kind"] == "x" for p in ops[:-1])

        def fold(j, blk):
            v0, v1 = chunks[j][:2]
            if chunks[j][2] == "n":
                return
            n = v1 - v0
            base = 16 * v0 + 8 * n * blk
            srcs = [reg("P", base + kk * n, base + (kk + 1) * n) for kk in range(8)]
            dst = reg("FM%d%d" % (r, blk), v0, v1)
            add("G", ([(srcs, [dst])], "par", "fl%d" % r, 3 if chunks[j][2 + blk][0] == "D" else 2), srcs, [dst], "f",
                16 * n, sig=("f%d_%d%d" % (r, j, blk), None), rows=128)

        def compare(j, blk):
            v0, v1 = chunks[j][:2]
            n = v1 - v0
            if chunks[j][2] == "n":
                if blk:
                    return
                for u in range(v0, v1, 128):
                    cown, nv = reg(tab, own0 + u, own0 + u + 128), 4 - chunks[j][4]
                    cb = bank()
                    for i in range(4 if nv else 0):
                        mm(reg(cb, i, 512, 4), eye, cown, True, True, far + [reg("P", 16 * u, 16 * u + 16)])
                    for i in range(4):
                        out, quarter = reg("CM", 16 * u + 512 * i, 16 * u + 512 * i + 512), reg("P", 16 * u + i, 16 * (u + 128), 4)
                        if i < nv:
                            tt(out, quarter, reg(cb, 0, 512), ALU.is_gt)
                            continue
                        db = bank()
                        mm(reg(db, 0, 512), eye, quarter, True, False, boost=mid)
                        for x in range(4):
                            mm(reg(db, x, 512, 4), full("nI"), cown, False, x == 3, far, boost=mid)
                        act(out, reg(db, 0, 512), AF.Sign, bias=-0.5)
                return
            eng, w = chunks[j][2 + blk][0], int(chunks[j][2 + blk][1])
            base = 16 * v0 + 8 * n * blk
            if eng != "A":
                per, src = max(1, 1024 // n), "P" if eng == "V" else "CM"
                for k in range(0, 8 - w, per):
                    a, b = base + k * n, base + min(k + per, 8 - w) * n
                    tscal(reg("CM", a, b), reg(src, a, b), 0.0, None, ALU.is_gt if eng == "V" else ALU.is_lt, half=True)
                per = max(1, cfg["signcall"] // n)
                for k in range(8 - w, 8, per):
                    a, b = base + k * n, base + min(k + per, 8) * n
                    act(reg("CM", a, b), reg(src, a, b), AF.Sign, bias=-0.5, scale=1.0 if eng == "V" else -1.0)
                return
            cown = reg(tab, own0 + v0, own0 + v1)
            nv = 8 - w
            per = min(8, 512 // n)
            if nv:
                cb = bank()
                for i in range(min(per, nv)):
                    mm(reg(cb, i * n, (i + 1) * n), eye, cown, True, True, far + [reg("P", base, base + 16)])
            for k in range(0, nv, per):
                a, b = base + k * n, base + min(k + per, nv) * n
                tt(reg("CM", a, b), reg("P", a, b), reg(cb, 0, b - a), ALU.is_gt)
            for k0 in range(nv, 8, per):
                k1 = min(8, k0 + per)
                db = bank()
                mm(reg(db, 0, (k1 - k0) * n), eye, reg("P", base + k0 * n, base + k1 * n), True, False, boost=mid)
                for k in range(k0, k1):
                    mm(reg(db, (k - k0) * n, (k - k0 + 1) * n), full("nI"), cown, False, k == k1 - 1, far, boost=mid)
                act(reg("CM", base + k0 * n, base + k1 * n), reg(db, 0, (k1 - k0) * n), AF.Sign, bias=-0.5)

        def registers(j):
            c0, c1 = cfg["reg"][r][j]
            n = c1 - c0
            folded = chunk(r, c0)[2] != "n"
            terms = []
            if folded:
                for c in chunks:
                    a, b = max(c0, c[0]), min(c1, c[1])
                    if a < b:
                        nv = sum(1 for u in c[2:4] if u[0] == "V")
                        terms.append(([eye, full("I2"), full("I3")][nv], reg(tab, par0 + a, par0 + b), a - c0))
                        terms += [(full("nI") if c[2 + blk][0] == "D" else eye, reg("FM%d%d" % (r, blk), a, b), a - c0)
                                  for blk in range(2)]
            else:
                m0 = mcol[chunk(r, c0)[0]] + 16 * (c0 - chunk(r, c0)[0])
                terms = [(eye, reg(tab, own0 + c0, own0 + c1), 0)]
                terms += [(eye, reg("M", m0 + 7 + 8 * b, m0 + 16 * n, 16), 0) for b in range(2)]
            nxt = ("ypt" if folded else "ycb") if last else "tab%d" % (r + 1)
            d0 = c0 if last else (par0 if folded else own0) + c0
            x = reg(bank(), 0, n)
            lifted = c0 in cfg["regv"][r]
            if lifted:
                terms.insert(0, (full("K258"), reg("ones", 0, n), 0))
            terms.reverse()
            for i, (w, xx, a) in enumerate(terms):
                mm(reg(x[0], a, a + cnt(xx)), w, xx, i == 0, i == len(terms) - 1, far + [t[1] for t in terms])
            if lifted:
                act(reg("qr", c0, c1), x, AF.Identity, bias=-127.5)
                tt(reg(nxt, d0, d0 + n), x, reg("qr", c0, c1), ALU.subtract)
                ops[-1]["boost"] = 9
            else:
                x2 = reg(bank(), 0, n)
                ops[-1]["wr"].append(reg("open" + x[0], 0, 1))
                act(reg("qr", c0, c1), x, AF.Identity, bias=QOFF - 0.5 + 2.0 ** -9, scale=2.0 ** -8)
                for i, (w, xx, a) in enumerate(terms):
                    mm(reg(x2[0], a, a + cnt(xx)), w, xx, i == 0, False, far + [reg("open" + x[0], 0, 1)])
                mm(x2, full("nI256"), reg("qr", c0, c1), False, True)
                act(reg(nxt, d0, d0 + n), x2, AF.Identity, bias=QOFF * 256)
            if not last:
                send(r + 1, int(folded), c0, c1, cfg["route"][r][j], "via%d_%d" % (r, j))
                return
            if folded:
                src, dst = reg("ypt", c0, c1), reg("ycb", c0, c1)
                write("G", src, dst, "par", [src], [dst], "yb%d" % j)
            store("yc", "ycb", c0, c1, 2)

        def counts(c0, c1):
            n = c1 - c0
            fb = bank("f")
            at = list(enumerate(blocks(c0, c1)))
            m = 128 * len(at)
            F, Cc = reg(fb, 0, m), reg(fb, 256, 256 + n)
            ks = []
            for j, v in at:
                c = chunk(r, v)
                for k in range(16):
                    if c[2] != "n":
                        a = 16 * c[0] + k * (c[1] - c[0]) + v - c[0]
                        cm = reg("CM", a, a + 128)
                    else:
                        a = 16 * v + 512 * (k % 4)
                        cm = reg("CM", a + k // 4, a + 512, 4)
                    half = any(k in range(*x) for x in signset(r, v))
                    ks.append((128 * j + k, cm, reg("hv", 0, 8) if half else reg("ones", 0, 8)))
            made = [(i, o["wr"][0]) for i, o in enumerate(ops) if o["wr"] and o["wr"][0][0] == "CM"]
            ks.sort(key=lambda t: max(i for i, w in made if w[1] < t[1][2] <= w[2]))
            low = cfg["boost"]["F"]
            for j, v in at:
                mm(reg(fb, 128 * j, 128 * j + 128), reg("nth", v, v + 128), eye, j == 0, False, [ks[cfg["fopen"]][1]],
                   boost=low)
                if signset(r, v) and v in loose:
                    si = sets.index(signset(r, v))
                    mm(reg(fb, 128 * j, 128 * j + 128), full("ones"), reg("wb", 128 * si, 128 * si + 128), False, False,
                       boost=low)
            for i, (k, a, x) in enumerate(ks):
                mm(reg(fb, k, k // 128 * 128 + 128, 16), a, x, False, i == len(ks) - 1, boost=low)
            run = reg("run", 2 * c0, 2 * c0 + m)
            x = F
            if c0 in cfg["sign"][r]:
                x = reg("sg", 2 * c0, 2 * c0 + m)
                act(x, F, AF.Copy)
            add("V", lambda g, T: g.vector.tensor_tensor_scan(ap(T, run), T.r16[:, 0:m], ap(T, x), 0.5, ALU.max, ALU.min),
                [x, reg("r16", 0, 256)], [run], "v", m if x == F else m / 2)
            if last and c0 in cfg["short"]:
                a = 272 * cfg["short"].index(c0) + 16
                tscal(reg("now", a, a + m), run, 0.0, None, ALU.is_lt, half=True)
                tscal(reg("back", a + 16, a + m, 16), reg("run", 2 * c0 + 15, 2 * c0 + m - 16, 16), 0.0, None, ALU.is_lt,
                      half=True)
                Cc = reg(bank(), 0, n)
                for j in range(RO - 1):
                    mm(Cc, full("Dm"), reg("any%d" % j, c0, c1), j == 0, False, [ks[-1][1]])
                for j, v in at:
                    s, b = 0 if j == 0 else 256 - n, a + 128 * j
                    plus, minus = reg("J", 16 + s, 144), reg("nI", s, 128)
                    for x, w in ((reg("now", b, b + 128), plus), (reg("now", b - 1, b + 127), minus),
                                 (reg("back", b, b + 128), plus)):
                        mm(reg(Cc[0], v - c0 + s, v - c0 + 128), x, w, False, j == len(at) - 1 and x[0] == "back")
                tt(reg("ygb", c0, c1), Cc, reg("gpi", c0, c1), ALU.add)
                store("yg", "ygb", c0, c1, 4)
                return
            for j, v in at:
                mm(reg(fb, v - c0, v - c0 + 128), reg("run", 2 * c0 + 128 * j, 2 * c0 + 128 * j + 128), full("I2"), True,
                   True)
            act(reg("any%d" % r, c0, c1), reg(fb, 0, n), AF.Sign, bias=1.0, scale=-1.0)
            if last:
                for j in range(RO):
                    mm(Cc, full("Dm"), reg("any%d" % j, c0, c1), j == 0, j == RO - 1)
                tt(reg("ygb", c0, c1), Cc, reg("gpi", c0, c1), ALU.add)
                store("yg", "ygb", c0, c1, 4)
            elif c0 in cfg["yv"][r]:
                tt(reg("Y", c0, c1), reg(fb, 0, n), reg("own", c0, c1), ALU.mult)
            else:
                mm(Cc, eye, reg("own", c0, c1), True, False)
                mm(Cc, full("n2I"), reg("any%d" % r, c0, c1), False, True)
                act(reg("Y", c0, c1), Cc, AF.Abs, bias=1.0)
                if c0 in cfg["quick"]:
                    z = reg(bank(), 0, n)
                    mm(z, full("nY"), reg("Y", c0, c1), True, False)
                    mm(z, full("I16"), reg("S16", c0, c1), False, True)
                    act(reg("Hw", c0, c1), z, AF.Identity, bias=2.0 * TW + 3.0, scale=4.0)

        steps = {"g": unit, "c": compare, "o": fold, "f": lambda j: counts(*cfg["cnt"][r][j]), "r": registers}
        for word in cfg["seq"][r].split():
            at = len(ops)
            steps[word[0]](*map(int, word[1:]))
            for i in range(at, len(ops)):
                o = ops[i]
                o["word"] = "%d%s" % (r, word)
                if word in cfg["late"] and o["wr"] and o["wr"][0][0][:3] in ("any", "qr"):
                    o["rd"].append(reg("after%d" % r, 0, len(ops)))
                if o["kind"] == "ag":
                    o["wr"].append(reg("after%d" % r, i, i + 1))
    read = {x[0] for o in ops for x in o["rd"]}
    return [o for i, o in enumerate(ops) if not first_const <= i < last_const or o["wr"][0][0] in read]


def link(ops):
    hist, bank = {}, {}
    for i, o in enumerate(ops):
        pre = {}
        for rs, iswr in ((o["rd"], False), (o["wr"], True)):
            for name, lo, hi, step in rs:
                for j, a, b, st in hist.get((name, True), []) + (hist.get((name, False), []) if iswr else []):
                    if a < hi and lo < b and j != i:
                        if isinstance(st, tuple) and isinstance(step, tuple) and (st[3] <= step[2] or step[3] <= st[2]):
                            continue
                        both_pe = ops[j]["q"] == "P" and o["q"] == "P"
                        pre[j] = pre.get(j, False) or not both_pe
                if name[0] == "#":
                    j = bank.get(name)
                    if j is not None and j != i:
                        pre[j] = pre.get(j, False) or ops[j]["q"] != o["q"]
                    bank[name] = i
        for rs, iswr in ((o["rd"], False), (o["wr"], True)):
            for name, lo, hi, step in rs:
                if iswr and step == 1:
                    for w in (True, False):
                        hist[name, w] = [e for e in hist.get((name, w), []) if not (lo <= e[1] and e[2] <= hi)]
                hist.setdefault((name, iswr), []).append((i, lo, hi, step))
        o["pre"] = pre
    return ops


def cost(o, e):
    k, n = o["kind"], o["n"]
    if k == "v":
        return e["ov"] + max(64, n) * e["cyc"], 0, 0
    if k == "vg":
        return 50 + n * e["g"] * e["cyc"], 0, 0
    if k == "a":
        return e["oa"] + max(64, n) * e["cyc"] * e["ra"], 0, 0
    if k == "ag":
        return 65 + n * e["g"] * e["cyc"] * e["ra"], 0, 0
    if k == "p":
        return e["op"] + n * e["pe"], 0, 0
    if k == "g":
        return 170 + 2 * n * e["cyc"], 0, 0
    if k in "rh":
        near, far = WAYS[o["fn"][1]][:2]
        move = 8 * (near + far) * e["drow"] + 8 * n / e["dbw"] * (near + far * (3 * e["sx"] - 1) / 2)
        if k == "h":
            return e["riss"] + e["rfix"] + (e["rfirst"] if o["first"] else 0) + move, 0, 0
    else:
        move = (o["rows"] / 16 * e["drow"] * (e["frow"] if k == "f" else 1)
                + 8 * n / e["dbw"] * {"f": e["fb"], "x": e["xb"]}.get(k, 1))
    if k == "d":
        return 60, move, e["dfix"]
    if k == "x":
        return e["xiss"] + (e["rfirst"] if o["first"] else 0), move, e["dfix"]
    return e["riss"] + e["rw"] * (o["rows"] / 128 if k == "r" else 1) + (e["rfirst"] if o["first"] else 0), move, e["rfix"] + (e["fx"] if k == "f" else 0)


def schedule(ops, e, cfg):
    key, best = [(-o["boost"], i) for i, o in enumerate(ops)], None
    for _ in range(cfg["passes"]):
        start, banks, waits = greedy(ops, e, key, cfg)
        end, at, key = justify(hand_over(ops, waits), e, start)
        if best is None or end < best[0]:
            best = (end, at, banks, waits)
    at = best[1]
    LAST[:] = [at]
    return {q: sorted((i for i, o in enumerate(ops) if o["q"] == q), key=lambda i: (at[i], i)) for q in "VAPGSH"}, best[2], best[3]


def hand_over(ops, waits):
    ops = list(ops)
    for i, j in waits:
        ops[i] = dict(ops[i], pre=dict(ops[i]["pre"]))
        ops[i]["pre"][j] = ops[i]["pre"].get(j, False) or ops[j]["q"] != ops[i]["q"]
    return ops


def greedy(ops, e, key, cfg):
    n = len(ops)
    succ = [[] for _ in range(n)]
    opens, closes = {}, {}
    for i, o in enumerate(ops):
        for j in o["pre"]:
            succ[j].append(i)
        for x in o["rd"] + o["wr"]:
            if x[0][0] == "#":
                opens.setdefault(x[0], i)
                closes[x[0]] = i
    opens = {i: x for x, i in opens.items()}
    shut = {i: x for x, i in closes.items()}
    held = {b: (0.0, None) for b in "01234567"}
    banks, waits = {}, []
    left = [len(o["pre"]) for o in ops]
    fin, ready = [0.0] * n, [0.0] * n
    cand = {q: [] for q in "VAPGSH"}
    free = {q: 0.0 for q in "VAPGSH"}
    start = [0.0] * n
    dma = [0.0]
    for i in range(n):
        if left[i] == 0:
            cand[ops[i]["q"]].append(i)
    for _ in range(n):
        soon = {k: min((held[b][0] for b in v if held[b]), default=1e18) for k, v in cfg["banks"].items()}
        when = {i: max(ready[i], soon[opens[i][1]]) if i in opens else ready[i] for q in cand for i in cand[q]}
        t, q = min((max(free[q], min(when[i] for i in cand[q])), q) for q in cand if cand[q])
        assert t < 1e17
        i = min((i for i in cand[q] if when[i] <= t + cfg["delta"]), key=lambda i: key[i])
        cand[q].remove(i)
        a, b, c = cost(ops[i], e)
        st = max(free[q], when[i])
        if i in opens:
            bk = [x for x in cfg["banks"][opens[i][1]] if held[x] and held[x][0] <= st][0]
            if held[bk][1] is not None:
                waits.append((i, held[bk][1]))
            banks[opens[i]] = "B" + bk
            held[bk] = None
        if i in shut:
            held[banks[shut[i]][1]] = (st + a + e["sem"], i)
        start[i] = st
        free[q] = st + a
        if b:
            dma[0] = max(dma[0], st + a + c) + b
            fin[i] = dma[0]
        else:
            fin[i] = st + a
        for j in succ[i]:
            ready[j] = max(ready[j], fin[i] + (e["sem"] if ops[j]["pre"][i] else 0.0))
            left[j] -= 1
            if left[j] == 0:
                cand[ops[j]["q"]].append(j)
    return start, banks, waits


def justify(ops, e, start, rounds=2):
    n = len(ops)
    res, dur, pre = [o["q"] for o in ops], [cost(o, e)[0] for o in ops], [[] for o in ops]
    out, key = list(range(n)), list(start)
    for i, o in enumerate(ops):
        a, b, c = cost(o, e)
        if b:
            out[i] = len(res)
            res.append("D")
            dur.append(b)
            pre.append([(i, c)])
            key.append(start[i])
    for i, o in enumerate(ops):
        pre[i] = [(out[j], e["sem"] if w else 0.0) for j, w in o["pre"].items()]
    for q in "GS":
        pinned = [i for i, o in enumerate(ops) if "pin" in o and o["q"] == q]
        for j, i in zip(pinned, pinned[1:]):
            pre[i].append((j, 0.0))
            pre[out[i]].append((out[j], 0.0))
    m = len(res)
    suc = [[] for _ in range(m)]
    for i in range(m):
        for j, lag in pre[i]:
            suc[j].append((i, lag))

    def place(before, after, rank):
        left, ready, at = [len(x) for x in before], [0.0] * m, [0.0] * m
        busy = {q: [] for q in "VAPGSHD"}
        cand = sorted(((rank[i], i) for i in range(m) if not left[i]), reverse=True)
        while cand:
            i = cand.pop()[1]
            b, t = busy[res[i]], ready[i]
            p = len(b)
            while p and b[p - 1][1] > t:
                p -= 1
            while p < len(b) and b[p][0] < t + dur[i]:
                t = b[p][1]
                p += 1
            b.insert(p, (t, t + dur[i]))
            at[i] = t
            for j, lag in after[i]:
                ready[j] = max(ready[j], t + dur[i] + lag)
                left[j] -= 1
                if not left[j]:
                    cand.append((rank[j], j))
                    cand.sort(reverse=True)
        return at

    best = None
    for _ in range(rounds):
        for i, o in enumerate(ops):
            if "pin" in o:
                key[i] = key[out[i]] = o["pin"] - 1e9
        at = place(pre, suc, key)
        end = max(at[i] + dur[i] for i in range(m))
        if best is None or end < best[0]:
            best = (end, at)
        back = place(suc, pre, [-(at[i] + dur[i]) for i in range(m)])
        key = [-(back[i] + dur[i]) for i in range(m)]
    return best[0], best[1][:n], key[:n]


ORDER = []
BANK = {}
LAST = []


def rank_program(g, core, T, topo):
    by_die = sorted(range(NR), key=lambda q: (topo.die(T.cores[q]), q))
    spare = sorted((c for c in topo.cores_of(T.cores[0]) if c not in T.cores), key=lambda c: (topo.die(c), c))
    rank = T.rank_of(core)
    if rank is None and core not in spare:
        return
    aide = rank is None
    if aide:
        rank = by_die[spare.index(core)]
    at = by_die.index(rank)
    par = by_die[at ^ 1]
    if not ORDER:
        ORDER.extend(schedule(link(build(by_die[0], by_die, CFG)), EST, CFG))
        BANK.update(ORDER[1])
    order = ORDER[0]
    ops = hand_over(link(build(rank, by_die, CFG)), ORDER[2])
    dests = {"all": [c for c in T.cores if c != T.cores[rank]], "par": [T.cores[par]], "aide": [spare[at]],
             "mir": [T.cores[by_die[at ^ 2]]], "faraide": [spare[at ^ 2]], "pair": [T.cores[rank], T.cores[par]]}
    engines = [e for e in topo.engines(core, T.cores[par]) if all(e in topo.engines(core, c) for c in dests["all"])]
    neng = len(engines)

    def remote(o, eng):
        moves, to, loc, alu = o["fn"]
        ids = [DstId(rid=topo.addr(c)[0], pnc=topo.addr(c)[1]) for c in dests[to]]
        g.remote_dma_fused([RemoteDMATransfer(
            dst_ids=[d for x in dsts for d in ids], dma_engine_mask=sum(1 << e for e in eng),
            remote_sem=T.sem[o["sig"][0]], srcs=[T[x[0]][:, x[1]:x[2]] for x in srcs],
            dsts=[T[x[0]][:, x[1]:x[2]] for x in dsts for d in ids], alu_op=alu)
            for srcs, dsts in moves], local_sem=T.sem[loc])

    if aide:
        for i in order["H"]:
            for j in ops[i]["pre"]:
                g.wait_ge(T.sem[ops[j]["sig"][0]], neng)
            remote(ops[i], engines)
        if order["H"]:
            g.wait_ge(T.sem["loc"], neng * len(order["H"]))
        return
    total = {s: 0 for s in SEMAPHORES}
    for o in ops:
        if o["kind"] in "rfh":
            total[o["sig"][0]] += WAYS[o["fn"][1]][2] * neng
    for q in "VAPGS":
        k = 0
        for i in order[q]:
            o = ops[i]
            if o["sig"] is None:
                k += 1
                o["sig"] = (ENGSEM[q], k)
                total[ENGSEM[q]] = k
            elif o["kind"] in "rf":
                o["eng"] = engines
                o["sig"] = (o["sig"][0], total[o["sig"][0]])
                total[o["fn"][2]] += neng
            else:
                total[o["sig"][0]] += 16
    for o in ops:
        if o["kind"] in "dxh":
            o["sig"] = (o["sig"][0], total[o["sig"][0]])
    queue = {"V": g.vector, "A": g.scalar, "P": g.tensor, "G": g, "S": g.sync}
    for q in "VAPGS":
        seen = {}
        for i in order[q]:
            o = ops[i]
            need = {}
            for j, w in o["pre"].items():
                if w:
                    s, val = ops[j]["sig"]
                    if ops[j]["kind"] == "f" and all(x[0][:2] != "FM" for x in o["rd"]):
                        s = ops[j]["fn"][2]
                        val = total[s]
                    need[s] = max(need.get(s, 0), val)
            for s in sorted(need):
                if need[s] > seen.get(s, 0):
                    queue[q].wait_ge(T.sem[s], need[s])
                    seen[s] = need[s]
            if o["kind"] in "rf":
                remote(o, o["eng"])
            else:
                o["fn"](g, T).then_inc(T.sem[o["sig"][0]], 16 if o["kind"] in "dx" else 1)
    for s in SEMAPHORES:
        if total[s]:
            g.sync.wait_ge(T.sem[s], total[s])
